import numpy as np, ml_dtypes
CORES = [3,11,19,27,35,43,51,59]
N = 8
BF = ml_dtypes.bfloat16
def gentries(a):
    return np.ascontiguousarray(a.reshape(8, 16, -1).transpose(0, 2, 1)).reshape(8, -1)
def gtable(e):
    e = np.asarray(e); return np.ascontiguousarray(e.reshape(8, -1, 16).transpose(0, 2, 1)).reshape(128, -1).astype(np.int32)
W, S, U, H, C, R, TH, SH = 4096, 2048, 128, 3, 8, 3, 300, 8
B, LC = W // C, 3
def two(rng, lo, hi, shape):
    return np.where(rng.random(shape) < 0.5, lo, hi)
def pack(mu, fr, a, mix, s):
    return {"mu": np.ascontiguousarray(mu.reshape(N, 128, W)).astype(np.float32).astype(BF),
            "fr": np.ascontiguousarray(fr.reshape(N, 128, R * U)).astype(np.float32).astype(BF),
            "a0": np.ascontiguousarray(a.transpose(0, 1, 3, 2, 4)).reshape(N, 128, 16 * C).astype(np.float32).astype(BF),
            "mix": np.ascontiguousarray(mix.transpose(0, 1, 3, 2)).reshape(N, 128, S).astype(np.int32),
            "s0": np.stack([gtable(v) for v in s])}
def frames(rng, mu, mix, s):
    ri = np.arange(N)[:, None, None, None]; gi = np.arange(8)[None, :, None, None]
    st = (s[..., None] + (np.arange(R) * (H - 1)) // 2 + rng.integers(0, H, (N, 8, U, R))) & (S - 1)
    w = mix[ri, gi, st, rng.integers(0, 16, st.shape)]
    x = mu[ri, gi, :, w]
    x = np.where(rng.random((N, 8, U, R, 1)) < 0.5, np.clip(x + rng.integers(-3, 4, x.shape), -8, 7), rng.integers(-8, 8, x.shape))
    return np.ascontiguousarray(x.transpose(0, 1, 4, 3, 2))
def parts(rng):
    mu = rng.integers(-8, 8, (N, 8, 16, W))
    a = 64 * np.eye(16, dtype=np.int64) + rng.integers(-6, 7, (N, 8, C, 16, 16))
    wgt = np.exp2(rng.integers(0, 6, (8, C))); wgt[0] = 1.0; wgt[0, int(rng.integers(0, C))] = 32.0; wgt[1] = 1.0
    cum = np.add.accumulate(wgt, axis=1)
    v = rng.random((N, 8, S * 16, 1)) * cum[None, :, None, C - 1:]
    cl = np.minimum(np.add.reduce((v >= cum[None, :, None, :]).astype(np.int64), axis=-1), C - 1)
    mix = (cl * B + rng.integers(0, B, cl.shape)).reshape(N, 8, S, 16)
    s = rng.integers(0, S, (N, 8, U))
    return mu, a, mix, s
def setup_inputs(rng):
    mu, a, mix, s = parts(rng)
    return pack(mu, frames(rng, mu, mix, s), a, mix, s)
def setup_inputs_spread(rng):
    mu, a, mix, s = parts(rng)
    sz = np.array([1.0, 1.0, 0.5, 0.25, 0.125, 0.0])
    mu = np.floor(mu * rng.choice(sz, (N, 8, 1, W))).astype(np.int64)
    a = np.eye(16, dtype=np.int64) * rng.integers(16, 128, (N, 8, C, 1, 16)) + rng.integers(-127, 128, a.shape) * (rng.random(a.shape) < 0.0625)
    a = np.clip(a, -127, 127)
    mix[:, ::2] = np.minimum((W * rng.random((N, 4, S, 16)) ** 3).astype(np.int64), W - 1)
    s[:, 1::2] = np.minimum((S * rng.random((N, 4, U)) ** 4).astype(np.int64), S - 1)
    x = frames(rng, mu, mix, s)
    x = np.floor(x * rng.choice(sz, (N, 8, 1, R, U))).astype(np.int64)
    return pack(mu, x, a, mix, s)
def setup_inputs_ends(rng):
    mu = two(rng, -8, 7, (N, 8, 16, W)); x = two(rng, -8, 7, (N, 8, 16, R, U)); a = two(rng, -127, 127, (N, 8, C, 16, 16))
    kind = rng.integers(0, 3, (N, 8, S, 1))
    mix = np.where(kind == 0, 0, np.where(kind == 1, W - 1, two(rng, 0, W - 1, (N, 8, S, 16))))
    s = two(rng, 0, S - 1, (N, 8, U))
    mix[:, 7] = W - 1; mu[:, 7, :, W - 1] = -8; a[:, 7, C - 1] = 127; x[:, 7, :, 0::2] = 7; x[:, 7, :, 1::2] = -8
    mu[:, 6, :, 0] = -8; mu[:, 6, :, W - 1] = -8; a[:, 6, 0] = 127; a[:, 6, C - 1] = 127; x[:, 6] = two(rng, -8, 7, (N, 1, R, U))
    mix[:, 4] = W - 1; mu[:, 4, :, W - 1] = -8; a[:, 4, C - 1] = -127; x[:, 4] = -8
    return pack(mu, x, a, mix, s)
def setup_inputs_corners(rng):
    mu, a, mix, s = parts(rng); eye = 64 * np.eye(16, dtype=np.int64); low = (np.arange(16) < 8)[:, None]; slot = np.arange(16)[None, None, :]
    s[:, 2] = ((np.arange(N) & 1) * (S - 1))[:, None]
    mix[:, 3] = rng.choice(np.array([0, B - 1, B, W - 1]), (N, S, 1)); a[:, 3] = two(rng, -127, 127, (N, C, 16, 16))
    mix[:, 4] = rng.choice(np.concatenate([np.arange(C) * B, np.arange(C) * B + B - 1]), (N, S, 16))
    a[:, 5] = 0
    mu[:, 6] = rng.integers(-1, 2, (N, 16, W))
    s[:, 7] = rng.choice(np.array([0, 1, 2, 3, S - 2, S - 1]), (N, U))
    q = np.arange(W)[None, :] & 3
    mu[:, 0] = np.where(q == 0, 6, np.where(q == 1, -7, np.where(q == 2, np.where(low, 6, -8), np.where(low, -7, 7))))
    a[:, 0] = eye; ty = ((np.arange(S) // (H - 1)) & 1)[None, :, None]
    k = rng.integers(0, 16, (N, S, 1)); k[:, ::8] = 15; k[:, 3::8] = 0
    mix[:, 0] = 4 * rng.integers(0, W // 4, (N, S, 16)) + ty + 2 * (slot < k)
    s[:, 0] = (H - 1) * rng.integers(0, S // (H - 1), (N, U)); s[:, 0, :16] = S - (H - 1); s[:, 0, 16:32] = 0
    ft = rng.integers(0, 16, (N, 1, W))
    mu[:, 1] = -8 + ((np.arange(16)[None, :, None] == ft) & ((np.arange(W) & 1) == 1)[None, None, :]).astype(np.int64)
    a[:, 1] = eye; k = np.where(rng.random((N, S, 1)) < 0.5, rng.integers(1, 16, (N, S, 1)), 16)
    mix[:, 1] = 2 * rng.integers(0, W // 2, (N, S, 16)) + (slot < k)
    x = frames(rng, mu, mix, s)
    x[:, 6] = rng.integers(-1, 2, (N, 16, R, U)); x[:, 1] = -8
    cur = s[:, 0].copy(); u4 = (np.arange(U) & 3)[None, :]
    for t in range(R):
        mv = np.where(u4 == 0, 1, np.where(u4 == 1, 0, rng.integers(0, 2, (N, U))))
        x[:, 0, :, t] = np.where((((cur // (H - 1)) + mv) & 1) == 0, 7, -8)[:, None, :]
        cur = (cur + mv * (H - 1)) & (S - 1)
    return pack(mu, x, a, mix, s)
def setup_inputs_crowd(rng):
    mu, a, mix, s = parts(rng); T = N * U
    mix = ((np.arange(S) >> 4) & (C - 1))[None, None, :, None] * B + rng.integers(0, B, (N, 8, S, 16))
    kinds = [(1, TH - 1), (2, TH - 2), (3, TH - 3), (0, TH), (1, TH - 2)]
    for g in range(8):
        n = np.zeros((C // 2, 2), np.int64)
        if g == 0: n[C // 2 - 1, 1] = T
        elif g == 1: n[0, 0] = T - 1; n[C // 2 - 1, 1] = 1
        elif g == 2: n[0] = (TH, TH - 1); n[C // 2 - 1, 1] = T - 2 * TH + 1
        elif g in (3, 4):
            v = TH - 1 if g == 3 else TH; b = 2 * int(rng.integers(0, C // 4))
            h = v // 2 + int(rng.integers(-(v // 4), v // 4 + 1)); i = int(rng.integers(1, h)); j = int(rng.integers(1, v - h))
            n[b] = (i, h - i); n[b + 1] = (j, v - h - j)
            n[(b + C // 4) % (C // 2) + int(rng.integers(0, 2)), int(rng.integers(0, 2))] = T - v
        else:
            p = rng.permutation(C // 2)
            for i in range(3):
                v = kinds[(g + i) % 5]; n[p[i]] = v if rng.random() < 0.5 else v[::-1]
            n[p[3], int(rng.integers(0, 2))] = T - int(np.add.reduce(n.reshape(-1)))
        cl = rng.permutation(np.repeat(np.arange(C), n.reshape(-1))).reshape(N, U)
        s[:, g] = 16 * (cl + C * rng.integers(0, S // (16 * C), (N, U))) + rng.integers(0, 16 - R * (H - 1), (N, U))
    return pack(mu, frames(rng, mu, mix, s), a, mix, s)
def setup_inputs_tally(rng):
    mu, a, mix, s = parts(rng); T = N * U
    mix = ((np.arange(S) >> 4) & (C - 1))[None, None, :, None] * B + rng.integers(0, B, (N, 8, S, 16))
    for g in range(8):
        n = np.zeros(C, np.int64)
        if g in (0, 1, 2, 3, 7):
            q = N - 1 if g == 7 else int(rng.integers(0, N))
            c = C - 1 if g == 7 else 2 * int(rng.integers(0, C // 2)) + (1, 0, 0, 1)[g]
            m = TH - U - 1 if g == 3 else TH - U
            v = rng.choice(np.array([i for i in range(C) if i != c and (g != 3 or i != (c ^ 1))]), (N - 1) * U)
            v[:m] = c
            if g == 3: v[m] = c ^ 1
            v = rng.permutation(v).reshape(N - 1, U)
            cl = np.concatenate([v[:q], np.full((1, U), c, np.int64), v[q:]], axis=0)
        elif g == 4:
            o = 4 * int(rng.integers(0, C // 4)); p = (o + 4) % C; b = o + 2 * int(rng.integers(0, 2)); k = T - 2 * TH + 2
            n[b + int(rng.integers(0, 2))] = TH - 1; n[b ^ 2] = k // 2; n[(b ^ 2) + 1] = k - k // 2
            i = int(rng.integers(1, TH // 3)); j = int(rng.integers(1, TH // 3))
            n[p:p + 4] = rng.permutation(np.array([0, i, j, TH - 1 - i - j]))
            cl = rng.permutation(np.repeat(np.arange(C), n)).reshape(N, U)
        elif g == 5:
            p = rng.permutation(C // 2); k = TH // 15 + 1; left = T - 45 * k
            for i in range(3): n[2 * p[i]] = 7 * k; n[2 * p[i] + 1] = 8 * k
            n[2 * p[3]] = 7 * left // 15; n[2 * p[3] + 1] = left - 7 * left // 15
            cl = rng.permutation(np.repeat(np.arange(C), n)).reshape(N, U)
        else: cl = rng.integers(0, C, (N, U))
        s[:, g] = 16 * (cl + C * rng.integers(0, S // (16 * C), (N, U))) + rng.integers(0, 16 - R * (H - 1), (N, U))
    odd = ((np.arange(W) // B) & 1) == 1
    mu[:, 5] = np.where(odd[None, None, :], two(rng, 6, 7, (N, 16, W)), two(rng, -8, -7, (N, 16, W)))
    a[:, 5] = np.where((np.arange(C) & 1) == 1, -127, 127)[None, :, None, None]
    mu[:, 6, :14] = rng.integers(-8, -3, (N, 14, W)); a[:, 6, :, :14] = 127
    x = frames(rng, mu, mix, s)
    x[:, 5] = two(rng, 6, 7, (N, 16, R, U))
    x[:, 6, :14] = np.where(rng.random((N, 1, R, U)) < 0.5, 7, x[:, 6, :14])
    return pack(mu, x, a, mix, s)
def check_inputs(d):
    bad = []
    for k, lo, hi in (("mu", -8, 7), ("fr", -8, 7), ("a0", -127, 127), ("mix", 0, W - 1), ("s0", 0, S - 1)):
        v = np.asarray(d[k]).astype(np.float64)
        if not (np.min(v) >= lo and np.max(v) <= hi): bad.append("range of " + k)
        elif np.any(v != np.floor(v)): bad.append("whole numbers in " + k)
    return bad
def reference(mu, fr, a0, mix, s0):
    mi = mu.astype(np.float32).astype(np.int32).reshape(N, 8, 16, W)
    mf = np.ascontiguousarray(mi.reshape(N, 8, 16, C, B).transpose(0, 1, 3, 2, 4)).astype(np.float64)
    x = fr.astype(np.float32).astype(np.int32).reshape(N, 8, 16, R, U)
    a = a0.astype(np.float32).astype(np.int64).reshape(N, 8, 16, C, 16).transpose(0, 1, 3, 2, 4)
    lst = mix.astype(np.int64).reshape(N, 8, 16, S)
    s = np.stack([gentries(v) for v in s0]).astype(np.int64)
    yw = np.zeros((N, 8, R, U), np.float32)
    gi = np.arange(8)[:, None, None, None]; si = np.arange(16)[None, None, :, None]
    for t in range(R):
        z = np.matmul(a.astype(np.float64), mf).astype(np.int64)
        M = np.clip((z + 32) >> 6, -8, 7).astype(np.int32).transpose(0, 1, 3, 2, 4).reshape(N, 8, 16, W)
        G = np.zeros((8, C, 16, 16), np.int64); n = np.zeros((8, C), np.int64); new = []
        for r in range(N):
            st = (s[r][:, None, :] + np.arange(H)[None, :, None]) & (S - 1)
            cand = lst[r][gi, si, st[:, :, None, :]].reshape(8, 16 * H, U)
            mc = np.take_along_axis(M[r], cand.reshape(8, 1, 16 * H * U), 2).reshape(8, 16, 16 * H, U)
            xt = x[r, :, :, t]
            score = np.add.reduce(mc * (2 * xt[:, :, None, :] - mc), axis=1)
            k = np.argmax(score, axis=1)
            w = np.take_along_axis(cand, k[:, None, :], 1)[:, 0]
            e = xt - np.take_along_axis(M[r], w[:, None, :], 2)
            v = np.take_along_axis(mi[r], w[:, None, :], 2)
            hit = (w >> 9)[:, None, :] == np.arange(C)[None, :, None]
            left = (hit[:, :, None, :] * e[:, None]).astype(np.float64)
            G = G + np.matmul(left, v.transpose(0, 2, 1)[:, None].astype(np.float64)).astype(np.int64)
            n = n + np.add.reduce(hit.astype(np.int64), axis=2)
            yw[r, :, t] = w
            new.append((s[r] + (k >> 4)) & (S - 1))
        s = np.stack(new)
        took = np.zeros((8, C), bool); D = np.zeros_like(G)
        for l in range(LC + 1):
            gs = np.repeat(np.add.reduce(G.reshape(8, C >> l, 1 << l, 16, 16), axis=2), 1 << l, axis=1)
            ns = np.repeat(np.add.reduce(n.reshape(8, C >> l, 1 << l), axis=2), 1 << l, axis=1)
            now = (ns >= TH) & ~took
            D = np.where(now[:, :, None, None], gs, D); took = took | now
        a = np.clip(a + np.clip(D >> SH, -2, 2)[None], -127, 127)
    ya = np.ascontiguousarray(a.transpose(0, 1, 3, 2, 4)).reshape(N, 128, 16 * C)
    return {"ya": ya.astype(np.float32), "ys": s.astype(np.float32), "yw": yw.reshape(N, 8, R * U)}

@@ -1,0 +1,544 @@
+import numpy as np
+from concourse.bass import DstId, RemoteDMATransfer
+from concourse.mybir import AluOpType, AxisListType, ActivationFunctionType
+
+F, BF, I, U = "float32", "bfloat16", "int32", "uint16"
+R = 3
+SB = {
+    "mus": (4096, BF), "mixs": (2056, I), "frs": (384, BF), "a0s": (128, BF), "st": (8, I),
+    "mtab": (4096, BF), "dif": (6144, BF), "mg": (1024, BF), "xp": (384, BF), "x192": (384, BF), "xrep": (6144, BF),
+    "xtn": (384, BF), "bd": (1024, BF), "asum": (128, BF), "acl": (128, F), "am3": (128, F), "anat": (128, F),
+    "afin": (128, F), "yas": (128, F),
+    "lst": (48, U), "cand": (768, F), "tr": (768, F), "candt": (384, F), "hi": (384, BF), "offm": (384, U),
+    "sc": (768, F), "m01": (16, F), "mk": (16, I), "b0": (16, I), "b1": (16, I), "b2": (24, I), "off": (24, U), "hw": (8, I),
+    "s1": (8, I), "en": (128, BF), "muw": (128, BF), "win": (1024, BF), "em": (1024, BF), "junk": (128, F), "ncol": (4, F),
+    "s4": (80, F), "s2": (40, F), "yy": (40, F), "tt": (4, F), "osel": (2, U), "dcl": (16, F),
+    "w32": (32, F), "wexp": (512, F), "outs": (512, F),
+    "pi": (8, I), "pf": (16, F), "xi": (144, F), "ones": (512, BF), "ident": (128, BF), "i64": (128, BF), "in65": (128, BF), "in1": (128, BF),
+    "identf": (128, F), "za": (144, BF), "dlt": (392, BF), "stp": (384, F), "eb": (24, F), "i16": (16, BF), "i16x": (16, BF), "m16": (16, F), "bg": (8, F),
+    "lo": (8, F), "up": (8, F), "r64": (128, BF), "kca": (384, BF), "kcb": (384, BF), "ucon": (8, F), "nt": (24, F), "ci": (24, I),
+    "cf": (24, F), "biasl": (128, BF), "rst": (256, F), "ee": (512, BF), "io": (72, F), "lsel": (24, U), "lperm": (24, U),
+    "lx": (24, U), "lfin": (8, U), "z8": (8, F),
+}
+SCRATCH = {"b_" + k: ("sbuf", [128, n], d) for k, (n, d) in SB.items()}
+SCRATCH["b_mz"] = ("sbuf", [128, 8, 240], BF)
+SHAPE = {k: (n,) for k, (n, d) in SB.items()}
+SHAPE["mz"] = (8, 240)
+for _t in range(R):
+    SCRATCH["b_msg%d" % _t] = ("sbuf", [128, 8, 20], F)
+    SCRATCH["b_land%d" % _t] = ("sbuf", [128, 8, 20], F)
+    SCRATCH["b_dl%d" % _t] = ("sbuf", [128, 128], BF)
+    SHAPE["msg%d" % _t] = (8, 20)
+    SHAPE["land%d" % _t] = (8, 20)
+    SHAPE["dl%d" % _t] = (128,)
+for _b in range(8):
+    SCRATCH["b_ps%d" % _b] = ("psum", [128, 512], F)
+    SHAPE["ps%d" % _b] = (512,)
+DMAS = ["d_s0", "d_a0", "d_fr", "d_mix", "d_mu0", "d_mu1", "d_mu2", "d_mu3", "d_yw", "d_ys", "d_ya"]
+SEMAPHORES = ["qv", "qa", "qp", "qg", "sent"] + DMAS + ["ar%d" % t for t in range(R)] + ["dr%d" % t for t in range(R)]
+
+ALL = slice(None)
+
+
+def rank_program(g, core, T, topo):
+    rank = T.rank_of(core)
+    if rank is None:
+        return
+    N = len(T.cores)
+    Op, Fn = AluOpType, ActivationFunctionType
+    Q = {"v": g.vector, "a": g.scalar, "p": g.tensor, "g": g, "s": g.sync}
+    ops = []
+    hist = {}
+    index = {k: np.arange(int(np.prod(s))).reshape(s) for k, s in SHAPE.items()}
+
+    def V(name, *idx, part=ALL):
+        if not idx:
+            idx = (ALL,) * len(SHAPE[name])
+        bits = np.zeros(index[name].size + 8, np.uint8)
+        bits[index[name][idx].reshape(-1)] = 1
+        return (T["b_" + name][(part,) + tuple(idx)], [(name, int.from_bytes(np.packbits(bits).tobytes(), "big"))])
+
+    def C(name, a, b, step=1, part=ALL):
+        return V(name, slice(a, b, step), part=part)
+
+    def IND(win, offs):
+        return (win[0].indirect(offs[0]), win[1], offs[1])
+
+    def emit(q, call, reads, writes, sem=None, count=0):
+        me = len(ops)
+        deps = set()
+        acc = []
+        for r in reads:
+            if isinstance(r, tuple):
+                for part in r[1:]:
+                    acc += [(n, m, False) for n, m in part]
+        for w in writes:
+            acc += [(n, m, True) for n, m in w[1]]
+            for part in w[2:]:
+                acc += [(n, m, False) for n, m in part]
+        for n, m, wr in acc:
+            psum = n.startswith("ps")
+            for (m2, o, wr2) in hist.get(n, []):
+                same = ops[o][0] == q and ops[o][3] is None and sem is None
+                if psum and not same:
+                    deps.add(o)
+                elif (m & m2) and (wr or wr2) and not (same and q == "p"):
+                    deps.add(o)
+        ops.append([q, call, deps, sem, count])
+        for n, m, wr in acc:
+            h = hist.get(n, [])
+            if n.startswith("ps"):
+                h = [e for e in h if ops[e[1]][0] == q and (q != "p" or e[1] == me)]
+            if wr:
+                h = [e for e in h if (e[0] & ~m) or e[1] == me]
+            h.append((m, me, wr))
+            hist[n] = h
+        return me
+
+    def ap(x):
+        return x[0] if isinstance(x, tuple) else x
+
+    def ts(out, in0, s1, op0, s2=None, op1=None):
+        if op1 is None:
+            emit("v", lambda: g.vector.tensor_scalar(out[0], in0[0], ap(s1), None, op0), [in0, s1], [out])
+        else:
+            emit("v", lambda: g.vector.tensor_scalar(out[0], in0[0], ap(s1), ap(s2), op0, op1), [in0, s1, s2], [out])
+
+    def tt(out, in0, in1, op):
+        emit("v", lambda: g.vector.tensor_tensor(out[0], in0[0], in1[0], op), [in0, in1], [out])
+
+    def cp(out, in0):
+        emit("v", lambda: g.vector.tensor_copy(out[0], in0[0]), [in0], [out])
+
+    def ms(out, val):
+        emit("v", lambda: g.vector.memset(out[0], val), [], [out])
+
+    def act(out, in0, func=Fn.Identity, bias=0.0, scale=1.0, accum=None):
+        if accum is None:
+            emit("a", lambda: g.scalar.activation(out[0], in0[0], func, bias=ap(bias), scale=ap(scale)), [in0, bias, scale], [out])
+        else:
+            emit("a", lambda: g.scalar.activation(out[0], in0[0], func, accum_out=accum[0]), [in0], [out, accum])
+
+    def mm(out, lhsT, rhs, start, stop):
+        emit("p", lambda: g.tensor.matmul(out[0], lhsT[0], rhs[0], start, stop), [lhsT, rhs], [out])
+
+    def iota(out, pattern, base, cm, flt=True):
+        if flt:
+            emit("g", lambda: g.iota(out[0], pattern, base, cm, allow_small_or_imprecise_dtypes=True), [], [out])
+        else:
+            emit("g", lambda: g.iota(out[0], pattern, base, cm), [], [out])
+
+    def load(q, sem, out, src):
+        emit(q, lambda: Q[q].dma_start(out[0], src), [], [out], sem, 16)
+
+    def store(q, sem, dst, in0):
+        emit(q, lambda: Q[q].dma_start(dst, in0[0]), [in0], [], sem, 16)
+
+    def col(name, j):
+        return C(name, j, j + 1)
+
+    peers = [(rank + j) % N for j in range(1, N)]
+    common = topo.mask(core, T.cores[peers[0]])
+    for r in peers:
+        common &= topo.mask(core, T.cores[r])
+    engines = [e for e in topo.engines(core, T.cores[peers[0]]) if common >> e & 1]
+    wide = 1
+    while 2 * wide <= len(engines):
+        wide *= 2
+    wide_mask = sum(1 << e for e in engines[:wide])
+
+    def dst(r):
+        a = topo.addr(T.cores[r])
+        return DstId(rid=a[0], pnc=a[1])
+
+    sent = [0]
+
+    load("a", "d_s0", V("st"), T.s0[:])
+    load("s", "d_mix", C("mixs", 0, 2048), T.mix[:])
+    load("a", "d_a0", V("a0s"), T.a0[:])
+    load("a", "d_fr", V("frs"), T.fr[:])
+    for k in range(4):
+        load("s", "d_mu%d" % k, C("mus", 1024 * k, 1024 * (k + 1)), T.mu[:, 1024 * k:1024 * (k + 1)])
+
+    iota(col("pi", 0), [[1, 1]], 0, 1, False)
+    iota(C("io", 0, 24), [[128, 3], [2, 8]], 0, 0)
+    iota(V("xi"), [[1, 144]], 0, 0)
+    ms(V("ones"), 1.0)
+    emit("g", lambda: g.affine_select(T.b_ident[:], T.b_ones[:, 0:128], [[-1, 128]], Op.is_equal, 0.0, 0, 1), [C("ones", 0, 128)], [V("ident")])
+    iota(C("io", 24, 48), [[256, 3], [2, 8]], 0, 0)
+    iota(C("io", 48, 72), [[32, 24]], 0, 0)
+    iota(V("ci"), [[0, 3], [1, 8]], 0, 0, False)
+    one = slice(0, 1)
+    emit("g", lambda: g.affine_select(T.b_ee[:], T.b_ones[:], [[1, 4], [16, 8], [0, 16]], Op.is_equal, 0.0, 0, -1), [V("ones")], [V("ee")])
+    iota(V("kca", part=one), [[1024, 3], [0, 8], [64, 16]], -192, 0)
+    iota(V("kcb", part=one), [[0, 384]], 0, 0)
+    iota(V("rst"), [[0, 256]], 0, 0)
+    iota(V("z8"), [[0, 8]], 0, 0)
+    for t in range(R):
+        iota(V("msg%d" % t, ALL, 19), [[0, 8]], 0, 0)
+    iota(V("win"), [[0, 1024]], 0, 0)
+    for k in range(8):
+        iota(V("mz", k, ALL), [[0, 240]], 0, 0)
+    p0 = col("pi", 0)
+    ts(col("pi", 1), p0, 15, Op.bitwise_and)
+    ts(col("pi", 2), p0, 4, Op.logical_shift_right)
+    ts(col("pi", 3), p0, 7, Op.bitwise_and)
+    ts(col("pi", 4), p0, 3, Op.logical_shift_right, 1, Op.bitwise_and)
+    ts(col("pi", 5), p0, 31, Op.bitwise_and)
+    ts(col("pi", 6), p0, 1, Op.logical_shift_right, 7, Op.bitwise_and)
+    ts(col("pi", 7), p0, 2, Op.logical_shift_right, 3, Op.bitwise_and)
+    cp(C("pf", 0, 8), V("pi"))
+    pq, pg, pq8, pqh, p32 = col("pf", 1), col("pf", 2), col("pf", 3), col("pf", 4), col("pf", 5)
+    ts(col("pf", 8), pq8, 16.0, Op.mult, pqh, Op.add)
+    ts(col("pf", 9), pq8, 32.0, Op.mult, pqh, Op.add)
+    ts(col("pf", 10), pg, 16.0, Op.mult, 15.0, Op.add)
+    ts(V("bg"), C("xi", 0, 8), pg, Op.is_equal)
+    ts(V("i16"), C("xi", 0, 16), pq, Op.is_equal)
+    ts(V("lx"), C("io", 0, 24), col("pf", 8), Op.add)
+    ts(V("lo"), V("bg"), -127.0 / 64, Op.mult)
+    ts(V("up"), V("bg"), 127.0 / 64, Op.mult)
+    ts(V("lperm"), C("io", 24, 48), col("pf", 9), Op.add)
+    ts(V("lsel"), C("io", 48, 72), p32, Op.add)
+    ms(V("biasl", part=slice(0, 32)), 6.0)
+    ms(V("biasl", part=slice(32, 64)), 1.0 / 4096)
+    ms(V("r64", part=one), 64.0)
+    ts(V("za"), V("xi"), col("pf", 10), Op.is_equal, 262144.0, Op.mult)
+    ts(V("ucon"), C("xi", 0, 8), 16.0, Op.mult, pq, Op.add)
+    ts(col("pf", 11), pq, 8.0, Op.mult)
+    ts(col("pf", 12), col("pf", 6), 20.0, Op.add)
+    ts(col("pf", 13), col("pf", 7), 28.0, Op.add)
+    ts(col("pf", 14), pqh, 32.0, Op.add)
+    cp(C("b1", 8, 16), V("ucon"))
+    ts(V("lfin"), C("xi", 0, 8), col("pf", 11), Op.add)
+
+    def block_diagonal(src):
+        for k in range(8):
+            ts(C("bd", 128 * k, 128 * (k + 1)), src, col("lo", k), Op.max, col("up", k), Op.min)
+
+    def state_list():
+        for h in range(3):
+            for x in range(2):
+                ts(C("lst", 16 * h + x, 16 * h + 16, 2), V("st"), float(h), Op.add)
+
+    def spread_frames(t):
+        for i in range(16):
+            act(C("xrep", 2048 * t + i, 2048 * (t + 1), 16), C("xp", 128 * t, 128 * (t + 1)))
+
+    ts(V("asum"), IND(V("a0s"), C("lx", 0, 8)), 1.0 / 64, Op.mult)
+    ts(V("xp"), IND(V("frs"), V("lx")), 192.0, Op.add)
+    block_diagonal(V("asum"))
+    for c in range(8):
+        mm(C("ps4", c, 128, 8), C("bd", c, 1024, 8), V("i16"), True, True)
+    spread_frames(0)
+    for t in range(R):
+        mm(C("ps5", 128 * t, 128 * (t + 1)), C("frs", 128 * t, 128 * (t + 1)), V("ident"), True, True)
+    state_list()
+    cp(V("asum"), C("ps4", 0, 128))
+    block_diagonal(V("asum"))
+    act(V("xtn"), C("ps5", 0, 384), scale=-1.0)
+    act(V("i64"), V("ident"), scale=64.0)
+    act(V("in65"), V("ident"), scale=-65.0)
+    act(V("in1"), V("ident"), scale=-1.0)
+    act(V("identf"), V("ident"))
+    act(V("x192"), V("frs"), bias=192.0)
+    act(V("i16x"), V("i16"), scale=64.0)
+    act(V("m16"), V("i16"))
+    ts(C("ci", 8, 16), C("ci", 8, 16), 1, Op.logical_shift_right)
+    ts(C("ci", 16, 24), C("ci", 16, 24), 2, Op.logical_shift_right)
+    ts(col("pi", 6), p0, 1, Op.logical_shift_right, 3, Op.bitwise_and)
+    ts(col("pi", 7), p0, 2, Op.logical_shift_right, 1, Op.bitwise_and)
+    cp(V("cf"), V("ci"))
+    cp(C("pf", 6, 8), C("pi", 6, 8))
+    for l, j in ((0, 3), (1, 6), (2, 7)):
+        ts(C("cf", 8 * l, 8 * l + 8), C("cf", 8 * l, 8 * l + 8), col("pf", j), Op.is_equal, -64.0, Op.mult)
+    ts(V("nt"), V("cf"), 18.75, Op.add)
+    ms(C("rst", 0, 256, 16), 4.0e9)
+    ms(C("kcb", 0, 384, 16, part=one), 4.0e9)
+    ms(col("dlt", 0), 0.0)
+
+    def keep_matrices():
+        ts(V("acl"), V("asum"), -127.0 / 64, Op.max, 127.0 / 64, Op.min)
+        act(V("am3"), V("acl"), bias=-3.0)
+
+    def candidates_a():
+        cp(V("cand"), IND(C("mixs", 0, 2050), V("lst")))
+
+    def bias(bank):
+        mm(V(bank), V("biasl", part=slice(0, 64)), V("ones", part=slice(0, 64)), True, False)
+
+    def candidates_b():
+        emit("v", lambda: g.vector.transpose(T.b_tr[:], T.b_cand[:]), [V("cand")], [V("tr")])
+        cp(V("offm"), IND(V("cand"), V("lperm")))
+
+    def key_terms():
+        act(V("candt"), IND(V("tr"), V("lsel")))
+        act(V("hi"), V("candt"), bias=192.0 - 0.5 + 1.0 / 128, scale=1.0 / 64)
+        work = C("ps1", 0, 384)
+        mm(work, V("identf"), V("candt"), True, False)
+        mm(work, V("in65"), V("hi"), False, True)
+
+    def key_terms_b():
+        work = C("ps1", 0, 384)
+        act(C("dlt", 1, 385), work, bias=64.0 * 65 * 192, scale=64.0)
+        for ba, a, b in (("ps0", 0, 256), ("ps2", 256, 384)):
+            mm(C(ba, 0, b - a), V("r64", part=one), C("kca", a, b, part=one), True, False)
+            mm(C(ba, 0, b - a), V("i64"), C("hi", a, b), False, False)
+        mm(work, C("ones", 0, 128, part=one), V("kcb", part=one), True, False)
+        mm(work, V("ident"), C("dlt", 0, 384), False, False)
+        mm(work, V("in1"), C("dlt", 1, 385), False, True)
+
+    def key_steps():
+        act(V("stp"), C("ps1", 0, 384))
+
+    bias("ps6")
+    bias("ps7")
+    bias("ps3")
+    cp(C("mixs", 2048, 2050), C("mixs", 0, 2))
+    candidates_a()
+    candidates_b()
+
+    for t in range(R):
+        last = t == R - 1
+        def cls(name, c):
+            return C(name, 512 * c, 512 * (c + 1))
+
+        def prod(c, bank, start):
+            mm(V(bank), C("bd", c, 1024, 8), cls("mus", c), start, True)
+
+        def by_scalar(c, bank):
+            act(cls("mtab", c), V(bank), bias=192.0 + 1.0 / 128)
+
+        def by_vector(c, bank):
+            ts(cls("mtab", c), V(bank), 184.0, Op.max, 199.0, Op.min)
+
+        def clip(c):
+            ts(cls("mtab", c), cls("mtab", c), 184.0, Op.max, 199.0, Op.min)
+
+        prod(0, "ps4", True); prod(1, "ps6", False); prod(2, "ps5", True); prod(3, "ps7", False)
+        by_scalar(0, "ps4"); by_vector(1, "ps6"); by_scalar(2, "ps5"); clip(0)
+        prod(4, "ps4", True); prod(5, "ps3", False)
+        if t == 0:
+            key_terms()
+        by_vector(3, "ps7"); by_scalar(4, "ps4"); clip(2)
+        prod(6, "ps5", True); by_scalar(6, "ps5"); clip(4)
+        prod(7, "ps6", True); by_vector(5, "ps3"); by_scalar(7, "ps6"); clip(6); clip(7)
+        if t > 0:
+            key_steps()
+        else:
+            key_terms_b()
+
+        def span(h, u0, u1):
+            return 2048 * h + 128 * u0, 2048 * h + 128 * u1
+
+        def offs(h, u0, u1):
+            return C("offm", 128 * h + 8 * u0, 128 * h + 8 * u1)
+
+        def gather_v(h, u0, u1):
+            a, b = span(h, u0, u1)
+            tt(C("dif", a, b), IND(V("mtab"), offs(h, u0, u1)), C("xrep", 2048 * t + 128 * u0, 2048 * t + 128 * u1), Op.subtract)
+
+        def sums(h, u0, u1, stop):
+            ba, o = ("ps0", 128 * h) if h < 2 else ("ps2", 0)
+            for u in range(u0, u1):
+                a, b = span(h, u, u + 1)
+                mm(C(ba, o, o + 128), C("za", 15 - u, 143 - u), C("dif", a, b), False, stop and u == u1 - 1)
+
+        def square(h, u0, u1, stop=False):
+            a, b = span(h, u0, u1)
+            act(C("dif", a, b), C("dif", a, b), Fn.Square)
+            sums(h, u0, u1, stop)
+
+        def gather_a(h):
+            m = C("mg", 512 * h, 512 * (h + 1))
+            act(m, IND(V("mtab"), offs(h, 0, 4)))
+            mm(V("ps%d" % (4 + h)), C("xtn", 128 * t, 128 * (t + 1)), V("ee"), True, False)
+            mm(V("ps%d" % (4 + h)), V("ident"), m, False, True)
+
+        def square_a(h):
+            a, b = span(h, 0, 4)
+            act(C("dif", a, b), V("ps%d" % (4 + h)), Fn.Square, bias=-192.0)
+            sums(h, 0, 4, False)
+
+        chunks = [(0, 4, 8), (0, 8, 12), (0, 12, 16), (1, 4, 8), (1, 8, 12), (1, 12, 16),
+                  (2, 0, 4), (2, 4, 8), (2, 8, 12), (2, 12, 14), (2, 14, 15), (2, 15, 16)]
+        for ch in chunks:
+            gather_v(*ch)
+        gather_a(0)
+        if t == 0:
+            key_steps()
+        square(*chunks[0]); gather_a(1); square_a(0); square(*chunks[1]); square(*chunks[2]); square_a(1)
+        for k in range(3, len(chunks)):
+            square(*chunks[k], stop=k in (5, len(chunks) - 1))
+
+        def scan(key, a, b):
+            src = C("ps0", a, b) if a < 256 else C("ps2", a - 256, b - 256)
+            out = C("sc", 384 * key + a, 384 * key + b)
+            d0 = C("stp", a, b) if key else C("rst", 0, b - a)
+            emit("v", lambda: g.vector.tensor_tensor_scan(out[0], d0[0], src[0], 0.0, Op.add, Op.min), [d0, src], [out])
+
+        def ends(key, a, b):
+            return C("sc", 384 * key + a + 15, 384 * key + b, 16)
+
+        ka, kb = C("mk", 0, 8), C("mk", 8, 16)
+        scan(1, 0, 256); scan(0, 0, 256)
+        tt(C("eb", 0, 16), ends(1, 0, 256), C("dlt", 16, 257, 16), Op.add)
+        tt(C("m01", 0, 8), ends(0, 0, 128), ends(0, 128, 256), Op.min)
+        tt(C("m01", 8, 16), C("eb", 0, 8), C("eb", 8, 16), Op.min)
+        scan(1, 256, 384); scan(0, 256, 384)
+        tt(C("eb", 16, 24), ends(1, 256, 384), C("dlt", 272, 385, 16), Op.add)
+        tt(ka, C("m01", 0, 8), ends(0, 256, 384), Op.min)
+        tt(kb, C("m01", 8, 16), C("eb", 16, 24), Op.min)
+        ts(C("b0", 0, 8), ka, 0xFC0, Op.bitwise_and)
+        ts(C("b0", 8, 16), ka, 0xE00, Op.bitwise_and, 2, Op.logical_shift_right)
+        ts(C("b2", 16, 24), ka, 9, Op.logical_shift_right, 7, Op.bitwise_and)
+        ts(C("b1", 0, 8), kb, 6, Op.logical_shift_right, 63, Op.bitwise_and)
+        tt(C("b2", 0, 16), V("b0"), V("b1"), Op.add)
+        cp(V("off"), V("b2"))
+
+        ow, osc, ocl = C("off", 0, 8), C("off", 8, 16), C("off", 16, 24)
+        act(V("muw"), IND(V("mus"), ow))
+        tt(V("en"), IND(V("mtab"), ow), C("x192", 128 * t, 128 * (t + 1)), Op.subtract)
+        rows, cols = ("en", "muw") if last else ("muw", "en")
+        cp(IND(V("win"), osc), V(cols))
+        mm(C("ps6", 0, 128), V(rows), V("ident"), True, True)
+        msg, land, dl = "msg%d" % t, "land%d" % t, "dl%d" % t
+
+        def count(l):
+            act(V("junk"), IND(C("nt", 8 * l, 8 * l + 8), ocl), accum=col("ncol", l))
+
+        count(0); count(1)
+        act(V("mz", slice(0, 8), slice(112, 128)), C("ps6", 0, 128))
+        count(2)
+        for half in range(2):
+            for c in range(8):
+                mm(C("ps%d" % (4 + half), c, 512, 8), C("win", 128 * c, 128 * (c + 1)), C("ident", 64 * half, 64 * (half + 1)), True, True)
+        act(C("em", 0, 512), V("ps4"))
+        cp(C("em", 512, 1024), V("ps5"))
+        for l in range(3):
+            act(V(msg, ALL, 16 + l), V("z8"), bias=col("ncol", l))
+        for k in range(8):
+            mm(C("ps7", 0, 128), V("mz", k, slice(112 - 16 * k, 240 - 16 * k)), C("em", 128 * k, 128 * (k + 1)), k == 0, k == 7)
+        unit = 1.0 if last else 1.0 / 64
+        ts(V(msg, ALL, slice(0, 16)), C("ps7", 0, 128), -unit / 256, Op.mult)
+
+        def send_sums(msg=msg, land=land, t=t):
+            trs = [RemoteDMATransfer(dst_ids=[dst(r)], dma_engine_mask=1 << engines[j], remote_sem=T.sem["ar%d" % t],
+                                     src=T["b_" + msg][:, r, :], dst=T["b_" + land][:, rank, :]) for j, r in enumerate(peers)]
+            g.remote_dma_fused(trs, local_sem=T.sem.sent)
+        emit("g", send_sums, [V(msg)], [], "remote")
+        sent[0] += len(peers)
+
+        cp(V(land, rank, ALL), V(msg, rank, ALL))
+        ts(V("hw"), ka, 16, Op.logical_shift_right, 3, Op.bitwise_and)
+        cp(C("w32", 8 * t, 8 * t + 8), C("b2", 0, 8))
+        tt(V("s1"), V("st"), V("hw"), Op.add)
+        ts(V("st"), V("s1"), 2047, Op.bitwise_and)
+        if not last:
+            state_list()
+            spread_frames(t + 1)
+            bias("ps6"); bias("ps7"); bias("ps3")
+            candidates_a()
+        else:
+            cp(C("w32", 24, 32), V("st"))
+            for c in range(8):
+                mm(C("ps5", 16 * c, 16 * (c + 1)), C("bd", c, 1024, 8), V("i16x"), True, True)
+            for u in range(16):
+                act(C("wexp", u, 512, 16), V("w32"), scale=col("m16", u))
+            mm(V("ps4", part=slice(0, 8)), V("bg"), V("wexp"), True, True)
+            act(V("anat"), C("ps5", 0, 128), bias=-192.0)
+            act(V("outs", part=slice(0, 8)), V("ps4", part=slice(0, 8)))
+            store("s", "d_yw", T.yw[:], C("outs", 0, 384, part=slice(0, 8)))
+            store("s", "d_ys", T.ys[:], C("outs", 384, 512, part=slice(0, 8)))
+
+        emit("x", None, [], [V(land, r, ALL) for r in peers], "ar%d" % t, len(peers))
+        tt(V("s4"), V(land, slice(0, 4), ALL), V(land, slice(4, 8), ALL), Op.add)
+        tt(V("s2"), C("s4", 0, 40), C("s4", 40, 80), Op.add)
+        tt(C("yy", 0, 20), C("s2", 0, 20), C("s2", 20, 40), Op.add)
+        tt(C("yy", 20, 28), C("yy", 0, 16, 2), C("yy", 1, 16, 2), Op.add)
+        ts(col("tt", 0), col("yy", 16), pq, Op.max, col("pf", 12), Op.min)
+        tt(C("tt", 1, 3), C("yy", 17, 19), C("pf", 13, 15), Op.min)
+        for k in range(2):
+            o, s = col("yy", 32 + k), C("yy", 8 * k, 8 * k + 8)
+            emit("v", lambda o=o, s=s: g.vector.tensor_reduce(o[0], s[0], AxisListType.X, Op.add), [s], [o])
+        tt(C("yy", 28, 32), C("yy", 20, 28, 2), C("yy", 21, 28, 2), Op.add)
+        ts(col("osel", 0), col("tt", 0), col("tt", 1), Op.max, col("tt", 2), Op.max)
+        ts(V("dcl"), IND(C("yy", 0, 34), col("osel", 0)), -2.0 * unit, Op.max, 2.0 * unit, Op.min)
+        mine = C(dl, 16 * rank, 16 * rank + 16)
+        ts(mine, V("dcl"), (192.0 - 0.5 + 1.0 / 512) * unit, Op.add)
+
+        def send_steps(mine=mine, t=t):
+            tr = RemoteDMATransfer(dst_ids=[dst(r) for r in peers], dma_engine_mask=wide_mask, remote_sem=T.sem["dr%d" % t],
+                                   srcs=[mine[0]], dsts=[mine[0] for r in peers])
+            g.remote_dma_fused([tr], local_sem=T.sem.sent)
+        emit("g", send_steps, [mine], [], "remote")
+        sent[0] += wide
+
+        if not last:
+            keep_matrices()
+            candidates_b()
+            key_terms()
+            key_terms_b()
+            iota(V("win"), [[0, 1024]], 0, 0)
+        emit("x", None, [], [C(dl, 16 * r, 16 * r + 16) for r in peers], "dr%d" % t, wide * len(peers))
+        if not last:
+            tt(V("asum"), V("am3"), V(dl), Op.add)
+            block_diagonal(V("asum"))
+        else:
+            tt(V("afin"), IND(V(dl), V("lfin")), V("anat"), Op.add)
+            ts(V("yas"), V("afin"), -127.0, Op.max, 127.0, Op.min)
+            store("s", "d_ya", T.ya[:], V("yas"))
+
+    qsem = {"v": "qv", "a": "qa", "p": "qp", "g": "qg"}
+    known = {q: {} for q in Q}
+    clocks = []
+    waits = []
+    marked = set()
+    for i, (q, call, deps, sem, count) in enumerate(ops):
+        need = []
+        if q != "x":
+            kn = known[q]
+            for o in sorted(deps, reverse=True):
+                oq, osem = ops[o][0], ops[o][3]
+                if osem == "remote":
+                    continue
+                key = osem if osem is not None else oq
+                if osem is None and oq != "p":
+                    marked.add(o)
+                if kn.get(key, -1) >= o:
+                    continue
+                need.append(o)
+                marked.add(o)
+                for k2, v2 in clocks[o].items():
+                    if kn.get(k2, -1) < v2:
+                        kn[k2] = v2
+            ck = dict(kn)
+        else:
+            ck = {}
+        ck[sem if sem is not None else q] = i
+        clocks.append(ck)
+        waits.append(need)
+    number = {}
+    total = {q: 0 for q in qsem}
+    for i, o in enumerate(ops):
+        if o[3] is None and i in marked:
+            total[o[0]] += 1
+            number[i] = total[o[0]]
+    for i, (q, call, deps, sem, count) in enumerate(ops):
+        if q == "x":
+            continue
+        for o in waits[i]:
+            if ops[o][3] is None:
+                Q[q].wait_ge(T.sem[qsem[ops[o][0]]], number[o])
+            else:
+                Q[q].wait_ge(T.sem[ops[o][3]], ops[o][4])
+        ins = call()
+        if sem is None:
+            if i in number:
+                ins.then_inc(T.sem[qsem[q]], 1)
+        elif sem != "remote":
+            ins.then_inc(T.sem[sem], 16)
+    for q in qsem:
+        g.wait_ge(T.sem[qsem[q]], total[q])
+    g.wait_ge(T.sem.sent, sent[0])
+    for s in ("d_yw", "d_ys", "d_ya"):
+        g.sync.wait_ge(T.sem[s], 16)

@@ -6,38 +6,43 @@ F, BF, I, U = "float32", "bfloat16", "int32", "uint16"
 R = 3
 SB = {
     "mus": (4096, BF), "mixs": (2056, I), "frs": (384, BF), "a0s": (128, BF), "st": (8, I),
-    "mtab": (4096, BF), "dif": (6144, BF), "mg": (1024, BF), "xp": (384, BF), "x192": (384, BF), "xrep": (6144, BF),
-    "xtn": (384, BF), "bd": (1024, BF), "asum": (128, BF), "acl": (128, F), "am3": (128, F), "anat": (128, F),
+    "mtab": (4096, BF), "dif": (6144, BF), "mg": (1536, BF), "xp": (384, BF), "x192": (384, BF), "xrep": (6144, BF),
+    "xtn": (384, BF), "bd": (1024, BF), "asum": (128, BF), "acl": (128, F), "anat": (128, F),
     "afin": (128, F), "yas": (128, F),
-    "lst": (48, U), "cand": (768, F), "tr": (768, F), "candt": (384, F), "hi": (384, BF), "offm": (384, U),
-    "sc": (768, F), "m01": (16, F), "mk": (16, I), "b0": (16, I), "b1": (16, I), "b2": (24, I), "off": (24, U), "hw": (8, I),
-    "s1": (8, I), "en": (128, BF), "muw": (128, BF), "win": (1024, BF), "em": (1024, BF), "junk": (128, F), "ncol": (4, F),
-    "s4": (80, F), "s2": (40, F), "yy": (40, F), "tt": (4, F), "osel": (2, U), "dcl": (16, F),
+    "lst": (24, U), "cand": (384, F), "tr": (384, F), "candt": (384, F), "hi": (384, BF), "offm": (384, U),
+    "sc": (768, F), "mk": (16, I), "b1": (16, I), "b2": (32, I), "off": (24, U), "hw": (8, I),
+    "s1": (8, I), "en": (128, BF), "muw": (128, BF), "win": (1024, BF), "em": (1024, BF), "junk": (384, F), "ncol": (4, F),
+    "s4": (80, F), "s2": (40, F), "yy": (72, F), "tt": (4, F), "osel": (2, U), "dcl": (16, F),
     "w32": (32, F), "wexp": (512, F), "outs": (512, F),
-    "pi": (8, I), "pf": (16, F), "xi": (144, F), "ones": (512, BF), "ident": (128, BF), "i64": (128, BF), "in65": (128, BF), "in1": (128, BF),
-    "identf": (128, F), "za": (144, BF), "dlt": (392, BF), "stp": (384, F), "eb": (24, F), "i16": (16, BF), "i16x": (16, BF), "m16": (16, F), "bg": (8, F),
-    "lo": (8, F), "up": (8, F), "r64": (128, BF), "kca": (384, BF), "kcb": (384, BF), "ucon": (8, F), "nt": (24, F), "ci": (24, I),
-    "cf": (24, F), "biasl": (128, BF), "rst": (256, F), "ee": (512, BF), "io": (72, F), "lsel": (24, U), "lperm": (24, U),
-    "lx": (24, U), "lfin": (8, U), "z8": (8, F),
+    "pi": (8, I), "pf": (24, F), "xi": (176, F), "ones": (512, BF), "ident": (128, BF), "in65": (128, BF),
+    "identf": (128, F), "za": (144, BF), "dlt": (392, BF), "stp": (400, F), "i16": (16, BF), "i16x": (16, BF), "m16": (16, F), "bg": (8, F),
+    "lo": (8, F), "up": (8, F), "r64": (128, BF), "kca": (192, BF), "kcb": (400, BF), "nt": (24, F), "na": (24, F),
+    "biasl": (128, BF), "rst": (192, F), "ee": (512, BF), "io": (80, F), "i3": (24, I), "lf": (24, F), "lsel": (24, U), "lperm": (24, U),
+    "l0": (8, U), "la": (8, U), "lfin": (8, U), "z8": (8, F), "selp": (320, BF), "seln": (320, BF), "sel64": (320, BF),
+    "sd": (48, F), "pp": (4, F),
 }
 SCRATCH = {"b_" + k: ("sbuf", [128, n], d) for k, (n, d) in SB.items()}
 SCRATCH["b_mz"] = ("sbuf", [128, 8, 240], BF)
 SHAPE = {k: (n,) for k, (n, d) in SB.items()}
 SHAPE["mz"] = (8, 240)
 for _t in range(R):
-    SCRATCH["b_msg%d" % _t] = ("sbuf", [128, 8, 20], F)
-    SCRATCH["b_land%d" % _t] = ("sbuf", [128, 8, 20], F)
+    SCRATCH["b_msg%d" % _t] = ("sbuf", [128, 8, 5, 4], F)
+    SCRATCH["b_land%d" % _t] = ("sbuf", [128, 8, 5, 4], F)
     SCRATCH["b_dl%d" % _t] = ("sbuf", [128, 128], BF)
-    SHAPE["msg%d" % _t] = (8, 20)
-    SHAPE["land%d" % _t] = (8, 20)
+    SHAPE["msg%d" % _t] = (8, 5, 4)
+    SHAPE["land%d" % _t] = (8, 5, 4)
     SHAPE["dl%d" % _t] = (128,)
 for _b in range(8):
-    SCRATCH["b_ps%d" % _b] = ("psum", [128, 512], F)
-    SHAPE["ps%d" % _b] = (512,)
-DMAS = ["d_s0", "d_a0", "d_fr", "d_mix", "d_mu0", "d_mu1", "d_mu2", "d_mu3", "d_yw", "d_ys", "d_ya"]
+    SCRATCH["b_ps%d" % _b] = ("psum", [128, 128, 4, 2], BF) if _b == 2 else ("psum", [128, 512], F)
+    SHAPE["ps%d" % _b] = (128, 4, 2) if _b == 2 else (512,)
+DMAS = ["d_s0", "d_a0", "d_fr", "d_mix", "d_mu0", "d_mu1", "d_mu2", "d_mu3", "d_mu4", "d_yw", "d_ys", "d_ya"]
 SEMAPHORES = ["qv", "qa", "qp", "qg", "sent"] + DMAS + ["ar%d" % t for t in range(R)] + ["dr%d" % t for t in range(R)]
 
 ALL = slice(None)
+PARTS = [(0, 4, "ps0", 0), (4, 4, "ps1", 64)]
+CHUNKS = [(0, 0, 8, 16), (0, 1, 8, 16), (0, 2, 0, 16), (1, 0, 0, 16), (1, 1, 0, 8), (1, 1, 8, 16), (1, 2, 0, 7), (1, 2, 7, 12), (1, 2, 12, 15),
+          (1, 2, 15, 16)]
+LOADS = [0, 1024, 2048, 3072, 3584, 4096]
 
 
 def rank_program(g, core, T, topo):
@@ -113,20 +118,29 @@ def rank_program(g, core, T, topo):
     def ms(out, val):
         emit("v", lambda: g.vector.memset(out[0], val), [], [out])
 
+    def scan(out, d0, d1, init, op0, op1):
+        emit("v", lambda: g.vector.tensor_tensor_scan(out[0], d0[0], d1[0], ap(init), op0, op1), [d0, d1, init], [out])
+
     def act(out, in0, func=Fn.Identity, bias=0.0, scale=1.0, accum=None):
         if accum is None:
             emit("a", lambda: g.scalar.activation(out[0], in0[0], func, bias=ap(bias), scale=ap(scale)), [in0, bias, scale], [out])
         else:
-            emit("a", lambda: g.scalar.activation(out[0], in0[0], func, accum_out=accum[0]), [in0], [out, accum])
+            emit("a", lambda: g.scalar.activation(out[0], in0[0], func, bias=bias, scale=scale, accum_out=accum[0]), [in0], [out, accum])
 
     def mm(out, lhsT, rhs, start, stop):
         emit("p", lambda: g.tensor.matmul(out[0], lhsT[0], rhs[0], start, stop), [lhsT, rhs], [out])
+
+    def turn(out, in0, ident):
+        emit("p", lambda: g.tensor.transpose(out[0], in0[0], ident[0]), [in0, ident], [out])
 
     def iota(out, pattern, base, cm, flt=True):
         if flt:
             emit("g", lambda: g.iota(out[0], pattern, base, cm, allow_small_or_imprecise_dtypes=True), [], [out])
         else:
             emit("g", lambda: g.iota(out[0], pattern, base, cm), [], [out])
+
+    def select(out, in0, pattern, op, base, cm, fill=0.0):
+        emit("g", lambda: g.affine_select(out[0], in0[0], pattern, op, fill, base, cm), [in0], [out])
 
     def load(q, sem, out, src):
         emit(q, lambda: Q[q].dma_start(out[0], src), [], [out], sem, 16)
@@ -138,6 +152,11 @@ def rank_program(g, core, T, topo):
         return C(name, j, j + 1)
 
     peers = [(rank + j) % N for j in range(1, N)]
+
+    def nearness(r):
+        a, b = topo.chip(core), topo.chip(T.cores[r])
+        return 2 if topo.mates(a, b) else 1 if topo.same_plane(a, b) else 0
+    peers.sort(key=nearness)
     common = topo.mask(core, T.cores[peers[0]])
     for r in peers:
         common &= topo.mask(core, T.cores[r])
@@ -153,63 +172,57 @@ def rank_program(g, core, T, topo):
 
     sent = [0]
 
-    load("a", "d_s0", V("st"), T.s0[:])
-    load("s", "d_mix", C("mixs", 0, 2048), T.mix[:])
-    load("a", "d_a0", V("a0s"), T.a0[:])
+    load("s", "d_a0", V("a0s"), T.a0[:])
     load("a", "d_fr", V("frs"), T.fr[:])
-    for k in range(4):
-        load("s", "d_mu%d" % k, C("mus", 1024 * k, 1024 * (k + 1)), T.mu[:, 1024 * k:1024 * (k + 1)])
+    load("s", "d_s0", V("st"), T.s0[:])
+    load("s", "d_mix", C("mixs", 0, 2048), T.mix[:])
+    for k in range(5):
+        load("s", "d_mu%d" % k, C("mus", LOADS[k], LOADS[k + 1]), T.mu[:, LOADS[k]:LOADS[k + 1]])
+
+    one = slice(0, 1)
+
+    def xi(a, b):
+        return C("xi", 16 + a, 16 + b)
 
     iota(col("pi", 0), [[1, 1]], 0, 1, False)
-    iota(C("io", 0, 24), [[128, 3], [2, 8]], 0, 0)
-    iota(V("xi"), [[1, 144]], 0, 0)
+    iota(C("io", 0, 8), [[2, 8]], 0, 0)
+    iota(C("io", 8, 32), [[64, 2], [128, 3], [4, 4]], 0, 0)
+    iota(V("xi"), [[1, 176]], -16, 0)
     ms(V("ones"), 1.0)
-    emit("g", lambda: g.affine_select(T.b_ident[:], T.b_ones[:, 0:128], [[-1, 128]], Op.is_equal, 0.0, 0, 1), [C("ones", 0, 128)], [V("ident")])
-    iota(C("io", 24, 48), [[256, 3], [2, 8]], 0, 0)
-    iota(C("io", 48, 72), [[32, 24]], 0, 0)
-    iota(V("ci"), [[0, 3], [1, 8]], 0, 0, False)
-    one = slice(0, 1)
-    emit("g", lambda: g.affine_select(T.b_ee[:], T.b_ones[:], [[1, 4], [16, 8], [0, 16]], Op.is_equal, 0.0, 0, -1), [V("ones")], [V("ee")])
-    iota(V("kca", part=one), [[1024, 3], [0, 8], [64, 16]], -192, 0)
-    iota(V("kcb", part=one), [[0, 384]], 0, 0)
-    iota(V("rst"), [[0, 256]], 0, 0)
-    iota(V("z8"), [[0, 8]], 0, 0)
-    for t in range(R):
-        iota(V("msg%d" % t, ALL, 19), [[0, 8]], 0, 0)
-    iota(V("win"), [[0, 1024]], 0, 0)
-    for k in range(8):
-        iota(V("mz", k, ALL), [[0, 240]], 0, 0)
-    p0 = col("pi", 0)
-    ts(col("pi", 1), p0, 15, Op.bitwise_and)
-    ts(col("pi", 2), p0, 4, Op.logical_shift_right)
-    ts(col("pi", 3), p0, 7, Op.bitwise_and)
-    ts(col("pi", 4), p0, 3, Op.logical_shift_right, 1, Op.bitwise_and)
-    ts(col("pi", 5), p0, 31, Op.bitwise_and)
-    ts(col("pi", 6), p0, 1, Op.logical_shift_right, 7, Op.bitwise_and)
-    ts(col("pi", 7), p0, 2, Op.logical_shift_right, 3, Op.bitwise_and)
-    cp(C("pf", 0, 8), V("pi"))
-    pq, pg, pq8, pqh, p32 = col("pf", 1), col("pf", 2), col("pf", 3), col("pf", 4), col("pf", 5)
-    ts(col("pf", 8), pq8, 16.0, Op.mult, pqh, Op.add)
-    ts(col("pf", 9), pq8, 32.0, Op.mult, pqh, Op.add)
-    ts(col("pf", 10), pg, 16.0, Op.mult, 15.0, Op.add)
-    ts(V("bg"), C("xi", 0, 8), pg, Op.is_equal)
-    ts(V("i16"), C("xi", 0, 16), pq, Op.is_equal)
-    ts(V("lx"), C("io", 0, 24), col("pf", 8), Op.add)
-    ts(V("lo"), V("bg"), -127.0 / 64, Op.mult)
-    ts(V("up"), V("bg"), 127.0 / 64, Op.mult)
-    ts(V("lperm"), C("io", 24, 48), col("pf", 9), Op.add)
-    ts(V("lsel"), C("io", 48, 72), p32, Op.add)
+    iota(C("io", 32, 56), [[0, 8], [16, 3]], -1, 0)
+    iota(C("io", 56, 80), [[16, 2], [32, 4], [2048, 3]], 0, 0)
+    select(V("ident"), C("ones", 0, 128), [[-1, 128]], Op.is_equal, 0, 1)
+    iota(V("r64", part=one), [[0, 128]], 64, 0)
+    iota(V("kca", part=one), [[0, 4], [64, 16], [1024, 3]], -192, 0)
+    iota(col("dlt", 0), [[0, 1]], 0, 0)
+
+    for j, m in enumerate((15, 14, 12, 8, 16)):
+        ts(col("pi", 1 + j), col("pi", 0), m, Op.bitwise_and)
+    cp(C("pf", 0, 6), C("pi", 0, 6))
+    pp_, pq, m1, m2, m3, m4 = [col("pf", j) for j in range(6)]
+    q16, ca, cb, cla, pg16, x1, x0, q128, zc, q8 = [col("pf", j) for j in range(6, 16)]
+    ts(q16, pq, 16.0, Op.mult)
+    ts(pg16, pp_, pq, Op.subtract)
+    ts(ca, m2, -15.75, Op.mult, q16, Op.add)
+    ts(cla, m3, -15.875, Op.mult, q16, Op.add)
+    ts(C("l0", 0, 4), C("io", 8, 12), ca, Op.add)
+    ts(C("l0", 4, 8), C("io", 20, 24), ca, Op.add)
+    ts(V("bg"), xi(0, 8), 16.0, Op.mult, pg16, Op.is_equal)
+    ts(V("la"), C("io", 0, 8), cla, Op.add)
+    act(q128, pq, scale=128.0)
+    act(x1, m4, scale=1.0 / 16)
+    act(x0, m4, scale=-1.0 / 16, bias=1.0)
+    act(zc, pg16, bias=15.0)
+    act(q8, pq, scale=8.0)
+    act(V("lo"), V("bg"), scale=-127.0 / 64)
+    act(V("up"), V("bg"), scale=127.0 / 64)
+    ts(V("i16"), xi(0, 16), pq, Op.is_equal)
+    ts(V("lperm"), C("io", 8, 32), ca, Op.add)
+    ts(V("i3"), C("io", 32, 56), pq, Op.add, 1.0 / 3, Op.mult)
     ms(V("biasl", part=slice(0, 32)), 6.0)
+    ts(V("lf"), V("i3"), -383.0, Op.mult, q128, Op.add)
     ms(V("biasl", part=slice(32, 64)), 1.0 / 4096)
-    ms(V("r64", part=one), 64.0)
-    ts(V("za"), V("xi"), col("pf", 10), Op.is_equal, 262144.0, Op.mult)
-    ts(V("ucon"), C("xi", 0, 8), 16.0, Op.mult, pq, Op.add)
-    ts(col("pf", 11), pq, 8.0, Op.mult)
-    ts(col("pf", 12), col("pf", 6), 20.0, Op.add)
-    ts(col("pf", 13), col("pf", 7), 28.0, Op.add)
-    ts(col("pf", 14), pqh, 32.0, Op.add)
-    cp(C("b1", 8, 16), V("ucon"))
-    ts(V("lfin"), C("xi", 0, 8), col("pf", 11), Op.add)
+    tt(V("lf"), V("lf"), C("io", 56, 80), Op.add)
 
     def block_diagonal(src):
         for k in range(8):
@@ -217,85 +230,127 @@ def rank_program(g, core, T, topo):
 
     def state_list():
         for h in range(3):
-            for x in range(2):
-                ts(C("lst", 16 * h + x, 16 * h + 16, 2), V("st"), float(h), Op.add)
+            ts(C("lst", 8 * h, 8 * h + 8), V("st"), float(h), Op.add)
 
-    def spread_frames(t):
-        for i in range(16):
-            act(C("xrep", 2048 * t + i, 2048 * (t + 1), 16), C("xp", 128 * t, 128 * (t + 1)))
+    def spread_frames(t, i0=0, i1=16):
+        for i in range(i0, i1):
+            select(C("xrep", 2048 * t + i, 2048 * (t + 1), 16), C("xp", 128 * t, 128 * (t + 1)), [[0, 128]], Op.is_ge, 0, 0)
 
-    ts(V("asum"), IND(V("a0s"), C("lx", 0, 8)), 1.0 / 64, Op.mult)
-    ts(V("xp"), IND(V("frs"), V("lx")), 192.0, Op.add)
+    for t in range(R):
+        act(C("xp", 128 * t, 128 * (t + 1)), IND(C("frs", 128 * t, 128 * (t + 1)), V("l0")), bias=192.0)
+    spread_frames(0)
+    ts(V("asum"), IND(V("a0s"), V("la")), 1.0 / 64, Op.mult)
+    cp(V("lsel"), V("lf"))
     block_diagonal(V("asum"))
     for c in range(8):
         mm(C("ps4", c, 128, 8), C("bd", c, 1024, 8), V("i16"), True, True)
-    spread_frames(0)
     for t in range(R):
         mm(C("ps5", 128 * t, 128 * (t + 1)), C("frs", 128 * t, 128 * (t + 1)), V("ident"), True, True)
+    act(V("identf"), V("ident"))
+    act(V("in65"), V("ident"), scale=-65.0)
     state_list()
-    cp(V("asum"), C("ps4", 0, 128))
+    ts(C("selp", 0, 160), C("xi", 0, 160), pp_, Op.is_equal, x0, Op.mult)
+    act(V("asum"), C("ps4", 0, 128))
+    ts(C("selp", 160, 320), C("xi", 0, 160), pp_, Op.is_equal, x1, Op.mult)
     block_diagonal(V("asum"))
     act(V("xtn"), C("ps5", 0, 384), scale=-1.0)
-    act(V("i64"), V("ident"), scale=64.0)
-    act(V("in65"), V("ident"), scale=-65.0)
-    act(V("in1"), V("ident"), scale=-1.0)
-    act(V("identf"), V("ident"))
-    act(V("x192"), V("frs"), bias=192.0)
-    act(V("i16x"), V("i16"), scale=64.0)
-    act(V("m16"), V("i16"))
-    ts(C("ci", 8, 16), C("ci", 8, 16), 1, Op.logical_shift_right)
-    ts(C("ci", 16, 24), C("ci", 16, 24), 2, Op.logical_shift_right)
-    ts(col("pi", 6), p0, 1, Op.logical_shift_right, 3, Op.bitwise_and)
-    ts(col("pi", 7), p0, 2, Op.logical_shift_right, 1, Op.bitwise_and)
-    cp(V("cf"), V("ci"))
-    cp(C("pf", 6, 8), C("pi", 6, 8))
-    for l, j in ((0, 3), (1, 6), (2, 7)):
-        ts(C("cf", 8 * l, 8 * l + 8), C("cf", 8 * l, 8 * l + 8), col("pf", j), Op.is_equal, -64.0, Op.mult)
-    ts(V("nt"), V("cf"), 18.75, Op.add)
-    ms(C("rst", 0, 256, 16), 4.0e9)
-    ms(C("kcb", 0, 384, 16, part=one), 4.0e9)
-    ms(col("dlt", 0), 0.0)
+    act(C("x192", 0, 256), C("frs", 0, 256), bias=192.0)
+    act(V("sel64"), V("selp"), scale=64.0)
+    act(V("seln"), V("selp"), scale=-1.0)
+
+    select(V("ee"), V("ones"), [[1, 8], [16, 4], [0, 16]], Op.is_equal, 0, -1)
+    iota(V("rst"), [[0, 192]], 0, 0)
+    select(V("rst"), V("rst"), [[0, 4], [1, 48]], Op.not_equal, 0, 0, 4.0e9)
+    for k in range(3):
+        iota(C("na", 8 * k, 8 * k + 8), [[4 >> k, 2 << k], [0, 4 >> k]], 0, 0)
+    iota(V("z8"), [[0, 8]], 0, 0)
+    for t in range(R):
+        iota(V("msg%d" % t, ALL, 4, 3), [[0, 8]], 0, 0)
+    for l in range(3):
+        iota(C("sd", 16 * l, 16 * l + 16), [[0, 8 >> l], [1, 2 << l]], 0, 0)
+    iota(V("win"), [[0, 1024]], 0, 0)
+    iota(V("mz"), [[0, 1920]], 0, 0)
+
+    def late_constants():
+        ms(V("kcb", part=one), 0.0)
+        ts(V("za"), xi(0, 144), zc, Op.is_equal, 262144.0, Op.mult)
+        ms(C("kcb", 0, 384, 48, part=one), 4.0e9)
+        ts(C("pf", 16, 19), C("pf", 1, 4), m3, Op.subtract)
+        ts(C("b1", 0, 8), xi(0, 8), 128.0, Op.mult, q8, Op.add)
+
+    def count_tables():
+        for k in range(3):
+            ts(C("nt", 8 * k, 8 * k + 8), C("na", 8 * k, 8 * k + 8), col("pf", 18 - k), Op.is_equal)
+
+    def owner_constants():
+        ts(col("pp", 0), m2, 39.0, Op.add)
+        ts(col("pp", 1), m1, 21.0, Op.add)
+        cp(col("pp", 2), pq)
+        ts(col("pp", 3), m3, 59.0, Op.add)
+        ts(V("sd"), V("sd"), 1.0, Op.min)
+        ts(V("lfin"), xi(0, 8), q8, Op.add)
 
     def keep_matrices():
         ts(V("acl"), V("asum"), -127.0 / 64, Op.max, 127.0 / 64, Op.min)
-        act(V("am3"), V("acl"), bias=-3.0)
-
-    def candidates_a():
-        cp(V("cand"), IND(C("mixs", 0, 2050), V("lst")))
+        act(C("ps4", 0, 128), V("acl"), bias=-3.0)
 
     def bias(bank):
         mm(V(bank), V("biasl", part=slice(0, 64)), V("ones", part=slice(0, 64)), True, False)
 
-    def candidates_b():
+    def candidates():
+        cp(V("cand"), IND(C("mixs", 0, 2054), V("lst")))
         emit("v", lambda: g.vector.transpose(T.b_tr[:], T.b_cand[:]), [V("cand")], [V("tr")])
+
+    def offsets():
         cp(V("offm"), IND(V("cand"), V("lperm")))
 
-    def key_terms():
+    def moved(name, j, e):
+        a = 160 * (j % 2) + 16 - 16 * (e - j % 2)
+        return C(name, a, a + 128)
+
+    def key_a():
         act(V("candt"), IND(V("tr"), V("lsel")))
         act(V("hi"), V("candt"), bias=192.0 - 0.5 + 1.0 / 128, scale=1.0 / 64)
-        work = C("ps1", 0, 384)
+
+    def key_b(bank):
+        work = C(bank, 0, 384)
         mm(work, V("identf"), V("candt"), True, False)
         mm(work, V("in65"), V("hi"), False, True)
 
-    def key_terms_b():
-        work = C("ps1", 0, 384)
-        act(C("dlt", 1, 385), work, bias=64.0 * 65 * 192, scale=64.0)
-        for ba, a, b in (("ps0", 0, 256), ("ps2", 256, 384)):
-            mm(C(ba, 0, b - a), V("r64", part=one), C("kca", a, b, part=one), True, False)
-            mm(C(ba, 0, b - a), V("i64"), C("hi", a, b), False, False)
-        mm(work, C("ones", 0, 128, part=one), V("kcb", part=one), True, False)
-        mm(work, V("ident"), C("dlt", 0, 384), False, False)
-        mm(work, V("in1"), C("dlt", 1, 385), False, True)
+    def key_start(parts):
+        for j0, nj, bank, x in parts:
+            mm(C(bank, 0, 48 * nj), V("r64", part=one), C("kca", 0, 48 * nj, part=one), True, False)
+            for j in range(j0, j0 + nj):
+                for e in range(2):
+                    b = 192 * e + 48 * (j // 2)
+                    mm(C(bank, 48 * (j - j0), 48 * (j - j0 + 1)), moved("sel64", j, e), C("hi", b, b + 48), False, False)
 
-    def key_steps():
-        act(V("stp"), C("ps1", 0, 384))
+    def key_delta(bank):
+        act(C("dlt", 1, 385), C(bank, 0, 384), bias=64.0 * 65 * 192, scale=64.0)
+
+    def key_c(bank, j0=0, j1=8):
+        if j0 == 0:
+            mm(C(bank, 0, 400), C("ones", 0, 128, part=one), V("kcb", part=one), True, False)
+        for j in range(j0, j1):
+            for e in range(2):
+                b = 192 * e + 48 * (j // 2)
+                mm(C(bank, 48 * j, 48 * j + 48), moved("selp", j, e), C("dlt", b, b + 48), False, False)
+                mm(C(bank, 48 * j, 48 * j + 48), moved("seln", j, e), C("dlt", b + 1, b + 49), False, False)
+        for x in range(2 if j1 == 8 else 0):
+            for e in range(2):
+                mm(C(bank, 384 + x, 392, 2), moved("selp", x, e), C("dlt", 192 * e + 48, 192 * e + 193, 48), False, x + e == 2)
+
+    def key_d(bank):
+        act(V("stp"), C(bank, 0, 400))
 
     bias("ps6")
     bias("ps7")
     bias("ps3")
-    cp(C("mixs", 2048, 2050), C("mixs", 0, 2))
-    candidates_a()
-    candidates_b()
+    bias("ps0")
+    cp(C("mixs", 2048, 2054), C("mixs", 0, 6))
+    candidates()
+    offsets()
+    spread_frames(1, 0, 8)
 
     for t in range(R):
         last = t == R - 1
@@ -311,135 +366,166 @@ def rank_program(g, core, T, topo):
         def by_vector(c, bank):
             ts(cls("mtab", c), V(bank), 184.0, Op.max, 199.0, Op.min)
 
-        def clip(c):
-            ts(cls("mtab", c), cls("mtab", c), 184.0, Op.max, 199.0, Op.min)
+        def clip(c, n=1):
+            m = C("mtab", 512 * c, 512 * (c + n))
+            ts(m, m, 184.0, Op.max, 199.0, Op.min)
 
-        prod(0, "ps4", True); prod(1, "ps6", False); prod(2, "ps5", True); prod(3, "ps7", False)
-        by_scalar(0, "ps4"); by_vector(1, "ps6"); by_scalar(2, "ps5"); clip(0)
-        prod(4, "ps4", True); prod(5, "ps3", False)
         if t == 0:
-            key_terms()
-        by_vector(3, "ps7"); by_scalar(4, "ps4"); clip(2)
-        prod(6, "ps5", True); by_scalar(6, "ps5"); clip(4)
-        prod(7, "ps6", True); by_vector(5, "ps3"); by_scalar(7, "ps6"); clip(6); clip(7)
-        if t > 0:
-            key_steps()
+            prod(0, "ps4", True); prod(1, "ps6", False)
+            by_scalar(0, "ps4"); key_a(); by_vector(1, "ps6")
+            late_constants()
+            prod(2, "ps5", True); prod(3, "ps7", False)
+            clip(0); by_scalar(2, "ps5"); by_vector(3, "ps7")
+            key_b("ps1")
+            prod(4, "ps4", True); prod(5, "ps0", False)
+            key_delta("ps1")
+            clip(2)
+            by_scalar(4, "ps4"); by_vector(5, "ps0")
+            prod(6, "ps5", True); prod(7, "ps3", False)
+            key_c("ps6")
+            clip(4); by_scalar(6, "ps5"); by_vector(7, "ps3"); clip(6)
+            key_start(PARTS)
         else:
-            key_terms_b()
+            prod(0, "ps4", True); prod(5, "ps6", False); prod(1, "ps5", True); prod(6, "ps7", False)
+            by_scalar(0, "ps4"); by_vector(5, "ps6"); by_scalar(1, "ps5"); by_vector(6, "ps7")
+            prod(2, "ps4", True); prod(7, "ps3", False)
+            by_scalar(2, "ps4"); clip(0, 2); by_vector(7, "ps3")
+            prod(3, "ps5", True); by_scalar(3, "ps5")
+            prod(4, "ps4", True); clip(2, 2); by_scalar(4, "ps4"); clip(4)
 
-        def span(h, u0, u1):
-            return 2048 * h + 128 * u0, 2048 * h + 128 * u1
+        def entry(k, h, q):
+            return 192 * k + 64 * h + 4 * q
 
-        def offs(h, u0, u1):
-            return C("offm", 128 * h + 8 * u0, 128 * h + 8 * u1)
+        def span(k, h, q0, q1):
+            return 16 * entry(k, h, q0), 16 * entry(k, h, q1)
 
-        def gather_v(h, u0, u1):
-            a, b = span(h, u0, u1)
-            tt(C("dif", a, b), IND(V("mtab"), offs(h, u0, u1)), C("xrep", 2048 * t + 128 * u0, 2048 * t + 128 * u1), Op.subtract)
+        def offs(k, h, q0, q1):
+            return C("offm", entry(k, h, q0), entry(k, h, q1))
 
-        def sums(h, u0, u1, stop):
-            ba, o = ("ps0", 128 * h) if h < 2 else ("ps2", 0)
-            for u in range(u0, u1):
-                a, b = span(h, u, u + 1)
-                mm(C(ba, o, o + 128), C("za", 15 - u, 143 - u), C("dif", a, b), False, stop and u == u1 - 1)
+        def gather_v(k, h, q0, q1):
+            a, b = span(k, h, q0, q1)
+            j0, nj, bank, x = PARTS[k]
+            x = 2048 * t + 16 * x
+            tt(C("dif", a, b), IND(V("mtab"), offs(k, h, q0, q1)), C("xrep", x + 16 * nj * q0, x + 16 * nj * q1), Op.subtract)
 
-        def square(h, u0, u1, stop=False):
-            a, b = span(h, u0, u1)
+        def sums(k, h, q0, q1, stop):
+            j0, nj, bank, x = PARTS[k]
+            for q in range(q0, q1):
+                a, b = span(k, h, q, q + 1)
+                mm(C(bank, h, 48 * nj, 3), C("za", 15 - q, 143 - q), C("dif", a, b), False, stop and q == q1 - 1)
+
+        def square(k, h, q0, q1, stop=False):
+            a, b = span(k, h, q0, q1)
             act(C("dif", a, b), C("dif", a, b), Fn.Square)
-            sums(h, u0, u1, stop)
+            sums(k, h, q0, q1, stop)
 
-        def gather_a(h):
-            m = C("mg", 512 * h, 512 * (h + 1))
-            act(m, IND(V("mtab"), offs(h, 0, 4)))
-            mm(V("ps%d" % (4 + h)), C("xtn", 128 * t, 128 * (t + 1)), V("ee"), True, False)
-            mm(V("ps%d" % (4 + h)), V("ident"), m, False, True)
+        def gather_a(h, n):
+            m = C("mg", 512 * h, 512 * h + 64 * n)
+            bank = C("ps%d" % (4 + h % 2), 0, 64 * n)
+            act(m, IND(V("mtab"), offs(0, h, 0, n)))
+            mm(bank, C("xtn", 128 * t, 128 * (t + 1)), C("ee", 0, 64 * n), True, False)
+            mm(bank, V("ident"), m, False, True)
 
-        def square_a(h):
-            a, b = span(h, 0, 4)
-            act(C("dif", a, b), V("ps%d" % (4 + h)), Fn.Square, bias=-192.0)
-            sums(h, 0, 4, False)
+        def square_a(h, n, stop=False):
+            a, b = span(0, h, 0, n)
+            act(C("dif", a, b), C("ps%d" % (4 + h % 2), 0, 64 * n), Fn.Square, bias=-192.0)
+            sums(0, h, 0, n, stop)
 
-        chunks = [(0, 4, 8), (0, 8, 12), (0, 12, 16), (1, 4, 8), (1, 8, 12), (1, 12, 16),
-                  (2, 0, 4), (2, 4, 8), (2, 8, 12), (2, 12, 14), (2, 14, 15), (2, 15, 16)]
-        for ch in chunks:
+        def scans(k):
+            j0, nj, bank, x = PARTS[k]
+            a, n = 48 * j0, 48 * nj
+            scan(C("sc", a, a + n), C("stp", a, a + n), C(bank, 0, n), 0.0, Op.add, Op.min)
+            scan(C("sc", 384 + a, 384 + a + n), C("rst", 0, n), C(bank, 0, n), 0.0, Op.add, Op.min)
+
+        for ch in CHUNKS:
             gather_v(*ch)
-        gather_a(0)
+        gather_a(0, 8)
         if t == 0:
-            key_steps()
-        square(*chunks[0]); gather_a(1); square_a(0); square(*chunks[1]); square(*chunks[2]); square_a(1)
-        for k in range(3, len(chunks)):
-            square(*chunks[k], stop=k in (5, len(chunks) - 1))
+            key_d("ps6")
+        square(*CHUNKS[0]); gather_a(1, 8); square_a(0, 8)
+        square(*CHUNKS[1]); square_a(1, 8); square(*CHUNKS[2], stop=True)
+        if t == 0:
+            count_tables()
+        scans(0)
+        for ch in CHUNKS[3:]:
+            square(*ch, stop=ch == CHUNKS[-1])
+        scans(1)
 
-        def scan(key, a, b):
-            src = C("ps0", a, b) if a < 256 else C("ps2", a - 256, b - 256)
-            out = C("sc", 384 * key + a, 384 * key + b)
-            d0 = C("stp", a, b) if key else C("rst", 0, b - a)
-            emit("v", lambda: g.vector.tensor_tensor_scan(out[0], d0[0], src[0], 0.0, Op.add, Op.min), [d0, src], [out])
-
-        def ends(key, a, b):
-            return C("sc", 384 * key + a + 15, 384 * key + b, 16)
-
-        ka, kb = C("mk", 0, 8), C("mk", 8, 16)
-        scan(1, 0, 256); scan(0, 0, 256)
-        tt(C("eb", 0, 16), ends(1, 0, 256), C("dlt", 16, 257, 16), Op.add)
-        tt(C("m01", 0, 8), ends(0, 0, 128), ends(0, 128, 256), Op.min)
-        tt(C("m01", 8, 16), C("eb", 0, 8), C("eb", 8, 16), Op.min)
-        scan(1, 256, 384); scan(0, 256, 384)
-        tt(C("eb", 16, 24), ends(1, 256, 384), C("dlt", 272, 385, 16), Op.add)
-        tt(ka, C("m01", 0, 8), ends(0, 256, 384), Op.min)
-        tt(kb, C("m01", 8, 16), C("eb", 16, 24), Op.min)
-        ts(C("b0", 0, 8), ka, 0xFC0, Op.bitwise_and)
-        ts(C("b0", 8, 16), ka, 0xE00, Op.bitwise_and, 2, Op.logical_shift_right)
+        kb, ka = C("mk", 0, 8), C("mk", 8, 16)
+        tt(V("mk"), C("sc", 47, 768, 48), C("stp", 384, 400), Op.add)
+        ts(C("b2", 24, 32), ka, 0xFC0, Op.bitwise_and)
+        ts(C("b1", 8, 16), kb, 6, Op.logical_shift_right, 63, Op.bitwise_and)
         ts(C("b2", 16, 24), ka, 9, Op.logical_shift_right, 7, Op.bitwise_and)
-        ts(C("b1", 0, 8), kb, 6, Op.logical_shift_right, 63, Op.bitwise_and)
-        tt(C("b2", 0, 16), V("b0"), V("b1"), Op.add)
-        cp(V("off"), V("b2"))
+        tt(C("b2", 8, 16), C("b2", 24, 32), C("b1", 8, 16), Op.add)
+        tt(C("b2", 0, 8), C("b2", 16, 24), C("b1", 0, 8), Op.add)
+        cp(C("off", 8, 24), C("b2", 8, 24))
+        cp(C("off", 0, 8), C("b2", 0, 8))
 
-        ow, osc, ocl = C("off", 0, 8), C("off", 8, 16), C("off", 16, 24)
-        act(V("muw"), IND(V("mus"), ow))
-        tt(V("en"), IND(V("mtab"), ow), C("x192", 128 * t, 128 * (t + 1)), Op.subtract)
-        rows, cols = ("en", "muw") if last else ("muw", "en")
-        cp(IND(V("win"), osc), V(cols))
-        mm(C("ps6", 0, 128), V(rows), V("ident"), True, True)
+        osc, ow, ocl = C("off", 0, 8), C("off", 8, 16), C("off", 16, 24)
+        if last:
+            act(V("muw"), IND(V("mtab"), ow), bias=-192.0)
+            cp(V("en"), IND(V("mus"), ow))
+            mm(C("ps6", 0, 128), V("ident"), C("xtn", 128 * t, 128 * (t + 1)), True, False)
+        else:
+            act(V("muw"), IND(V("mus"), ow))
+            tt(V("en"), IND(V("mtab"), ow), C("x192", 128 * t, 128 * (t + 1)), Op.subtract)
+        cp(IND(V("win"), osc), V("en"))
+        mm(C("ps6", 0, 128), V("muw"), V("ident"), not last, True)
         msg, land, dl = "msg%d" % t, "land%d" % t, "dl%d" % t
 
         def count(l):
-            act(V("junk"), IND(C("nt", 8 * l, 8 * l + 8), ocl), accum=col("ncol", l))
+            act(C("junk", 128 * l, 128 * (l + 1)), IND(C("nt", 8 * l, 8 * l + 8), ocl), bias=37.5, scale=-128.0, accum=col("ncol", l))
 
-        count(0); count(1)
+        count(0)
         act(V("mz", slice(0, 8), slice(112, 128)), C("ps6", 0, 128))
+        count(1)
         count(2)
+        for c in range(4):
+            turn(V("ps2", slice(0, 64), c, ALL), C("win", c, 1024, 8), V("ident"))
         for half in range(2):
-            for c in range(8):
-                mm(C("ps%d" % (4 + half), c, 512, 8), C("win", 128 * c, 128 * (c + 1)), C("ident", 64 * half, 64 * (half + 1)), True, True)
-        act(C("em", 0, 512), V("ps4"))
-        cp(C("em", 512, 1024), V("ps5"))
+            for c in range(4):
+                mm(C("ps%d" % (4 + half), c, 256, 4), C("win", 4 + c, 1024, 8), C("ident", 64 * half, 64 * (half + 1)), True, True)
+        ts(V("hw"), ka, 16, Op.logical_shift_right, 3, Op.bitwise_and)
+        cp(C("w32", 8 * t, 8 * t + 8), C("b2", 8, 16))
+        cp(C("em", 0, 512), V("ps2", slice(0, 64)))
+        act(C("em", 512, 768), C("ps4", 0, 256))
+        cp(C("em", 768, 1024), C("ps5", 0, 256))
+        tt(V("st"), V("st"), V("hw"), Op.add)
         for l in range(3):
-            act(V(msg, ALL, 16 + l), V("z8"), bias=col("ncol", l))
-        for k in range(8):
-            mm(C("ps7", 0, 128), V("mz", k, slice(112 - 16 * k, 240 - 16 * k)), C("em", 128 * k, 128 * (k + 1)), k == 0, k == 7)
+            act(V(msg, ALL, 4, l), V("z8"), bias=col("ncol", l))
         unit = 1.0 if last else 1.0 / 64
-        ts(V(msg, ALL, slice(0, 16)), C("ps7", 0, 128), -unit / 256, Op.mult)
+        for half, bank in enumerate(("ps7", "ps3")):
+            for k in range(8):
+                a = 512 * half + 64 * k
+                mm(C(bank, 0, 64), V("mz", k, slice(112 - 16 * k, 240 - 16 * k)), C("em", a, a + 64), k == 0, k == 7)
+            if half == 0:
+                for x in range(2):
+                    ts(V(msg, ALL, 2 * x, ALL), C(bank, x, 64, 2), -unit / 256, Op.mult)
+            else:
+                ts(V(msg, ALL, slice(1, 4, 2), ALL), C(bank, 0, 64), -unit / 256, Op.mult)
+        if not last:
+            state_list()
 
         def send_sums(msg=msg, land=land, t=t):
             trs = [RemoteDMATransfer(dst_ids=[dst(r)], dma_engine_mask=1 << engines[j], remote_sem=T.sem["ar%d" % t],
-                                     src=T["b_" + msg][:, r, :], dst=T["b_" + land][:, rank, :]) for j, r in enumerate(peers)]
+                                     src=T["b_" + msg][:, r], dst=T["b_" + land][:, rank]) for j, r in enumerate(peers)]
             g.remote_dma_fused(trs, local_sem=T.sem.sent)
         emit("g", send_sums, [V(msg)], [], "remote")
         sent[0] += len(peers)
 
-        cp(V(land, rank, ALL), V(msg, rank, ALL))
-        ts(V("hw"), ka, 16, Op.logical_shift_right, 3, Op.bitwise_and)
-        cp(C("w32", 8 * t, 8 * t + 8), C("b2", 0, 8))
-        tt(V("s1"), V("st"), V("hw"), Op.add)
-        ts(V("st"), V("s1"), 2047, Op.bitwise_and)
+        cp(V(land, rank), V(msg, rank))
+        if t == 0:
+            spread_frames(1, 8, 16)
+            owner_constants()
+            act(V("i16x"), V("i16"), scale=64.0)
+            act(V("m16"), V("i16"))
         if not last:
-            state_list()
-            spread_frames(t + 1)
+            candidates()
             bias("ps6"); bias("ps7"); bias("ps3")
-            candidates_a()
+            key_a(); key_b("ps5"); key_delta("ps5"); key_start(PARTS); key_c("ps4"); key_d("ps4")
         else:
-            cp(C("w32", 24, 32), V("st"))
+            ts(V("s1"), V("st"), 2047, Op.bitwise_and)
+            cp(C("w32", 24, 32), V("s1"))
             for c in range(8):
                 mm(C("ps5", 16 * c, 16 * (c + 1)), C("bd", c, 1024, 8), V("i16x"), True, True)
             for u in range(16):
@@ -450,19 +536,16 @@ def rank_program(g, core, T, topo):
             store("s", "d_yw", T.yw[:], C("outs", 0, 384, part=slice(0, 8)))
             store("s", "d_ys", T.ys[:], C("outs", 384, 512, part=slice(0, 8)))
 
-        emit("x", None, [], [V(land, r, ALL) for r in peers], "ar%d" % t, len(peers))
-        tt(V("s4"), V(land, slice(0, 4), ALL), V(land, slice(4, 8), ALL), Op.add)
+        emit("x", None, [], [V(land, r) for r in peers], "ar%d" % t, len(peers))
+        tt(V("s4"), V(land, slice(0, 4)), V(land, slice(4, 8)), Op.add)
         tt(V("s2"), C("s4", 0, 40), C("s4", 40, 80), Op.add)
         tt(C("yy", 0, 20), C("s2", 0, 20), C("s2", 20, 40), Op.add)
-        tt(C("yy", 20, 28), C("yy", 0, 16, 2), C("yy", 1, 16, 2), Op.add)
-        ts(col("tt", 0), col("yy", 16), pq, Op.max, col("pf", 12), Op.min)
-        tt(C("tt", 1, 3), C("yy", 17, 19), C("pf", 13, 15), Op.min)
-        for k in range(2):
-            o, s = col("yy", 32 + k), C("yy", 8 * k, 8 * k + 8)
-            emit("v", lambda o=o, s=s: g.vector.tensor_reduce(o[0], s[0], AxisListType.X, Op.add), [s], [o])
-        tt(C("yy", 28, 32), C("yy", 20, 28, 2), C("yy", 21, 28, 2), Op.add)
-        ts(col("osel", 0), col("tt", 0), col("tt", 1), Op.max, col("tt", 2), Op.max)
-        ts(V("dcl"), IND(C("yy", 0, 34), col("osel", 0)), -2.0 * unit, Op.max, 2.0 * unit, Op.min)
+        scan(C("tt", 0, 3), C("yy", 16, 19), C("pp", 0, 3), col("pp", 3), Op.min, Op.max)
+        scan(C("yy", 20, 36), C("sd", 0, 16), C("yy", 0, 16), 0.0, Op.mult, Op.add)
+        cp(col("osel", 0), col("tt", 2))
+        for l in (1, 2):
+            scan(C("yy", 20 + 16 * l, 36 + 16 * l), C("sd", 16 * l, 16 * l + 16), C("yy", 0, 16), 0.0, Op.mult, Op.add)
+        ts(V("dcl"), IND(C("yy", 0, 68), col("osel", 0)), -2.0 * unit, Op.max, 2.0 * unit, Op.min)
         mine = C(dl, 16 * rank, 16 * rank + 16)
         ts(mine, V("dcl"), (192.0 - 0.5 + 1.0 / 512) * unit, Op.add)
 
@@ -474,14 +557,14 @@ def rank_program(g, core, T, topo):
         sent[0] += wide
 
         if not last:
+            offsets()
             keep_matrices()
-            candidates_b()
-            key_terms()
-            key_terms_b()
             iota(V("win"), [[0, 1024]], 0, 0)
+            if t + 2 < R:
+                spread_frames(t + 2)
         emit("x", None, [], [C(dl, 16 * r, 16 * r + 16) for r in peers], "dr%d" % t, wide * len(peers))
         if not last:
-            tt(V("asum"), V("am3"), V(dl), Op.add)
+            tt(V("asum"), C("ps4", 0, 128), V(dl), Op.add)
             block_diagonal(V("asum"))
         else:
             tt(V("afin"), IND(V(dl), V("lfin")), V("anat"), Op.add)

@@ -7,24 +7,25 @@ R = 3
 SB = {
     "mus": (4096, BF), "mixs": (2056, I), "frs": (384, BF), "a0s": (128, BF), "st": (8, I),
     "mtab": (4096, BF), "dif": (6144, BF), "mg": (1536, BF), "xp": (384, BF), "x192": (384, BF), "xrep": (6144, BF),
-    "xtn": (384, BF), "bd": (1024, BF), "asum": (128, BF), "acl": (128, F), "anat": (128, F),
+    "xtn": (384, BF), "bd": (1024, BF), "asum": (128, BF), "acl": (128, BF), "anat": (128, F),
     "afin": (128, F), "yas": (128, F),
-    "lst": (24, U), "cand": (384, F), "tr": (384, F), "candt": (384, F), "hi": (384, BF), "offm": (384, U),
+    "lst": (24, U), "cand": (384, F), "tr": (384, F), "hi": (384, BF), "offm": (384, U),
     "sc": (768, F), "mk": (16, I), "b1": (16, I), "b2": (32, I), "off": (24, U), "hw": (8, I),
     "s1": (8, I), "en": (128, BF), "muw": (128, BF), "win": (1024, BF), "em": (1024, BF), "junk": (384, F), "ncol": (4, F),
     "s4": (80, F), "s2": (40, F), "yy": (72, F), "tt": (4, F), "osel": (2, U), "dcl": (16, F),
     "w32": (32, F), "wexp": (512, F), "outs": (512, F),
     "pi": (8, I), "pf": (24, F), "xi": (176, F), "ones": (512, BF), "ident": (128, BF), "in65": (128, BF),
-    "identf": (128, F), "za": (144, BF), "dlt": (392, BF), "stp": (400, F), "i16": (16, BF), "i16x": (16, BF), "m16": (16, F), "bg": (8, F),
-    "lo": (8, F), "up": (8, F), "r64": (128, BF), "kca": (192, BF), "kcb": (400, BF), "nt": (24, F), "na": (24, F),
-    "biasl": (128, BF), "rst": (192, F), "ee": (512, BF), "io": (80, F), "i3": (24, I), "lf": (24, F), "lsel": (24, U), "lperm": (24, U),
-    "l0": (8, U), "la": (8, U), "lfin": (8, U), "z8": (8, F), "selp": (320, BF), "seln": (320, BF), "sel64": (320, BF),
+    "identf": (128, F), "za": (144, BF), "stp": (400, F), "i16": (16, BF), "i16x": (16, BF), "m16": (16, F), "bg": (8, F),
+    "lo": (8, F), "up": (8, F), "m64": (8, F), "r64": (128, BF), "kca": (192, BF), "nt": (24, F), "na": (24, F),
+    "biasl": (128, BF), "rst": (192, F), "ee": (512, BF), "io": (24, F), "lperm": (24, U),
+    "l0": (8, U), "lfin": (8, U), "z8": (8, F), "selp": (320, BF), "seln": (320, BF), "sel64": (320, BF),
     "sd": (48, F), "pp": (4, F),
 }
 SCRATCH = {"b_" + k: ("sbuf", [128, n], d) for k, (n, d) in SB.items()}
-SCRATCH["b_mz"] = ("sbuf", [128, 8, 240], BF)
 SHAPE = {k: (n,) for k, (n, d) in SB.items()}
-SHAPE["mz"] = (8, 240)
+for _k, _s in (("mz", (8, 240)), ("dlt", (8, 49)), ("bd0", (8, 8, 16))):
+    SCRATCH["b_" + _k] = ("sbuf", [128] + list(_s), BF)
+    SHAPE[_k] = _s
 for _t in range(R):
     SCRATCH["b_msg%d" % _t] = ("sbuf", [128, 8, 5, 4], F)
     SCRATCH["b_land%d" % _t] = ("sbuf", [128, 8, 5, 4], F)
@@ -35,14 +36,16 @@ for _t in range(R):
 for _b in range(8):
     SCRATCH["b_ps%d" % _b] = ("psum", [128, 128, 4, 2], BF) if _b == 2 else ("psum", [128, 512], F)
     SHAPE["ps%d" % _b] = (128, 4, 2) if _b == 2 else (512,)
-DMAS = ["d_s0", "d_a0", "d_fr", "d_mix", "d_mu0", "d_mu1", "d_mu2", "d_mu3", "d_mu4", "d_yw", "d_ys", "d_ya"]
+DMAS = ["d_s0", "d_a0", "d_fr", "d_mix", "d_mx", "d_mu0", "d_mu1", "d_mu2", "d_mu3", "d_mu4", "d_yw", "d_ys", "d_ya", "d_yb"]
 SEMAPHORES = ["qv", "qa", "qp", "qg", "sent"] + DMAS + ["ar%d" % t for t in range(R)] + ["dr%d" % t for t in range(R)]
 
 ALL = slice(None)
 PARTS = [(0, 4, "ps0", 0), (4, 4, "ps1", 64)]
-CHUNKS = [(0, 0, 8, 16), (0, 1, 8, 16), (0, 2, 0, 16), (1, 0, 0, 16), (1, 1, 0, 8), (1, 1, 8, 16), (1, 2, 0, 7), (1, 2, 7, 12), (1, 2, 12, 15),
+NA = 0
+CHUNKS = [(0, 0, 8, 16), (0, 1, 8, 16), (0, 2, NA, 16), (1, 0, 0, 16), (1, 1, 0, 8), (1, 1, 8, 16), (1, 2, 0, 7), (1, 2, 7, 12), (1, 2, 12, 15),
           (1, 2, 15, 16)]
 LOADS = [0, 1024, 2048, 3072, 3584, 4096]
+XS = 3
 
 
 def rank_program(g, core, T, topo):
@@ -175,6 +178,7 @@ def rank_program(g, core, T, topo):
     load("s", "d_a0", V("a0s"), T.a0[:])
     load("a", "d_fr", V("frs"), T.fr[:])
     load("s", "d_s0", V("st"), T.s0[:])
+    load("a", "d_mx", C("mixs", 2048, 2056), T.mix[:, 0:8])
     load("s", "d_mix", C("mixs", 0, 2048), T.mix[:])
     for k in range(5):
         load("s", "d_mu%d" % k, C("mus", LOADS[k], LOADS[k + 1]), T.mu[:, LOADS[k]:LOADS[k + 1]])
@@ -185,78 +189,82 @@ def rank_program(g, core, T, topo):
         return C("xi", 16 + a, 16 + b)
 
     iota(col("pi", 0), [[1, 1]], 0, 1, False)
-    iota(C("io", 0, 8), [[2, 8]], 0, 0)
-    iota(C("io", 8, 32), [[64, 2], [128, 3], [4, 4]], 0, 0)
+    iota(V("io"), [[64, 2], [128, 3], [4, 4]], 0, 0)
     iota(V("xi"), [[1, 176]], -16, 0)
     ms(V("ones"), 1.0)
-    iota(C("io", 32, 56), [[0, 8], [16, 3]], -1, 0)
-    iota(C("io", 56, 80), [[16, 2], [32, 4], [2048, 3]], 0, 0)
     select(V("ident"), C("ones", 0, 128), [[-1, 128]], Op.is_equal, 0, 1)
     iota(V("r64", part=one), [[0, 128]], 64, 0)
     iota(V("kca", part=one), [[0, 4], [64, 16], [1024, 3]], -192, 0)
-    iota(col("dlt", 0), [[0, 1]], 0, 0)
 
     for j, m in enumerate((15, 14, 12, 8, 16)):
         ts(col("pi", 1 + j), col("pi", 0), m, Op.bitwise_and)
     cp(C("pf", 0, 6), C("pi", 0, 6))
     pp_, pq, m1, m2, m3, m4 = [col("pf", j) for j in range(6)]
-    q16, ca, cb, cla, pg16, x1, x0, q128, zc, q8 = [col("pf", j) for j in range(6, 16)]
+    q16, ca, pg16, x1, x0, zc, q8 = [col("pf", j) for j in range(6, 13)]
     ts(q16, pq, 16.0, Op.mult)
     ts(pg16, pp_, pq, Op.subtract)
     ts(ca, m2, -15.75, Op.mult, q16, Op.add)
-    ts(cla, m3, -15.875, Op.mult, q16, Op.add)
-    ts(C("l0", 0, 4), C("io", 8, 12), ca, Op.add)
-    ts(C("l0", 4, 8), C("io", 20, 24), ca, Op.add)
     ts(V("bg"), xi(0, 8), 16.0, Op.mult, pg16, Op.is_equal)
-    ts(V("la"), C("io", 0, 8), cla, Op.add)
-    act(q128, pq, scale=128.0)
+    ts(C("l0", 0, 4), C("io", 0, 4), ca, Op.add)
+    ts(C("l0", 4, 8), C("io", 12, 16), ca, Op.add)
+    act(V("biasl", part=slice(0, 32)), C("ones", 0, 128, part=slice(0, 32)), scale=6.0)
+    act(V("biasl", part=slice(32, 64)), C("ones", 0, 128, part=slice(32, 64)), scale=1.0 / 4096)
+    act(V("za"), C("ones", 0, 144), scale=0.0)
     act(x1, m4, scale=1.0 / 16)
     act(x0, m4, scale=-1.0 / 16, bias=1.0)
-    act(zc, pg16, bias=15.0)
     act(q8, pq, scale=8.0)
-    act(V("lo"), V("bg"), scale=-127.0 / 64)
-    act(V("up"), V("bg"), scale=127.0 / 64)
-    ts(V("i16"), xi(0, 16), pq, Op.is_equal)
-    ts(V("lperm"), C("io", 8, 32), ca, Op.add)
-    ts(V("i3"), C("io", 32, 56), pq, Op.add, 1.0 / 3, Op.mult)
-    ms(V("biasl", part=slice(0, 32)), 6.0)
-    ts(V("lf"), V("i3"), -383.0, Op.mult, q128, Op.add)
-    ms(V("biasl", part=slice(32, 64)), 1.0 / 4096)
-    tt(V("lf"), V("lf"), C("io", 56, 80), Op.add)
+    act(V("m64"), V("bg"), scale=1.0 / 64)
+    act(C("za", 15, 143, 16), V("bg"), scale=262144.0)
+    ts(V("lperm"), V("io"), ca, Op.add)
+    ts(C("selp", 0, 160), C("xi", 0, 160), pp_, Op.is_equal, x0, Op.mult)
+    ts(C("selp", 160, 320), C("xi", 0, 160), pp_, Op.is_equal, x1, Op.mult)
 
     def block_diagonal(src):
         for k in range(8):
-            ts(C("bd", 128 * k, 128 * (k + 1)), src, col("lo", k), Op.max, col("up", k), Op.min)
+            if k < 5:
+                ts(C("bd", 128 * k, 128 * (k + 1)), src, col("bg", k), Op.mult)
+            else:
+                act(C("bd", 128 * k, 128 * (k + 1)), src, scale=col("bg", k))
 
     def state_list():
         for h in range(3):
             ts(C("lst", 8 * h, 8 * h + 8), V("st"), float(h), Op.add)
 
-    def spread_frames(t, i0=0, i1=16):
-        for i in range(i0, i1):
-            select(C("xrep", 2048 * t + i, 2048 * (t + 1), 16), C("xp", 128 * t, 128 * (t + 1)), [[0, 128]], Op.is_ge, 0, 0)
-
-    for t in range(R):
+    def frames(t):
         act(C("xp", 128 * t, 128 * (t + 1)), IND(C("frs", 128 * t, 128 * (t + 1)), V("l0")), bias=192.0)
-    spread_frames(0)
-    ts(V("asum"), IND(V("a0s"), V("la")), 1.0 / 64, Op.mult)
-    cp(V("lsel"), V("lf"))
-    block_diagonal(V("asum"))
+
+    def spread_frames(t, i0, i1, queue="g"):
+        for i in range(i0, i1):
+            out, src = C("xrep", 2048 * t + i, 2048 * (t + 1), 16), C("xp", 128 * t, 128 * (t + 1))
+            if queue == "g":
+                select(out, src, [[0, 128]], Op.is_ge, 0, 0)
+            else:
+                act(out, src)
+
+    def turned_frames(t, bank):
+        mm(C(bank, 0, 128), C("frs", 128 * t, 128 * (t + 1)), V("ident"), True, True)
+        act(C("xtn", 128 * t, 128 * (t + 1)), C(bank, 0, 128), scale=-1.0)
+
+    frames(0)
+    spread_frames(0, XS, 16)
+    for k in range(8):
+        if k < 5:
+            ts(V("bd0", ALL, k), V("a0s"), col("m64", k), Op.mult)
+        else:
+            act(V("bd0", ALL, k), V("a0s"), scale=col("m64", k))
     for c in range(8):
-        mm(C("ps4", c, 128, 8), C("bd", c, 1024, 8), V("i16"), True, True)
-    for t in range(R):
-        mm(C("ps5", 128 * t, 128 * (t + 1)), C("frs", 128 * t, 128 * (t + 1)), V("ident"), True, True)
+        turn(V("ps2", slice(16 * c, 16 * c + 16)), V("bd0", c), V("ident"))
+    state_list()
+    ms(V("dlt", ALL, 0), 4.0e9)
+    ts(C("pf", 16, 19), C("pf", 1, 4), m3, Op.subtract)
+    ts(C("b1", 0, 8), xi(0, 8), 128.0, Op.mult, q8, Op.add)
+    cp(V("bd"), V("ps2"))
     act(V("identf"), V("ident"))
     act(V("in65"), V("ident"), scale=-65.0)
-    state_list()
-    ts(C("selp", 0, 160), C("xi", 0, 160), pp_, Op.is_equal, x0, Op.mult)
-    act(V("asum"), C("ps4", 0, 128))
-    ts(C("selp", 160, 320), C("xi", 0, 160), pp_, Op.is_equal, x1, Op.mult)
-    block_diagonal(V("asum"))
-    act(V("xtn"), C("ps5", 0, 384), scale=-1.0)
-    act(C("x192", 0, 256), C("frs", 0, 256), bias=192.0)
     act(V("sel64"), V("selp"), scale=64.0)
+    turned_frames(0, "ps5")
     act(V("seln"), V("selp"), scale=-1.0)
+    spread_frames(0, 0, XS, "a")
 
     select(V("ee"), V("ones"), [[1, 8], [16, 4], [0, 16]], Op.is_equal, 0, -1)
     iota(V("rst"), [[0, 192]], 0, 0)
@@ -271,13 +279,6 @@ def rank_program(g, core, T, topo):
     iota(V("win"), [[0, 1024]], 0, 0)
     iota(V("mz"), [[0, 1920]], 0, 0)
 
-    def late_constants():
-        ms(V("kcb", part=one), 0.0)
-        ts(V("za"), xi(0, 144), zc, Op.is_equal, 262144.0, Op.mult)
-        ms(C("kcb", 0, 384, 48, part=one), 4.0e9)
-        ts(C("pf", 16, 19), C("pf", 1, 4), m3, Op.subtract)
-        ts(C("b1", 0, 8), xi(0, 8), 128.0, Op.mult, q8, Op.add)
-
     def count_tables():
         for k in range(3):
             ts(C("nt", 8 * k, 8 * k + 8), C("na", 8 * k, 8 * k + 8), col("pf", 18 - k), Op.is_equal)
@@ -291,7 +292,6 @@ def rank_program(g, core, T, topo):
         ts(V("lfin"), xi(0, 8), q8, Op.add)
 
     def keep_matrices():
-        ts(V("acl"), V("asum"), -127.0 / 64, Op.max, 127.0 / 64, Op.min)
         act(C("ps4", 0, 128), V("acl"), bias=-3.0)
 
     def bias(bank):
@@ -309,48 +309,44 @@ def rank_program(g, core, T, topo):
         return C(name, a, a + 128)
 
     def key_a():
-        act(V("candt"), IND(V("tr"), V("lsel")))
-        act(V("hi"), V("candt"), bias=192.0 - 0.5 + 1.0 / 128, scale=1.0 / 64)
+        for h in range(3):
+            act(C("hi", h, 384, 3), C("tr", 128 * h, 128 * (h + 1)), bias=192.0 - 0.5 + 1.0 / 128, scale=1.0 / 64)
 
     def key_b(bank):
-        work = C(bank, 0, 384)
-        mm(work, V("identf"), V("candt"), True, False)
-        mm(work, V("in65"), V("hi"), False, True)
+        mm(C(bank, 0, 384), V("in65"), V("hi"), True, False)
+        for h in range(3):
+            mm(C(bank, h, 384, 3), V("identf"), C("tr", 128 * h, 128 * (h + 1)), False, h == 2)
 
     def key_start(parts):
         for j0, nj, bank, x in parts:
             mm(C(bank, 0, 48 * nj), V("r64", part=one), C("kca", 0, 48 * nj, part=one), True, False)
             for j in range(j0, j0 + nj):
                 for e in range(2):
-                    b = 192 * e + 48 * (j // 2)
+                    b = 48 * (2 * (j // 2) + e)
                     mm(C(bank, 48 * (j - j0), 48 * (j - j0 + 1)), moved("sel64", j, e), C("hi", b, b + 48), False, False)
 
     def key_delta(bank):
-        act(C("dlt", 1, 385), C(bank, 0, 384), bias=64.0 * 65 * 192, scale=64.0)
+        act(V("dlt", ALL, slice(1, 49)), C(bank, 0, 384), bias=64.0 * 65 * 192, scale=64.0)
 
-    def key_c(bank, j0=0, j1=8):
-        if j0 == 0:
-            mm(C(bank, 0, 400), C("ones", 0, 128, part=one), V("kcb", part=one), True, False)
-        for j in range(j0, j1):
+    def key_c(bank):
+        for j in range(8):
             for e in range(2):
-                b = 192 * e + 48 * (j // 2)
-                mm(C(bank, 48 * j, 48 * j + 48), moved("selp", j, e), C("dlt", b, b + 48), False, False)
-                mm(C(bank, 48 * j, 48 * j + 48), moved("seln", j, e), C("dlt", b + 1, b + 49), False, False)
-        for x in range(2 if j1 == 8 else 0):
+                b = 2 * (j // 2) + e
+                mm(C(bank, 48 * j, 48 * j + 48), moved("selp", j, e), V("dlt", b, slice(0, 48)), e == 0, False)
+                mm(C(bank, 48 * j, 48 * j + 48), moved("seln", j, e), V("dlt", b, slice(1, 49)), False, e == 1)
+        for x in range(2):
             for e in range(2):
-                mm(C(bank, 384 + x, 392, 2), moved("selp", x, e), C("dlt", 192 * e + 48, 192 * e + 193, 48), False, x + e == 2)
+                mm(C(bank, 384 + x, 392, 2), moved("selp", x, e), V("dlt", slice(e, 8, 2), 48), e == 0, e == 1)
 
     def key_d(bank):
-        act(V("stp"), C(bank, 0, 400))
+        act(C("stp", 0, 392), C(bank, 0, 392))
 
     bias("ps6")
     bias("ps7")
     bias("ps3")
     bias("ps0")
-    cp(C("mixs", 2048, 2054), C("mixs", 0, 6))
     candidates()
     offsets()
-    spread_frames(1, 0, 8)
 
     for t in range(R):
         last = t == R - 1
@@ -358,7 +354,8 @@ def rank_program(g, core, T, topo):
             return C(name, 512 * c, 512 * (c + 1))
 
         def prod(c, bank, start):
-            mm(V(bank), C("bd", c, 1024, 8), cls("mus", c), start, True)
+            left = C("bd", c, 1024, 8) if t else C("bd", 128 * c, 128 * (c + 1))
+            mm(V(bank), left, cls("mus", c), start, True)
 
         def by_scalar(c, bank):
             act(cls("mtab", c), V(bank), bias=192.0 + 1.0 / 128)
@@ -373,18 +370,18 @@ def rank_program(g, core, T, topo):
         if t == 0:
             prod(0, "ps4", True); prod(1, "ps6", False)
             by_scalar(0, "ps4"); key_a(); by_vector(1, "ps6")
-            late_constants()
             prod(2, "ps5", True); prod(3, "ps7", False)
             clip(0); by_scalar(2, "ps5"); by_vector(3, "ps7")
-            key_b("ps1")
             prod(4, "ps4", True); prod(5, "ps0", False)
-            key_delta("ps1")
             clip(2)
             by_scalar(4, "ps4"); by_vector(5, "ps0")
             prod(6, "ps5", True); prod(7, "ps3", False)
-            key_c("ps6")
+            key_b("ps1")
             clip(4); by_scalar(6, "ps5"); by_vector(7, "ps3"); clip(6)
-            key_start(PARTS)
+            key_delta("ps1")
+            key_start(PARTS[:1])
+            key_c("ps6")
+            key_start(PARTS[1:])
         else:
             prod(0, "ps4", True); prod(5, "ps6", False); prod(1, "ps5", True); prod(6, "ps7", False)
             by_scalar(0, "ps4"); by_vector(5, "ps6"); by_scalar(1, "ps5"); by_vector(6, "ps7")
@@ -434,32 +431,41 @@ def rank_program(g, core, T, topo):
         def scans(k):
             j0, nj, bank, x = PARTS[k]
             a, n = 48 * j0, 48 * nj
-            scan(C("sc", a, a + n), C("stp", a, a + n), C(bank, 0, n), 0.0, Op.add, Op.min)
             scan(C("sc", 384 + a, 384 + a + n), C("rst", 0, n), C(bank, 0, n), 0.0, Op.add, Op.min)
+            scan(C("sc", a, a + n), C("stp", a, a + n), C(bank, 0, n), 0.0, Op.add, Op.min)
 
         for ch in CHUNKS:
             gather_v(*ch)
         gather_a(0, 8)
+        square(*CHUNKS[0]); gather_a(1, 8); square_a(0, 8)
         if t == 0:
             key_d("ps6")
-        square(*CHUNKS[0]); gather_a(1, 8); square_a(0, 8)
-        square(*CHUNKS[1]); square_a(1, 8); square(*CHUNKS[2], stop=True)
+        square(*CHUNKS[1])
+        if NA:
+            gather_a(2, NA)
+        square_a(1, 8); square(*CHUNKS[2], stop=NA == 0)
+        if NA:
+            square_a(2, NA, True)
         if t == 0:
             count_tables()
         scans(0)
         for ch in CHUNKS[3:]:
             square(*ch, stop=ch == CHUNKS[-1])
+        if t == 0:
+            act(C("x192", 0, 128), C("frs", 0, 128), bias=192.0)
+        if not last:
+            frames(t + 1)
         scans(1)
 
         kb, ka = C("mk", 0, 8), C("mk", 8, 16)
-        tt(V("mk"), C("sc", 47, 768, 48), C("stp", 384, 400), Op.add)
+        cp(ka, C("sc", 384 + 47, 768, 48))
+        tt(kb, C("sc", 47, 384, 48), C("stp", 384, 392), Op.add)
         ts(C("b2", 24, 32), ka, 0xFC0, Op.bitwise_and)
         ts(C("b1", 8, 16), kb, 6, Op.logical_shift_right, 63, Op.bitwise_and)
         ts(C("b2", 16, 24), ka, 9, Op.logical_shift_right, 7, Op.bitwise_and)
-        tt(C("b2", 8, 16), C("b2", 24, 32), C("b1", 8, 16), Op.add)
-        tt(C("b2", 0, 8), C("b2", 16, 24), C("b1", 0, 8), Op.add)
-        cp(C("off", 8, 24), C("b2", 8, 24))
-        cp(C("off", 0, 8), C("b2", 0, 8))
+        tt(C("off", 8, 16), C("b2", 24, 32), C("b1", 8, 16), Op.add)
+        tt(C("off", 0, 8), C("b2", 16, 24), C("b1", 0, 8), Op.add)
+        cp(C("off", 16, 24), C("b2", 16, 24))
 
         osc, ow, ocl = C("off", 0, 8), C("off", 8, 16), C("off", 16, 24)
         if last:
@@ -486,7 +492,7 @@ def rank_program(g, core, T, topo):
             for c in range(4):
                 mm(C("ps%d" % (4 + half), c, 256, 4), C("win", 4 + c, 1024, 8), C("ident", 64 * half, 64 * (half + 1)), True, True)
         ts(V("hw"), ka, 16, Op.logical_shift_right, 3, Op.bitwise_and)
-        cp(C("w32", 8 * t, 8 * t + 8), C("b2", 8, 16))
+        cp(C("w32", 8 * t, 8 * t + 8), C("off", 8, 16))
         cp(C("em", 0, 512), V("ps2", slice(0, 64)))
         act(C("em", 512, 768), C("ps4", 0, 256))
         cp(C("em", 768, 1024), C("ps5", 0, 256))
@@ -514,8 +520,15 @@ def rank_program(g, core, T, topo):
         sent[0] += len(peers)
 
         cp(V(land, rank), V(msg, rank))
+        if not last:
+            spread_frames(t + 1, 0, 8)
+            turned_frames(t + 1, "ps5")
         if t == 0:
-            spread_frames(1, 8, 16)
+            act(C("x192", 128, 256), C("frs", 128, 256), bias=192.0)
+            ts(V("i16"), xi(0, 16), pq, Op.is_equal)
+            for c in range(8):
+                mm(C("ps4", c, 128, 8), V("bd0", c), V("i16"), True, True)
+            act(V("acl"), C("ps4", 0, 128))
             owner_constants()
             act(V("i16x"), V("i16"), scale=64.0)
             act(V("m16"), V("i16"))
@@ -542,9 +555,9 @@ def rank_program(g, core, T, topo):
         tt(C("yy", 0, 20), C("s2", 0, 20), C("s2", 20, 40), Op.add)
         scan(C("tt", 0, 3), C("yy", 16, 19), C("pp", 0, 3), col("pp", 3), Op.min, Op.max)
         scan(C("yy", 20, 36), C("sd", 0, 16), C("yy", 0, 16), 0.0, Op.mult, Op.add)
+        scan(C("yy", 36, 52), C("sd", 16, 32), C("yy", 0, 16), 0.0, Op.mult, Op.add)
         cp(col("osel", 0), col("tt", 2))
-        for l in (1, 2):
-            scan(C("yy", 20 + 16 * l, 36 + 16 * l), C("sd", 16 * l, 16 * l + 16), C("yy", 0, 16), 0.0, Op.mult, Op.add)
+        scan(C("yy", 52, 68), C("sd", 32, 48), C("yy", 0, 16), 0.0, Op.mult, Op.add)
         ts(V("dcl"), IND(C("yy", 0, 68), col("osel", 0)), -2.0 * unit, Op.max, 2.0 * unit, Op.min)
         mine = C(dl, 16 * rank, 16 * rank + 16)
         ts(mine, V("dcl"), (192.0 - 0.5 + 1.0 / 512) * unit, Op.add)
@@ -559,17 +572,18 @@ def rank_program(g, core, T, topo):
         if not last:
             offsets()
             keep_matrices()
+            spread_frames(t + 1, 8, 16)
             iota(V("win"), [[0, 1024]], 0, 0)
-            if t + 2 < R:
-                spread_frames(t + 2)
         emit("x", None, [], [C(dl, 16 * r, 16 * r + 16) for r in peers], "dr%d" % t, wide * len(peers))
         if not last:
             tt(V("asum"), C("ps4", 0, 128), V(dl), Op.add)
-            block_diagonal(V("asum"))
+            ts(V("acl"), V("asum"), -127.0 / 64, Op.max, 127.0 / 64, Op.min)
+            block_diagonal(V("acl"))
         else:
             tt(V("afin"), IND(V(dl), V("lfin")), V("anat"), Op.add)
             ts(V("yas"), V("afin"), -127.0, Op.max, 127.0, Op.min)
-            store("s", "d_ya", T.ya[:], V("yas"))
+            store("s", "d_ya", T.ya[0:64, :], V("yas", part=slice(0, 64)))
+            store("a", "d_yb", T.ya[64:128, :], V("yas", part=slice(64, 128)))
 
     qsem = {"v": "qv", "a": "qa", "p": "qp", "g": "qg"}
     known = {q: {} for q in Q}
@@ -623,5 +637,5 @@ def rank_program(g, core, T, topo):
     for q in qsem:
         g.wait_ge(T.sem[qsem[q]], total[q])
     g.wait_ge(T.sem.sent, sent[0])
-    for s in ("d_yw", "d_ys", "d_ya"):
+    for s in ("d_yw", "d_ys", "d_ya", "d_yb"):
         g.sync.wait_ge(T.sem[s], 16)

@@ -5,47 +5,49 @@ from concourse.mybir import AluOpType, AxisListType, ActivationFunctionType
 F, BF, I, U = "float32", "bfloat16", "int32", "uint16"
 R = 3
 SB = {
-    "mus": (4096, BF), "mixs": (2056, I), "frs": (384, BF), "a0s": (128, BF), "st": (8, I),
-    "mtab": (4096, BF), "dif": (6144, BF), "mg": (1536, BF), "xp": (384, BF), "x192": (384, BF), "xrep": (6144, BF),
-    "xtn": (384, BF), "bd": (1024, BF), "asum": (128, BF), "acl": (128, BF), "anat": (128, F),
+    "mus": (4096, BF), "mixs": (2056, I), "frs": (392, BF), "a0s": (128, BF), "st": (8, I),
+    "mtab": (4096, BF), "dif": (6144, BF), "xp": (384, BF), "x192": (384, BF), "xrep": (6144, BF),
+    "xtn": (768, BF), "bd": (1024, BF), "asum": (128, U), "upb": (128, BF), "acl": (128, BF), "anat": (128, F),
     "afin": (128, F), "yas": (128, F),
     "lst": (24, U), "cand": (384, F), "tr": (384, F), "hi": (384, BF), "offm": (384, U),
-    "sc": (768, F), "mk": (16, I), "b1": (16, I), "b2": (32, I), "off": (24, U), "hw": (8, I),
+    "sc": (816, I), "b1": (16, I), "b2": (16, I), "off": (24, U), "hw": (8, I),
     "s1": (8, I), "en": (128, BF), "muw": (128, BF), "win": (1024, BF), "em": (1024, BF), "junk": (384, F), "ncol": (4, F),
-    "s4": (80, F), "s2": (40, F), "yy": (72, F), "tt": (4, F), "osel": (2, U), "dcl": (16, F),
+    "s4": (144, F), "s2": (72, F), "yy": (132, F), "osel": (6, U), "dcl": (32, F),
     "w32": (32, F), "wexp": (512, F), "outs": (512, F),
     "pi": (8, I), "pf": (24, F), "xi": (176, F), "ones": (512, BF), "ident": (128, BF), "in65": (128, BF),
-    "identf": (128, F), "za": (144, BF), "stp": (400, F), "i16": (16, BF), "i16x": (16, BF), "m16": (16, F), "bg": (8, F),
-    "lo": (8, F), "up": (8, F), "m64": (8, F), "r64": (128, BF), "kca": (192, BF), "nt": (24, F), "na": (24, F),
-    "biasl": (128, BF), "rst": (192, F), "ee": (512, BF), "io": (24, F), "lperm": (24, U),
+    "identf": (128, F), "za": (144, BF), "stp": (408, F), "kca": (204, BF), "i16": (16, BF), "i16x": (16, BF), "m16": (16, F), "bg": (8, F),
+    "lo": (8, F), "up": (8, F), "m64": (8, F), "r64": (128, BF), "nt": (24, F), "na": (24, F),
+    "biasl": (128, BF), "rst": (204, F), "ee": (512, BF), "io": (24, F), "lperm": (24, U),
     "l0": (8, U), "lfin": (8, U), "z8": (8, F), "selp": (320, BF), "seln": (320, BF), "sel64": (320, BF),
-    "sd": (48, F), "pp": (4, F),
+    "sd": (96, F), "pp": (8, F),
 }
 SCRATCH = {"b_" + k: ("sbuf", [128, n], d) for k, (n, d) in SB.items()}
 SHAPE = {k: (n,) for k, (n, d) in SB.items()}
-for _k, _s in (("mz", (8, 240)), ("dlt", (8, 49)), ("bd0", (8, 8, 16))):
+for _k, _s in (("mz", (8, 240)), ("dlt", (8, 52)), ("sq", (384, 17)), ("bd0", (8, 8, 16))):
     SCRATCH["b_" + _k] = ("sbuf", [128] + list(_s), BF)
     SHAPE[_k] = _s
 for _t in range(R):
-    SCRATCH["b_msg%d" % _t] = ("sbuf", [128, 8, 5, 4], F)
-    SCRATCH["b_land%d" % _t] = ("sbuf", [128, 8, 5, 4], F)
-    SCRATCH["b_dl%d" % _t] = ("sbuf", [128, 128], BF)
-    SHAPE["msg%d" % _t] = (8, 5, 4)
-    SHAPE["land%d" % _t] = (8, 5, 4)
+    SCRATCH["b_msg%d" % _t] = ("sbuf", [128, 4, 9, 4], U)
+    SCRATCH["b_land%d" % _t] = ("sbuf", [128, 8, 10, 4], U)
+    SCRATCH["b_dl%d" % _t] = ("sbuf", [128, 128], BF if _t == R - 1 else U)
+    SHAPE["msg%d" % _t] = (4, 9, 4)
+    SHAPE["land%d" % _t] = (8, 10, 4)
     SHAPE["dl%d" % _t] = (128,)
+SCRATCH["b_pw"] = ("psum", [128, 1024], F)
 for _b in range(8):
-    SCRATCH["b_ps%d" % _b] = ("psum", [128, 128, 4, 2], BF) if _b == 2 else ("psum", [128, 512], F)
     SHAPE["ps%d" % _b] = (128, 4, 2) if _b == 2 else (512,)
+    if _b not in (4, 5):
+        SCRATCH["b_ps%d" % _b] = ("psum", [128] + list(SHAPE["ps%d" % _b]), BF if _b == 2 else F)
 DMAS = ["d_s0", "d_a0", "d_fr", "d_mix", "d_mx", "d_mu0", "d_mu1", "d_mu2", "d_mu3", "d_mu4", "d_yw", "d_ys", "d_ya", "d_yb"]
 SEMAPHORES = ["qv", "qa", "qp", "qg", "sent"] + DMAS + ["ar%d" % t for t in range(R)] + ["dr%d" % t for t in range(R)]
 
 ALL = slice(None)
 PARTS = [(0, 4, "ps0", 0), (4, 4, "ps1", 64)]
-NA = 0
-CHUNKS = [(0, 0, 8, 16), (0, 1, 8, 16), (0, 2, NA, 16), (1, 0, 0, 16), (1, 1, 0, 8), (1, 1, 8, 16), (1, 2, 0, 7), (1, 2, 7, 12), (1, 2, 12, 15),
-          (1, 2, 15, 16)]
+NA = [2, 3, 3]
+CHUNKS = [(0, 2, 0, 16), (1, 0, 0, 16), (1, 1, 0, 16), (1, 2, 0, 9), (1, 2, 9, 14), (1, 2, 14, 16)]
+OFFSET = 24576.0
 LOADS = [0, 1024, 2048, 3072, 3584, 4096]
-XS = 3
+XS = 1
 
 
 def rank_program(g, core, T, topo):
@@ -64,7 +66,12 @@ def rank_program(g, core, T, topo):
             idx = (ALL,) * len(SHAPE[name])
         bits = np.zeros(index[name].size + 8, np.uint8)
         bits[index[name][idx].reshape(-1)] = 1
-        return (T["b_" + name][(part,) + tuple(idx)], [(name, int.from_bytes(np.packbits(bits).tobytes(), "big"))])
+        touched = [(name, int.from_bytes(np.packbits(bits).tobytes(), "big"))]
+        if name in ("ps4", "ps5"):
+            a, b, step = idx[0].indices(512)
+            o = 512 * (name == "ps5")
+            return (T.b_pw[part, o + a:o + b:step], touched)
+        return (T["b_" + name][(part,) + tuple(idx)], touched)
 
     def C(name, a, b, step=1, part=ALL):
         return V(name, slice(a, b, step), part=part)
@@ -173,10 +180,18 @@ def rank_program(g, core, T, topo):
         a = topo.addr(T.cores[r])
         return DstId(rid=a[0], pnc=a[1])
 
+    pairs = []
+    for r in range(N):
+        if not any(r in p for p in pairs):
+            pairs.append([r] + [x for x in range(N) if topo.mates(topo.chip(T.cores[r]), topo.chip(T.cores[x]))])
+    block = [b for b, p in enumerate(pairs) if rank in p][0]
+    plane = [r for r in peers if nearness(r) == 1]
+    share = len(engines) // len(pairs)
+    sign = 1.0 if rank < N // 2 else -1.0
     sent = [0]
 
     load("s", "d_a0", V("a0s"), T.a0[:])
-    load("a", "d_fr", V("frs"), T.fr[:])
+    load("a", "d_fr", C("frs", 0, 384), T.fr[:])
     load("s", "d_s0", V("st"), T.s0[:])
     load("a", "d_mx", C("mixs", 2048, 2056), T.mix[:, 0:8])
     load("s", "d_mix", C("mixs", 0, 2048), T.mix[:])
@@ -193,12 +208,15 @@ def rank_program(g, core, T, topo):
     iota(V("xi"), [[1, 176]], -16, 0)
     ms(V("ones"), 1.0)
     select(V("ident"), C("ones", 0, 128), [[-1, 128]], Op.is_equal, 0, 1)
-    iota(V("r64", part=one), [[0, 128]], 64, 0)
-    iota(V("kca", part=one), [[0, 4], [64, 16], [1024, 3]], -192, 0)
+    iota(V("kca", part=one), [[0, 4], [64, 17], [1024, 3]], -192, 0)
 
     for j, m in enumerate((15, 14, 12, 8, 16)):
         ts(col("pi", 1 + j), col("pi", 0), m, Op.bitwise_and)
+    ms(V("msg0", ALL, 8, 3), 0)
+    ms(C("frs", 384, 392), 0.0)
     cp(C("pf", 0, 6), C("pi", 0, 6))
+    ms(V("msg1", ALL, 8, 3), 0)
+    ms(V("msg2", ALL, 8, 3), 0)
     pp_, pq, m1, m2, m3, m4 = [col("pf", j) for j in range(6)]
     q16, ca, pg16, x1, x0, zc, q8 = [col("pf", j) for j in range(6, 13)]
     ts(q16, pq, 16.0, Op.mult)
@@ -208,8 +226,8 @@ def rank_program(g, core, T, topo):
     ts(C("l0", 0, 4), C("io", 0, 4), ca, Op.add)
     ts(C("l0", 4, 8), C("io", 12, 16), ca, Op.add)
     act(V("biasl", part=slice(0, 32)), C("ones", 0, 128, part=slice(0, 32)), scale=6.0)
-    act(V("biasl", part=slice(32, 64)), C("ones", 0, 128, part=slice(32, 64)), scale=1.0 / 4096)
     act(V("za"), C("ones", 0, 144), scale=0.0)
+    act(V("biasl", part=slice(32, 64)), C("ones", 0, 128, part=slice(32, 64)), scale=1.0 / 4096)
     act(x1, m4, scale=1.0 / 16)
     act(x0, m4, scale=-1.0 / 16, bias=1.0)
     act(q8, pq, scale=8.0)
@@ -222,9 +240,9 @@ def rank_program(g, core, T, topo):
     def block_diagonal(src):
         for k in range(8):
             if k < 5:
-                ts(C("bd", 128 * k, 128 * (k + 1)), src, col("bg", k), Op.mult)
+                ts(C("bd", 128 * k, 128 * (k + 1)), src, -127.0, Op.add, col("m64", k), Op.mult)
             else:
-                act(C("bd", 128 * k, 128 * (k + 1)), src, scale=col("bg", k))
+                act(C("bd", 128 * k, 128 * (k + 1)), src, scale=col("m64", k), bias=col("lo", k))
 
     def state_list():
         for h in range(3):
@@ -242,8 +260,9 @@ def rank_program(g, core, T, topo):
                 act(out, src)
 
     def turned_frames(t, bank):
-        mm(C(bank, 0, 128), C("frs", 128 * t, 128 * (t + 1)), V("ident"), True, True)
-        act(C("xtn", 128 * t, 128 * (t + 1)), C(bank, 0, 128), scale=-1.0)
+        for k in range(2):
+            mm(C(bank, 128 * k, 128 * (k + 1)), C("frs", 128 * t + 8 * k, 128 * (t + 1) + 8 * k), V("ident"), True, True)
+        act(C("xtn", 256 * t, 256 * (t + 1)), C(bank, 0, 256), scale=-1.0)
 
     frames(0)
     spread_frames(0, XS, 16)
@@ -255,44 +274,50 @@ def rank_program(g, core, T, topo):
     for c in range(8):
         turn(V("ps2", slice(16 * c, 16 * c + 16)), V("bd0", c), V("ident"))
     state_list()
+    ms(V("dlt", ALL, slice(49, 52)), 0.0)
     ms(V("dlt", ALL, 0), 4.0e9)
-    ts(C("pf", 16, 19), C("pf", 1, 4), m3, Op.subtract)
+    ts(C("pf", 16, 19), C("pf", 1, 4), -1.0, Op.mult, m3, Op.add)
     ts(C("b1", 0, 8), xi(0, 8), 128.0, Op.mult, q8, Op.add)
     cp(V("bd"), V("ps2"))
+    act(V("r64", part=one), C("ones", 0, 128, part=one), scale=64.0)
     act(V("identf"), V("ident"))
     act(V("in65"), V("ident"), scale=-65.0)
     act(V("sel64"), V("selp"), scale=64.0)
     turned_frames(0, "ps5")
     act(V("seln"), V("selp"), scale=-1.0)
+    for h in range(3):
+        act(C("kca", 48 + h, 204, 51, part=one), C("ones", 0, 4, part=one), scale=16.0e6)
     spread_frames(0, 0, XS, "a")
 
     select(V("ee"), V("ones"), [[1, 8], [16, 4], [0, 16]], Op.is_equal, 0, -1)
-    iota(V("rst"), [[0, 192]], 0, 0)
-    select(V("rst"), V("rst"), [[0, 4], [1, 48]], Op.not_equal, 0, 0, 4.0e9)
+    iota(V("rst"), [[0, 204]], 0, 0)
+    select(V("rst"), V("rst"), [[0, 4], [1, 51]], Op.not_equal, 0, 0, 4.0e9)
     for k in range(3):
         iota(C("na", 8 * k, 8 * k + 8), [[4 >> k, 2 << k], [0, 4 >> k]], 0, 0)
     iota(V("z8"), [[0, 8]], 0, 0)
-    for t in range(R):
-        iota(V("msg%d" % t, ALL, 4, 3), [[0, 8]], 0, 0)
     for l in range(3):
-        iota(C("sd", 16 * l, 16 * l + 16), [[0, 8 >> l], [1, 2 << l]], 0, 0)
+        iota(C("sd", 32 * l, 32 * l + 32), [[0, 16 >> l], [1, 2 << l]], 0, 0)
     iota(V("win"), [[0, 1024]], 0, 0)
     iota(V("mz"), [[0, 1920]], 0, 0)
 
     def count_tables():
         for k in range(3):
-            ts(C("nt", 8 * k, 8 * k + 8), C("na", 8 * k, 8 * k + 8), col("pf", 18 - k), Op.is_equal)
+            act(C("na", 8 * k, 8 * k + 8), C("na", 8 * k, 8 * k + 8), Fn.Abs, bias=col("pf", 18 - k))
+        act(V("nt"), V("na"), Fn.Relu, bias=1.0, scale=-1.0)
 
     def owner_constants():
-        ts(col("pp", 0), m2, 39.0, Op.add)
-        ts(col("pp", 1), m1, 21.0, Op.add)
+        ts(col("pp", 0), m2, 71.0, Op.add)
+        ts(col("pp", 1), m1, 37.0, Op.add)
         cp(col("pp", 2), pq)
-        ts(col("pp", 3), m3, 59.0, Op.add)
+        ts(col("pp", 3), m3, 107.0, Op.add)
+        ts(C("pp", 4, 8), C("pp", 0, 4), 16.0, Op.add)
         ts(V("sd"), V("sd"), 1.0, Op.min)
         ts(V("lfin"), xi(0, 8), q8, Op.add)
 
     def keep_matrices():
-        act(C("ps4", 0, 128), V("acl"), bias=-3.0)
+        act(V("upb"), V("acl"), Fn.Relu, bias=252.0, scale=-1.0)
+        act(C("ps5", 256, 384), V("acl"), bias=-2.0)
+        act(C("ps5", 384, 512), V("upb"), bias=254.0, scale=-1.0)
 
     def bias(bank):
         mm(V(bank), V("biasl", part=slice(0, 64)), V("ones", part=slice(0, 64)), True, False)
@@ -313,17 +338,18 @@ def rank_program(g, core, T, topo):
             act(C("hi", h, 384, 3), C("tr", 128 * h, 128 * (h + 1)), bias=192.0 - 0.5 + 1.0 / 128, scale=1.0 / 64)
 
     def key_b(bank):
-        mm(C(bank, 0, 384), V("in65"), V("hi"), True, False)
+        mm(C(bank, 0, 384), C("za", 16, 144, part=one), C("ones", 0, 384, part=one), True, False)
         for h in range(3):
-            mm(C(bank, h, 384, 3), V("identf"), C("tr", 128 * h, 128 * (h + 1)), False, h == 2)
+            mm(C(bank, h, 384, 3), V("identf"), C("tr", 128 * h, 128 * (h + 1)), False, False)
+        mm(C(bank, 0, 384), V("in65"), V("hi"), False, True)
 
     def key_start(parts):
         for j0, nj, bank, x in parts:
-            mm(C(bank, 0, 48 * nj), V("r64", part=one), C("kca", 0, 48 * nj, part=one), True, False)
+            mm(C(bank, 0, 51 * nj), V("r64", part=one), V("kca", part=one), True, False)
             for j in range(j0, j0 + nj):
                 for e in range(2):
                     b = 48 * (2 * (j // 2) + e)
-                    mm(C(bank, 48 * (j - j0), 48 * (j - j0 + 1)), moved("sel64", j, e), C("hi", b, b + 48), False, False)
+                    mm(C(bank, 51 * (j - j0), 51 * (j - j0) + 48), moved("sel64", j, e), C("hi", b, b + 48), False, False)
 
     def key_delta(bank):
         act(V("dlt", ALL, slice(1, 49)), C(bank, 0, 384), bias=64.0 * 65 * 192, scale=64.0)
@@ -332,19 +358,15 @@ def rank_program(g, core, T, topo):
         for j in range(8):
             for e in range(2):
                 b = 2 * (j // 2) + e
-                mm(C(bank, 48 * j, 48 * j + 48), moved("selp", j, e), V("dlt", b, slice(0, 48)), e == 0, False)
-                mm(C(bank, 48 * j, 48 * j + 48), moved("seln", j, e), V("dlt", b, slice(1, 49)), False, e == 1)
-        for x in range(2):
-            for e in range(2):
-                mm(C(bank, 384 + x, 392, 2), moved("selp", x, e), V("dlt", slice(e, 8, 2), 48), e == 0, e == 1)
+                mm(C(bank, 51 * j, 51 * j + 51), moved("selp", j, e), V("dlt", b, slice(0, 51)), e == 0, False)
+                mm(C(bank, 51 * j, 51 * j + 51), moved("seln", j, e), V("dlt", b, slice(1, 52)), False, e == 1)
 
     def key_d(bank):
-        act(C("stp", 0, 392), C(bank, 0, 392))
+        act(V("stp"), C(bank, 0, 408))
 
     bias("ps6")
     bias("ps7")
     bias("ps3")
-    bias("ps0")
     candidates()
     offsets()
 
@@ -368,20 +390,18 @@ def rank_program(g, core, T, topo):
             ts(m, m, 184.0, Op.max, 199.0, Op.min)
 
         if t == 0:
-            prod(0, "ps4", True); prod(1, "ps6", False)
-            by_scalar(0, "ps4"); key_a(); by_vector(1, "ps6")
-            prod(2, "ps5", True); prod(3, "ps7", False)
-            clip(0); by_scalar(2, "ps5"); by_vector(3, "ps7")
-            prod(4, "ps4", True); prod(5, "ps0", False)
-            clip(2)
-            by_scalar(4, "ps4"); by_vector(5, "ps0")
-            prod(6, "ps5", True); prod(7, "ps3", False)
+            prod(0, "ps4", True); prod(1, "ps5", True)
+            prod(2, "ps6", False); prod(3, "ps7", False)
+            by_scalar(0, "ps4"); by_scalar(1, "ps5"); key_a()
+            by_vector(2, "ps6"); by_vector(3, "ps7"); clip(0, 2)
+            prod(4, "ps4", True); prod(5, "ps5", True)
+            by_scalar(4, "ps4"); by_scalar(5, "ps5")
+            prod(7, "ps3", False); prod(6, "ps4", True)
             key_b("ps1")
-            clip(4); by_scalar(6, "ps5"); by_vector(7, "ps3"); clip(6)
+            by_scalar(6, "ps4"); by_vector(7, "ps3"); clip(4, 2); clip(6)
+            act(V("sq", ALL, 16), C("ones", 0, 384), scale=0.0)
             key_delta("ps1")
             key_start(PARTS[:1])
-            key_c("ps6")
-            key_start(PARTS[1:])
         else:
             prod(0, "ps4", True); prod(5, "ps6", False); prod(1, "ps5", True); prod(6, "ps7", False)
             by_scalar(0, "ps4"); by_vector(5, "ps6"); by_scalar(1, "ps5"); by_vector(6, "ps7")
@@ -389,6 +409,8 @@ def rank_program(g, core, T, topo):
             by_scalar(2, "ps4"); clip(0, 2); by_vector(7, "ps3")
             prod(3, "ps5", True); by_scalar(3, "ps5")
             prod(4, "ps4", True); clip(2, 2); by_scalar(4, "ps4"); clip(4)
+            key_d("ps0")
+            key_start(PARTS)
 
         def entry(k, h, q):
             return 192 * k + 64 * h + 4 * q
@@ -408,79 +430,85 @@ def rank_program(g, core, T, topo):
         def sums(k, h, q0, q1, stop):
             j0, nj, bank, x = PARTS[k]
             for q in range(q0, q1):
-                a, b = span(k, h, q, q + 1)
-                mm(C(bank, h, 48 * nj, 3), C("za", 15 - q, 143 - q), C("dif", a, b), False, stop and q == q1 - 1)
+                mm(C(bank, h, 51 * nj, 3), C("za", 15 - q, 143 - q), V("sq", slice(entry(k, h, q), entry(k, h, q + 1))), False,
+                   stop and q == q1 - 1)
 
         def square(k, h, q0, q1, stop=False):
             a, b = span(k, h, q0, q1)
-            act(C("dif", a, b), C("dif", a, b), Fn.Square)
+            act(V("sq", slice(a // 16, b // 16), slice(0, 16)), C("dif", a, b), Fn.Square)
             sums(k, h, q0, q1, stop)
 
-        def gather_a(h, n):
-            m = C("mg", 512 * h, 512 * h + 64 * n)
-            bank = C("ps%d" % (4 + h % 2), 0, 64 * n)
-            act(m, IND(V("mtab"), offs(0, h, 0, n)))
-            mm(bank, C("xtn", 128 * t, 128 * (t + 1)), C("ee", 0, 64 * n), True, False)
-            mm(bank, V("ident"), m, False, True)
-
-        def square_a(h, n, stop=False):
+        def gather_a(h, n, banks):
             a, b = span(0, h, 0, n)
-            act(C("dif", a, b), C("ps%d" % (4 + h % 2), 0, 64 * n), Fn.Square, bias=-192.0)
+            act(C("dif", a, b), IND(V("mtab"), offs(0, h, 0, n)))
+            for k, bank in enumerate(banks):
+                w = min(512, b - a - 512 * k)
+                mm(C(bank, 0, w), C("xtn", 256 * t + 128 * k, 256 * t + 128 * (k + 1)), C("ee", 0, w), True, False)
+            for k, bank in enumerate(banks):
+                w = min(512, b - a - 512 * k)
+                mm(C(bank, 0, w), V("ident"), C("dif", a + 512 * k, a + 512 * k + w), False, True)
+
+        def square_a(h, n, src, stop=False):
+            a, b = span(0, h, 0, n)
+            act(V("sq", slice(a // 16, b // 16), slice(0, 16)), src, Fn.Square, bias=-192.0)
             sums(0, h, 0, n, stop)
 
         def scans(k):
             j0, nj, bank, x = PARTS[k]
-            a, n = 48 * j0, 48 * nj
-            scan(C("sc", 384 + a, 384 + a + n), C("rst", 0, n), C(bank, 0, n), 0.0, Op.add, Op.min)
-            scan(C("sc", a, a + n), C("stp", a, a + n), C(bank, 0, n), 0.0, Op.add, Op.min)
+            a, n = 51 * j0, 51 * nj
+            keys = C(bank, 0, n)
+            scan(C("sc", 408 + a, 408 + a + n), C("rst", 0, n), keys, 0.0, Op.add, Op.min)
+            scan(C("sc", a, a + n), C("stp", a, a + n), keys, 0.0, Op.add, Op.min)
 
-        for ch in CHUNKS:
+        na = NA[t]
+        chunks = [(0, 1, na, 16)] + CHUNKS
+        for ch in chunks:
             gather_v(*ch)
-        gather_a(0, 8)
-        square(*CHUNKS[0]); gather_a(1, 8); square_a(0, 8)
+        gather_a(0, 16, ("ps4", "ps5"))
+        square(*chunks[0])
+        gather_a(1, na, ("ps3",))
+        square_a(0, 16, (T.b_pw[:, :], V("ps4")[1] + V("ps5")[1]))
         if t == 0:
-            key_d("ps6")
-        square(*CHUNKS[1])
-        if NA:
-            gather_a(2, NA)
-        square_a(1, 8); square(*CHUNKS[2], stop=NA == 0)
-        if NA:
-            square_a(2, NA, True)
+            key_c("ps6")
+            key_start(PARTS[1:])
+        square(*chunks[1])
+        square_a(1, na, C("ps3", 0, 64 * na), True)
         if t == 0:
-            count_tables()
+            cp(V("stp"), C("ps6", 0, 408))
         scans(0)
-        for ch in CHUNKS[3:]:
-            square(*ch, stop=ch == CHUNKS[-1])
+        for ch in chunks[2:]:
+            square(*ch, stop=ch == chunks[-1])
         if t == 0:
             act(C("x192", 0, 128), C("frs", 0, 128), bias=192.0)
-        if not last:
-            frames(t + 1)
+            count_tables()
+            frames(1)
         scans(1)
 
-        kb, ka = C("mk", 0, 8), C("mk", 8, 16)
-        cp(ka, C("sc", 384 + 47, 768, 48))
-        tt(kb, C("sc", 47, 384, 48), C("stp", 384, 392), Op.add)
-        ts(C("b2", 24, 32), ka, 0xFC0, Op.bitwise_and)
+        kb, ka = C("sc", 50, 408, 51), C("sc", 408 + 50, 816, 51)
+        ts(C("b2", 0, 8), ka, 0xFC0, Op.bitwise_and)
+        ts(C("b2", 8, 16), ka, 9, Op.logical_shift_right, 7, Op.bitwise_and)
         ts(C("b1", 8, 16), kb, 6, Op.logical_shift_right, 63, Op.bitwise_and)
-        ts(C("b2", 16, 24), ka, 9, Op.logical_shift_right, 7, Op.bitwise_and)
-        tt(C("off", 8, 16), C("b2", 24, 32), C("b1", 8, 16), Op.add)
-        tt(C("off", 0, 8), C("b2", 16, 24), C("b1", 0, 8), Op.add)
-        cp(C("off", 16, 24), C("b2", 16, 24))
+        ts(V("hw"), ka, 16, Op.logical_shift_right, 3, Op.bitwise_and)
+        cp(C("off", 16, 24), C("b2", 8, 16))
+        tt(C("off", 8, 16), C("b2", 0, 8), C("b1", 8, 16), Op.add)
+        tt(C("off", 0, 8), C("b2", 8, 16), C("b1", 0, 8), Op.add)
 
         osc, ow, ocl = C("off", 0, 8), C("off", 8, 16), C("off", 16, 24)
         if last:
             act(V("muw"), IND(V("mtab"), ow), bias=-192.0)
             cp(V("en"), IND(V("mus"), ow))
-            mm(C("ps6", 0, 128), V("ident"), C("xtn", 128 * t, 128 * (t + 1)), True, False)
+            mm(C("ps6", 0, 128), V("ident"), C("xtn", 256 * t, 256 * t + 128), True, False)
         else:
             act(V("muw"), IND(V("mus"), ow))
             tt(V("en"), IND(V("mtab"), ow), C("x192", 128 * t, 128 * (t + 1)), Op.subtract)
+        tt(V("st"), V("st"), V("hw"), Op.add)
         cp(IND(V("win"), osc), V("en"))
         mm(C("ps6", 0, 128), V("muw"), V("ident"), not last, True)
         msg, land, dl = "msg%d" % t, "land%d" % t, "dl%d" % t
 
         def count(l):
-            act(C("junk", 128 * l, 128 * (l + 1)), IND(C("nt", 8 * l, 8 * l + 8), ocl), bias=37.5, scale=-128.0, accum=col("ncol", l))
+            act(C("junk", 128 * l, 128 * (l + 1)), IND(C("nt", 8 * l, 8 * l + 8), ocl), bias=75.0 * sign + OFFSET / 128,
+                scale=-256.0 * sign, accum=col("ncol", l))
 
         count(0)
         act(V("mz", slice(0, 8), slice(112, 128)), C("ps6", 0, 128))
@@ -491,51 +519,59 @@ def rank_program(g, core, T, topo):
         for half in range(2):
             for c in range(4):
                 mm(C("ps%d" % (4 + half), c, 256, 4), C("win", 4 + c, 1024, 8), C("ident", 64 * half, 64 * (half + 1)), True, True)
-        ts(V("hw"), ka, 16, Op.logical_shift_right, 3, Op.bitwise_and)
-        cp(C("w32", 8 * t, 8 * t + 8), C("off", 8, 16))
+        if not last:
+            state_list()
         cp(C("em", 0, 512), V("ps2", slice(0, 64)))
         act(C("em", 512, 768), C("ps4", 0, 256))
         cp(C("em", 768, 1024), C("ps5", 0, 256))
-        tt(V("st"), V("st"), V("hw"), Op.add)
         for l in range(3):
-            act(V(msg, ALL, 4, l), V("z8"), bias=col("ncol", l))
-        unit = 1.0 if last else 1.0 / 64
+            ts(V(msg, ALL, 8, l), C("z8", 0, 4), col("ncol", l), Op.add)
         for half, bank in enumerate(("ps7", "ps3")):
             for k in range(8):
                 a = 512 * half + 64 * k
                 mm(C(bank, 0, 64), V("mz", k, slice(112 - 16 * k, 240 - 16 * k)), C("em", a, a + 64), k == 0, k == 7)
             if half == 0:
                 for x in range(2):
-                    ts(V(msg, ALL, 2 * x, ALL), C(bank, x, 64, 2), -unit / 256, Op.mult)
+                    ts(V(msg, ALL, slice(2 * x, 8, 4), ALL), C(bank, x, 64, 2), sign, Op.mult, OFFSET, Op.add)
             else:
-                ts(V(msg, ALL, slice(1, 4, 2), ALL), C(bank, 0, 64), -unit / 256, Op.mult)
-        if not last:
-            state_list()
+                ts(V(msg, ALL, slice(1, 8, 2), ALL), C(bank, 0, 64), sign, Op.mult, OFFSET, Op.add)
 
         def send_sums(msg=msg, land=land, t=t):
-            trs = [RemoteDMATransfer(dst_ids=[dst(r)], dma_engine_mask=1 << engines[j], remote_sem=T.sem["ar%d" % t],
-                                     src=T["b_" + msg][:, r], dst=T["b_" + land][:, rank]) for j, r in enumerate(peers)]
+            trs = []
+            for b in range(len(pairs)):
+                to = [r for r in peers if r in pairs[b]]
+                mask = sum(1 << e for e in engines[share * b:share * (b + 1)])
+                trs.append(RemoteDMATransfer(dst_ids=[dst(r) for r in to], dma_engine_mask=mask, remote_sem=T.sem["ar%d" % t],
+                                             srcs=[T["b_" + msg][:, b]], dsts=[T["b_" + land][:, rank, 0:9] for r in to]))
             g.remote_dma_fused(trs, local_sem=T.sem.sent)
         emit("g", send_sums, [V(msg)], [], "remote")
-        sent[0] += len(peers)
+        sent[0] += share * len(pairs)
 
-        cp(V(land, rank), V(msg, rank))
-        if not last:
-            spread_frames(t + 1, 0, 8)
-            turned_frames(t + 1, "ps5")
-        if t == 0:
-            act(C("x192", 128, 256), C("frs", 128, 256), bias=192.0)
-            ts(V("i16"), xi(0, 16), pq, Op.is_equal)
-            for c in range(8):
-                mm(C("ps4", c, 128, 8), V("bd0", c), V("i16"), True, True)
-            act(V("acl"), C("ps4", 0, 128))
-            owner_constants()
-            act(V("i16x"), V("i16"), scale=64.0)
-            act(V("m16"), V("i16"))
         if not last:
             candidates()
+        cp(V(land, rank, slice(0, 9)), V(msg, block))
+        cp(C("w32", 8 * t, 8 * t + 8), C("off", 8, 16))
+        if t == 0:
+            spread_frames(1, 0, 8)
+            ts(V("i16"), xi(0, 16), pq, Op.is_equal)
+            owner_constants()
+        if not last:
+            turned_frames(t + 1, "ps5")
             bias("ps6"); bias("ps7"); bias("ps3")
-            key_a(); key_b("ps5"); key_delta("ps5"); key_start(PARTS); key_c("ps4"); key_d("ps4")
+            key_a(); key_b("ps1")
+            key_delta("ps1")
+            if t == 0:
+                for c in range(8):
+                    mm(C("ps4", c, 128, 8), V("bd0", c), V("i16"), True, True)
+                act(V("lo"), V("bg"), scale=-127.0 / 64)
+                act(V("acl"), C("ps4", 0, 128), scale=64.0, bias=127.0)
+            keep_matrices()
+            key_c("ps0")
+            if t == 0:
+                frames(2)
+                act(C("x192", 128, 256), C("frs", 128, 256), bias=192.0)
+                act(V("i16x"), V("i16"), scale=64.0)
+                act(V("m16"), V("i16"))
         else:
             ts(V("s1"), V("st"), 2047, Op.bitwise_and)
             cp(C("w32", 24, 32), V("s1"))
@@ -549,35 +585,40 @@ def rank_program(g, core, T, topo):
             store("s", "d_yw", T.yw[:], C("outs", 0, 384, part=slice(0, 8)))
             store("s", "d_ys", T.ys[:], C("outs", 384, 512, part=slice(0, 8)))
 
-        emit("x", None, [], [V(land, r) for r in peers], "ar%d" % t, len(peers))
-        tt(V("s4"), V(land, slice(0, 4)), V(land, slice(4, 8)), Op.add)
-        tt(V("s2"), C("s4", 0, 40), C("s4", 40, 80), Op.add)
-        tt(C("yy", 0, 20), C("s2", 0, 20), C("s2", 20, 40), Op.add)
-        scan(C("tt", 0, 3), C("yy", 16, 19), C("pp", 0, 3), col("pp", 3), Op.min, Op.max)
-        scan(C("yy", 20, 36), C("sd", 0, 16), C("yy", 0, 16), 0.0, Op.mult, Op.add)
-        scan(C("yy", 36, 52), C("sd", 16, 32), C("yy", 0, 16), 0.0, Op.mult, Op.add)
-        cp(col("osel", 0), col("tt", 2))
-        scan(C("yy", 52, 68), C("sd", 32, 48), C("yy", 0, 16), 0.0, Op.mult, Op.add)
-        ts(V("dcl"), IND(C("yy", 0, 68), col("osel", 0)), -2.0 * unit, Op.max, 2.0 * unit, Op.min)
-        mine = C(dl, 16 * rank, 16 * rank + 16)
-        ts(mine, V("dcl"), (192.0 - 0.5 + 1.0 / 512) * unit, Op.add)
+        emit("x", None, [], [V(land, r) for r in peers], "ar%d" % t, share * len(peers))
+        tt(V("s4"), V(land, slice(0, 4), slice(0, 9)), V(land, slice(4, 8), slice(0, 9)), Op.subtract)
+        tt(V("s2"), C("s4", 0, 72), C("s4", 72, 144), Op.add)
+        tt(C("yy", 0, 36), C("s2", 0, 36), C("s2", 36, 72), Op.add)
+        for l in range(3):
+            scan(C("yy", 36 + 32 * l, 68 + 32 * l), C("sd", 32 * l, 32 * l + 32), C("yy", 0, 32), 0.0, Op.mult, Op.add)
+        for x in range(2):
+            scan(C("osel", x, 6, 2), C("yy", 32, 35), C("pp", 4 * x, 4 * x + 3), col("pp", 4 * x + 3), Op.min, Op.max)
+        picked = IND(V("yy"), C("osel", 4, 6))
+        mine = C(dl, 32 * block, 32 * block + 32)
+        if last:
+            ts(V("dcl"), picked, -512.0, Op.max, 512.0, Op.min)
+            ts(mine, V("dcl"), -1.0 / 256, Op.mult, 192.0 - 0.5 + 1.0 / 512, Op.add)
+        else:
+            ts(mine, picked, -1.0 / 256, Op.mult, 2.0 - 0.5 + 1.0 / 512, Op.add)
 
         def send_steps(mine=mine, t=t):
-            tr = RemoteDMATransfer(dst_ids=[dst(r) for r in peers], dma_engine_mask=wide_mask, remote_sem=T.sem["dr%d" % t],
-                                   srcs=[mine[0]], dsts=[mine[0] for r in peers])
+            tr = RemoteDMATransfer(dst_ids=[dst(r) for r in plane], dma_engine_mask=wide_mask, remote_sem=T.sem["dr%d" % t],
+                                   srcs=[mine[0]], dsts=[mine[0] for r in plane])
             g.remote_dma_fused([tr], local_sem=T.sem.sent)
         emit("g", send_steps, [mine], [], "remote")
         sent[0] += wide
 
         if not last:
             offsets()
-            keep_matrices()
-            spread_frames(t + 1, 8, 16)
+            if t == 0:
+                spread_frames(1, 8, 16)
             iota(V("win"), [[0, 1024]], 0, 0)
-        emit("x", None, [], [C(dl, 16 * r, 16 * r + 16) for r in peers], "dr%d" % t, wide * len(peers))
+            if t == 0:
+                spread_frames(2, 0, 16)
+        emit("x", None, [], [C(dl, 32 * b, 32 * b + 32) for b in range(len(pairs)) if b != block], "dr%d" % t, wide * len(plane))
         if not last:
-            tt(V("asum"), C("ps4", 0, 128), V(dl), Op.add)
-            ts(V("acl"), V("asum"), -127.0 / 64, Op.max, 127.0 / 64, Op.min)
+            tt(V("asum"), C("ps5", 256, 384), V(dl), Op.add)
+            tt(V("acl"), C("ps5", 384, 512), V("asum"), Op.min)
             block_diagonal(V("acl"))
         else:
             tt(V("afin"), IND(V(dl), V("lfin")), V("anat"), Op.add)

@@ -5,27 +5,28 @@ from concourse.mybir import AluOpType, AxisListType, ActivationFunctionType
 F, BF, I, U = "float32", "bfloat16", "int32", "uint16"
 R = 3
 SB = {
-    "mus": (4096, BF), "mixs": (2056, I), "frs": (392, BF), "a0s": (128, BF), "st": (8, I),
-    "mtab": (4096, BF), "dif": (6144, BF), "xp": (384, BF), "x192": (384, BF), "xrep": (6144, BF),
-    "xtn": (768, BF), "bd": (1024, BF), "asum": (128, U), "upb": (128, BF), "acl": (128, BF), "anat": (128, F),
-    "afin": (128, F), "yas": (128, F),
+    "mus": (4096, BF), "mixs": (2056, I), "frs": (384, BF), "a0s": (128, BF), "st": (8, I),
+    "mtab": (4096, BF), "dif": (6144, BF), "xp": (384, BF), "xneg": (384, BF), "xrep": (6144, BF),
+    "asum": (128, U), "upb": (128, BF), "acl": (128, BF),
     "lst": (24, U), "cand": (384, F), "tr": (384, F), "hi": (384, BF), "offm": (384, U),
     "sc": (816, I), "b1": (16, I), "b2": (16, I), "off": (24, U), "hw": (8, I),
-    "s1": (8, I), "en": (128, BF), "muw": (128, BF), "win": (1024, BF), "em": (1024, BF), "junk": (384, F), "ncol": (4, F),
-    "s4": (144, F), "s2": (72, F), "yy": (132, F), "osel": (6, U), "dcl": (32, F),
-    "w32": (32, F), "wexp": (512, F), "outs": (512, F),
+    "s1": (8, I), "en": (128, BF), "muw": (128, BF), "win": (1024, BF), "em": (1024, BF), "junk": (128, F), "ncol": (1, F),
+    "s4": (72, F), "s2": (72, F), "yy": (145, F), "osel": (6, U), "dcl": (32, F),
+    "anat": (128, F), "afin": (128, F), "w32": (32, F), "wexp": (512, F), "outs": (512, F),
     "pi": (8, I), "pf": (24, F), "xi": (176, F), "ones": (512, BF), "ident": (128, BF), "in65": (128, BF),
-    "identf": (128, F), "za": (144, BF), "stp": (408, F), "kca": (204, BF), "i16": (16, BF), "i16x": (16, BF), "m16": (16, F), "bg": (8, F),
-    "lo": (8, F), "up": (8, F), "m64": (8, F), "r64": (128, BF), "nt": (24, F), "na": (24, F),
-    "biasl": (128, BF), "rst": (204, F), "ee": (512, BF), "io": (24, F), "lperm": (24, U),
-    "l0": (8, U), "lfin": (8, U), "z8": (8, F), "selp": (320, BF), "seln": (320, BF), "sel64": (320, BF),
-    "sd": (96, F), "pp": (8, F),
+    "identf": (128, F), "za": (144, BF), "stp": (408, F), "kca": (204, BF), "i16": (16, BF), "m16": (16, F), "bg": (8, F),
+    "r64": (128, BF), "bd": (1024, BF), "ncb": (4, BF),
+    "biasl": (128, BF), "rst": (204, F), "io": (24, F), "lperm": (24, U),
+    "l0": (8, U), "lfin": (2, U), "lbd": (8, U), "m4": (4, F), "m127": (64, BF), "selp": (320, BF), "seln": (320, BF),
+    "sd": (96, BF), "pp": (8, F), "row": (14, F),
 }
 SCRATCH = {"b_" + k: ("sbuf", [128, n], d) for k, (n, d) in SB.items()}
 SHAPE = {k: (n,) for k, (n, d) in SB.items()}
-for _k, _s in (("mz", (8, 240)), ("dlt", (8, 52)), ("sq", (384, 17)), ("bd0", (8, 8, 16))):
+for _k, _s in (("mz", (8, 240)), ("dlt", (8, 52)), ("sq", (384, 17)), ("bd0", (8, 8, 16)), ("tree", (3, 8, 2, 8))):
     SCRATCH["b_" + _k] = ("sbuf", [128] + list(_s), BF)
     SHAPE[_k] = _s
+SCRATCH["b_yas"] = ("sbuf", [128, 8, 16], F)
+SHAPE["yas"] = (8, 16)
 for _t in range(R):
     SCRATCH["b_msg%d" % _t] = ("sbuf", [128, 4, 9, 4], U)
     SCRATCH["b_land%d" % _t] = ("sbuf", [128, 8, 10, 4], U)
@@ -33,21 +34,31 @@ for _t in range(R):
     SHAPE["msg%d" % _t] = (4, 9, 4)
     SHAPE["land%d" % _t] = (8, 10, 4)
     SHAPE["dl%d" % _t] = (128,)
-SCRATCH["b_pw"] = ("psum", [128, 1024], F)
+WIDE = ("ps3", "ps4", "ps5")
+SCRATCH["b_pw"] = ("psum", [128, 1536], F)
 for _b in range(8):
     SHAPE["ps%d" % _b] = (128, 4, 2) if _b == 2 else (512,)
-    if _b not in (4, 5):
+    if "ps%d" % _b not in WIDE:
         SCRATCH["b_ps%d" % _b] = ("psum", [128] + list(SHAPE["ps%d" % _b]), BF if _b == 2 else F)
-DMAS = ["d_s0", "d_a0", "d_fr", "d_mix", "d_mx", "d_mu0", "d_mu1", "d_mu2", "d_mu3", "d_mu4", "d_yw", "d_ys", "d_ya", "d_yb"]
-SEMAPHORES = ["qv", "qa", "qp", "qg", "sent"] + DMAS + ["ar%d" % t for t in range(R)] + ["dr%d" % t for t in range(R)]
+DMAS = ["d_s0", "d_a0", "d_fr", "d_mix", "d_mx", "d_mu0", "d_mu1", "d_mu2", "d_mu3", "d_mz0", "d_mz1", "d_yw", "d_ys", "d_ya", "d_yb"]
+SEMAPHORES = (["qv", "qa", "qp", "qg", "sent"] + DMAS + ["ar%d_%d" % (t, p) for t in range(R) for p in range(2)]
+              + ["dr%d_%d" % (t, b) for t in range(R) for b in range(4)])
 
 ALL = slice(None)
-PARTS = [(0, 4, "ps0", 0), (4, 4, "ps1", 64)]
-NA = [2, 3, 3]
-CHUNKS = [(0, 2, 0, 16), (1, 0, 0, 16), (1, 1, 0, 16), (1, 2, 0, 9), (1, 2, 9, 14), (1, 2, 14, 16)]
+KEYS = ["ps0", "ps1"]
+ROWS = 19
+CHUNKS = [(0, 32, 48), (1, 0, 16), (1, 16, 32), (1, 32, 41), (1, 41, 46), (1, 46, 48)]
 OFFSET = 24576.0
-LOADS = [0, 1024, 2048, 3072, 3584, 4096]
-XS = 1
+SEATS = [0, 4, 1, 3, 5, 7, 2, 6]
+PLACES = [(0, 2, 0), (1, 4, 2), (2, 2, 0)]
+LOADS = [0, 1536, 2560, 3584, 4096]
+EARLY = 1
+XS = 2
+XW = 5
+LEVEL = 40
+JV = 2
+BV = 5
+MID, LOW, HIGH = 64.0 * 192, 64.0 * 184, 64.0 * 199
 
 
 def rank_program(g, core, T, topo):
@@ -67,9 +78,9 @@ def rank_program(g, core, T, topo):
         bits = np.zeros(index[name].size + 8, np.uint8)
         bits[index[name][idx].reshape(-1)] = 1
         touched = [(name, int.from_bytes(np.packbits(bits).tobytes(), "big"))]
-        if name in ("ps4", "ps5"):
+        if name in WIDE:
             a, b, step = idx[0].indices(512)
-            o = 512 * (name == "ps5")
+            o = 512 * WIDE.index(name)
             return (T.b_pw[part, o + a:o + b:step], touched)
         return (T["b_" + name][(part,) + tuple(idx)], touched)
 
@@ -161,11 +172,11 @@ def rank_program(g, core, T, topo):
     def col(name, j):
         return C(name, j, j + 1)
 
-    peers = [(rank + j) % N for j in range(1, N)]
-
-    def nearness(r):
-        a, b = topo.chip(core), topo.chip(T.cores[r])
+    def nearness(r, s=rank):
+        a, b = topo.chip(T.cores[s]), topo.chip(T.cores[r])
         return 2 if topo.mates(a, b) else 1 if topo.same_plane(a, b) else 0
+
+    peers = [(rank + j) % N for j in range(1, N)]
     peers.sort(key=nearness)
     common = topo.mask(core, T.cores[peers[0]])
     for r in peers:
@@ -183,20 +194,42 @@ def rank_program(g, core, T, topo):
     pairs = []
     for r in range(N):
         if not any(r in p for p in pairs):
-            pairs.append([r] + [x for x in range(N) if topo.mates(topo.chip(T.cores[r]), topo.chip(T.cores[x]))])
-    block = [b for b, p in enumerate(pairs) if rank in p][0]
-    plane = [r for r in peers if nearness(r) == 1]
+            pairs.append([r] + [x for x in range(N) if nearness(x, r) == 2])
+
+    def side_of(r):
+        return 0 if r == 0 or nearness(r, 0) == 1 else 1
+
+    def seat(s, r):
+        return sorted([x for x in range(N) if x != r], key=lambda x: side_of(x) == side_of(r)).index(s)
+
+    def block_of(r):
+        return [b for b, p in enumerate(pairs) if r in p][0]
+
+    def plane_of(s):
+        return [r for r in [(s + j) % N for j in range(1, N)] if nearness(r, s) == 1]
+
+    def senders(r):
+        return [r] + sorted(plane_of(r), key=lambda s: plane_of(s).index(r))
+
+    block, plane = block_of(rank), plane_of(rank)
+    blocks = [block_of(s) for s in senders(rank)]
+    side = side_of(rank)
     share = len(engines) // len(pairs)
-    sign = 1.0 if rank < N // 2 else -1.0
+    sign = 1.0 - 2.0 * side
     sent = [0]
+
+    def load_means(k):
+        load("s", "d_mu%d" % k, C("mus", LOADS[k], LOADS[k + 1]), T.mu[:, LOADS[k]:LOADS[k + 1]])
 
     load("s", "d_a0", V("a0s"), T.a0[:])
     load("a", "d_fr", C("frs", 0, 384), T.fr[:])
     load("s", "d_s0", V("st"), T.s0[:])
     load("a", "d_mx", C("mixs", 2048, 2056), T.mix[:, 0:8])
+    for k in range(EARLY):
+        load_means(k)
     load("s", "d_mix", C("mixs", 0, 2048), T.mix[:])
-    for k in range(5):
-        load("s", "d_mu%d" % k, C("mus", LOADS[k], LOADS[k + 1]), T.mu[:, LOADS[k]:LOADS[k + 1]])
+    for k in range(EARLY, len(LOADS) - 1):
+        load_means(k)
 
     one = slice(0, 1)
 
@@ -208,48 +241,51 @@ def rank_program(g, core, T, topo):
     iota(V("xi"), [[1, 176]], -16, 0)
     ms(V("ones"), 1.0)
     select(V("ident"), C("ones", 0, 128), [[-1, 128]], Op.is_equal, 0, 1)
-    iota(V("kca", part=one), [[0, 4], [64, 17], [1024, 3]], -192, 0)
 
-    for j, m in enumerate((15, 14, 12, 8, 16)):
+    for j, m in enumerate((8, 12, 14, 15, 16)):
         ts(col("pi", 1 + j), col("pi", 0), m, Op.bitwise_and)
-    ms(V("msg0", ALL, 8, 3), 0)
-    ms(C("frs", 384, 392), 0.0)
     cp(C("pf", 0, 6), C("pi", 0, 6))
-    ms(V("msg1", ALL, 8, 3), 0)
-    ms(V("msg2", ALL, 8, 3), 0)
-    pp_, pq, m1, m2, m3, m4 = [col("pf", j) for j in range(6)]
-    q16, ca, pg16, x1, x0, zc, q8 = [col("pf", j) for j in range(6, 13)]
+    pp_, m3, m2, m1, pq, m4 = [col("pf", j) for j in range(6)]
+    q16, ca, pg16, x1, x0, q8, t1, t2, t3, t4, t5 = [col("pf", j) for j in range(6, 17)]
     ts(q16, pq, 16.0, Op.mult)
     ts(pg16, pp_, pq, Op.subtract)
     ts(ca, m2, -15.75, Op.mult, q16, Op.add)
     ts(V("bg"), xi(0, 8), 16.0, Op.mult, pg16, Op.is_equal)
     ts(C("l0", 0, 4), C("io", 0, 4), ca, Op.add)
     ts(C("l0", 4, 8), C("io", 12, 16), ca, Op.add)
-    act(V("biasl", part=slice(0, 32)), C("ones", 0, 128, part=slice(0, 32)), scale=6.0)
+    act(V("biasl", part=slice(0, 32)), C("ones", 0, 128, part=slice(0, 32)), scale=MID / 32)
     act(V("za"), C("ones", 0, 144), scale=0.0)
-    act(V("biasl", part=slice(32, 64)), C("ones", 0, 128, part=slice(32, 64)), scale=1.0 / 4096)
+    act(V("biasl", part=slice(32, 64)), C("ones", 0, 128, part=slice(32, 64)), scale=1.0 / 64)
     act(x1, m4, scale=1.0 / 16)
     act(x0, m4, scale=-1.0 / 16, bias=1.0)
     act(q8, pq, scale=8.0)
-    act(V("m64"), V("bg"), scale=1.0 / 64)
     act(C("za", 15, 143, 16), V("bg"), scale=262144.0)
     ts(V("lperm"), V("io"), ca, Op.add)
     ts(C("selp", 0, 160), C("xi", 0, 160), pp_, Op.is_equal, x0, Op.mult)
     ts(C("selp", 160, 320), C("xi", 0, 160), pp_, Op.is_equal, x1, Op.mult)
+    iota(V("kca", part=one), [[0, 4], [64, 17], [1024, 3]], -192, 0)
+    ts(C("b1", 0, JV), xi(0, JV), 128.0, Op.mult, q8, Op.add)
+    ts(C("b1", JV, 8), xi(0, 8 - JV), 128.0, Op.mult, q8, Op.add)
 
-    def block_diagonal(src):
-        for k in range(8):
-            if k < 5:
-                ts(C("bd", 128 * k, 128 * (k + 1)), src, -127.0, Op.add, col("m64", k), Op.mult)
-            else:
-                act(C("bd", 128 * k, 128 * (k + 1)), src, scale=col("m64", k), bias=col("lo", k))
+    def bias(bank):
+        mm(V(bank), V("biasl", part=slice(0, 64)), V("ones", part=slice(0, 64)), True, False)
+
+    def turn_blocks(out, in0):
+        emit("v", lambda: g.vector.transpose(out[0], in0[0]), [in0], [out])
+
+    bias("ps6")
+    bias("ps7")
+    bias("ps3")
 
     def state_list():
         for h in range(3):
             ts(C("lst", 8 * h, 8 * h + 8), V("st"), float(h), Op.add)
 
     def frames(t):
-        act(C("xp", 128 * t, 128 * (t + 1)), IND(C("frs", 128 * t, 128 * (t + 1)), V("l0")), bias=192.0)
+        act(C("xp", 128 * t, 128 * (t + 1)), IND(C("frs", 128 * t, 128 * (t + 1)), V("l0")), bias=-MID, scale=-64.0)
+
+    def frames_off(t):
+        act(C("xneg", 128 * t, 128 * (t + 1)), C("frs", 128 * t, 128 * (t + 1)), bias=-MID, scale=-64.0)
 
     def spread_frames(t, i0, i1, queue="g"):
         for i in range(i0, i1):
@@ -259,72 +295,84 @@ def rank_program(g, core, T, topo):
             else:
                 act(out, src)
 
-    def turned_frames(t, bank):
-        for k in range(2):
-            mm(C(bank, 128 * k, 128 * (k + 1)), C("frs", 128 * t + 8 * k, 128 * (t + 1) + 8 * k), V("ident"), True, True)
-        act(C("xtn", 256 * t, 256 * (t + 1)), C(bank, 0, 256), scale=-1.0)
-
     frames(0)
     spread_frames(0, XS, 16)
     for k in range(8):
-        if k < 5:
-            ts(V("bd0", ALL, k), V("a0s"), col("m64", k), Op.mult)
+        if k < BV:
+            ts(V("bd0", ALL, k), V("a0s"), col("bg", k), Op.mult)
         else:
-            act(V("bd0", ALL, k), V("a0s"), scale=col("m64", k))
-    for c in range(8):
-        turn(V("ps2", slice(16 * c, 16 * c + 16)), V("bd0", c), V("ident"))
+            act(V("bd0", ALL, k), V("a0s"), scale=col("bg", k))
+    for c, n, at in PLACES:
+        k = SEATS.index(c)
+        turn_blocks(C("bd", 128 * k, 128 * (k + n)), V("bd0", slice(c, 8, 8 // n)))
     state_list()
-    ms(V("dlt", ALL, slice(49, 52)), 0.0)
-    ms(V("dlt", ALL, 0), 4.0e9)
-    ts(C("pf", 16, 19), C("pf", 1, 4), -1.0, Op.mult, m3, Op.add)
-    ts(C("b1", 0, 8), xi(0, 8), 128.0, Op.mult, q8, Op.add)
-    cp(V("bd"), V("ps2"))
     act(V("r64", part=one), C("ones", 0, 128, part=one), scale=64.0)
     act(V("identf"), V("ident"))
-    act(V("in65"), V("ident"), scale=-65.0)
-    act(V("sel64"), V("selp"), scale=64.0)
-    turned_frames(0, "ps5")
+    act(V("in65"), V("ident"), scale=-65.0 / 64)
     act(V("seln"), V("selp"), scale=-1.0)
     for h in range(3):
         act(C("kca", 48 + h, 204, 51, part=one), C("ones", 0, 4, part=one), scale=16.0e6)
     spread_frames(0, 0, XS, "a")
 
-    select(V("ee"), V("ones"), [[1, 8], [16, 4], [0, 16]], Op.is_equal, 0, -1)
+    iota(V("sq", ALL, 16), [[0, 384]], 0, 0)
+    iota(V("dlt", ALL, slice(49, 52)), [[0, 24]], 0, 0)
+    select(V("dlt", ALL, 0), C("ones", 0, 8), [[0, 8]], Op.not_equal, 0, 0, 4.0e9)
     iota(V("rst"), [[0, 204]], 0, 0)
-    select(V("rst"), V("rst"), [[0, 4], [1, 51]], Op.not_equal, 0, 0, 4.0e9)
-    for k in range(3):
-        iota(C("na", 8 * k, 8 * k + 8), [[4 >> k, 2 << k], [0, 4 >> k]], 0, 0)
-    iota(V("z8"), [[0, 8]], 0, 0)
-    for l in range(3):
-        iota(C("sd", 32 * l, 32 * l + 32), [[0, 16 >> l], [1, 2 << l]], 0, 0)
+    select(C("rst", 0, 204, 51), C("rst", 0, 204, 51), [[0, 4]], Op.not_equal, 0, 0, 4.0e9)
     iota(V("win"), [[0, 1024]], 0, 0)
-    iota(V("mz"), [[0, 1920]], 0, 0)
-
-    def count_tables():
-        for k in range(3):
-            act(C("na", 8 * k, 8 * k + 8), C("na", 8 * k, 8 * k + 8), Fn.Abs, bias=col("pf", 18 - k))
-        act(V("nt"), V("na"), Fn.Relu, bias=1.0, scale=-1.0)
+    for x in range(2):
+        out, src = V("mz", slice(4 * x, 4 * x + 4)), C("win", 0, 960)
+        emit("s", lambda out=out, src=src: g.sync.dma_start(out[0], src[0]), [src], [out], "d_mz%d" % x, 16)
+    select(V("tree", 2), C("ones", 0, 128), [[-16, 8], [0, 2], [-1, 8]], Op.is_equal, 0, 1)
+    for l in range(2):
+        w = 4 >> l
+        for x in range(2):
+            select(V("tree", l, ALL, x), C("ones", 0, 64), [[-16, 8], [-w, 8 // w], [0, w]], Op.is_ge, 0, 1)
+            select(V("tree", l, ALL, x), V("tree", l, ALL, x), [[16, 8], [w, 8 // w], [0, w]], Op.is_ge, w - 1, -1)
+    iota(C("row", 0, 8), [[16, 2], [-LEVEL, 4]], 3 * LEVEL, 0)
+    for s, b in enumerate(blocks):
+        iota(col("row", 8 + s), [[0, 1]], 4 * b, 0)
+    for x in range(2):
+        iota(col("row", 12 + x), [[0, 1]], blocks[2 * x + 1] - blocks[2 * x] - 1, 0)
+    for l in range(3):
+        select(C("sd", 32 * l, 32 * l + 32), C("ones", 0, 32), [[0, 16 >> l], [1, 2 << l]], Op.not_equal, 0, 0)
+    iota(C("yy", 36, 113), [[0, 77]], 0, 0)
+    iota(V("m127"), [[0, 64]], -127, 0)
 
     def owner_constants():
-        ts(col("pp", 0), m2, 71.0, Op.add)
-        ts(col("pp", 1), m1, 37.0, Op.add)
-        cp(col("pp", 2), pq)
-        ts(col("pp", 3), m3, 107.0, Op.add)
-        ts(C("pp", 4, 8), C("pp", 0, 4), 16.0, Op.add)
-        ts(V("sd"), V("sd"), 1.0, Op.min)
-        ts(V("lfin"), xi(0, 8), q8, Op.add)
+        ts(t1, m1, -127.5, Op.mult, pg16, Op.add)
+        ts(t4, m2, -127.75, Op.mult, pg16, Op.add)
+        ts(C("pf", 20, 22), C("row", 12, 14), m3, Op.mult, 0.5, Op.mult)
+        ts(t2, pq, 128.0, Op.mult, t1, Op.add)
+        ts(t5, pq, 128.0, Op.mult, t4, Op.add)
+        tt(C("pf", 22, 24), C("pf", 20, 22), C("row", 8, 12, 2), Op.add)
+        tt(C("pp", 0, 4), C("pf", 1, 5), C("row", 0, 4), Op.add)
+        ts(C("lbd", 2, 6), C("row", 8, 12), t5, Op.add)
+        ts(C("lbd", 0, 2), C("pf", 22, 24), t2, Op.add)
+        tt(C("pp", 4, 8), C("pf", 1, 5), C("row", 4, 8), Op.add)
+        ts(V("m4"), xi(0, 4), 4.0, Op.mult, m2, Op.is_equal)
+        tt(V("m4"), V("m4"), C("row", 8, 12), Op.mult)
+        emit("v", lambda: g.vector.tensor_reduce(t3[0], T.b_m4[:], AxisListType.X, Op.add), [V("m4")], [t3])
+        ts(col("lbd", 6), t3, pp_, Op.add, m2, Op.subtract)
+
+    def final_lists():
+        ts(t3, m2, -7.75, Op.mult, q8, Op.add)
+        ts(V("i16"), xi(0, 16), pq, Op.is_equal)
+        ts(V("m16"), xi(0, 16), pq, Op.is_equal)
+        ts(V("lfin"), xi(0, 2), 4.0, Op.mult, t3, Op.add)
+
+    def diagonal(c, n, at):
+        k = SEATS.index(c)
+        return IND(C("bd", 128 * k, 128 * (k + n)), C("lbd", at, at + n))
 
     def keep_matrices():
         act(V("upb"), V("acl"), Fn.Relu, bias=252.0, scale=-1.0)
         act(C("ps5", 256, 384), V("acl"), bias=-2.0)
         act(C("ps5", 384, 512), V("upb"), bias=254.0, scale=-1.0)
 
-    def bias(bank):
-        mm(V(bank), V("biasl", part=slice(0, 64)), V("ones", part=slice(0, 64)), True, False)
-
     def candidates():
         cp(V("cand"), IND(C("mixs", 0, 2054), V("lst")))
-        emit("v", lambda: g.vector.transpose(T.b_tr[:], T.b_cand[:]), [V("cand")], [V("tr")])
+        turn_blocks(V("tr"), V("cand"))
 
     def offsets():
         cp(V("offm"), IND(V("cand"), V("lperm")))
@@ -335,21 +383,19 @@ def rank_program(g, core, T, topo):
 
     def key_a():
         for h in range(3):
-            act(C("hi", h, 384, 3), C("tr", 128 * h, 128 * (h + 1)), bias=192.0 - 0.5 + 1.0 / 128, scale=1.0 / 64)
+            act(C("hi", h, 384, 3), C("tr", 128 * h, 128 * (h + 1)), bias=MID - 31.5)
 
     def key_b(bank):
-        mm(C(bank, 0, 384), C("za", 16, 144, part=one), C("ones", 0, 384, part=one), True, False)
         for h in range(3):
-            mm(C(bank, h, 384, 3), V("identf"), C("tr", 128 * h, 128 * (h + 1)), False, False)
+            mm(C(bank, h, 384, 3), V("identf"), C("tr", 128 * h, 128 * (h + 1)), h == 0, False)
         mm(C(bank, 0, 384), V("in65"), V("hi"), False, True)
 
-    def key_start(parts):
-        for j0, nj, bank, x in parts:
-            mm(C(bank, 0, 51 * nj), V("r64", part=one), V("kca", part=one), True, False)
-            for j in range(j0, j0 + nj):
-                for e in range(2):
-                    b = 48 * (2 * (j // 2) + e)
-                    mm(C(bank, 51 * (j - j0), 51 * (j - j0) + 48), moved("sel64", j, e), C("hi", b, b + 48), False, False)
+    def key_start(k):
+        mm(C(KEYS[k], 0, 204), V("r64", part=one), V("kca", part=one), True, False)
+        for j in range(4 * k, 4 * k + 4):
+            for e in range(2):
+                b = 48 * (2 * (j // 2) + e)
+                mm(C(KEYS[k], 51 * (j % 4), 51 * (j % 4) + 48), moved("selp", j, e), C("hi", b, b + 48), False, False)
 
     def key_delta(bank):
         act(V("dlt", ALL, slice(1, 49)), C(bank, 0, 384), bias=64.0 * 65 * 192, scale=64.0)
@@ -364,168 +410,157 @@ def rank_program(g, core, T, topo):
     def key_d(bank):
         act(V("stp"), C(bank, 0, 408))
 
-    bias("ps6")
-    bias("ps7")
-    bias("ps3")
-    candidates()
-    offsets()
+    def left(c):
+        k = SEATS.index(c)
+        return C("bd", 128 * k, 128 * (k + 1))
 
     for t in range(R):
         last = t == R - 1
-        def cls(name, c):
-            return C(name, 512 * c, 512 * (c + 1))
+        def cls(name, c, a=0, b=512):
+            return C(name, 512 * c + a, 512 * c + b)
 
-        def prod(c, bank, start):
-            left = C("bd", c, 1024, 8) if t else C("bd", 128 * c, 128 * (c + 1))
-            mm(V(bank), left, cls("mus", c), start, True)
+        def prod(c, bank, start, a=0, b=512):
+            mm(C(bank, 0, b - a), left(c), cls("mus", c, a, b), start, True)
 
-        def by_scalar(c, bank):
-            act(cls("mtab", c), V(bank), bias=192.0 + 1.0 / 128)
+        def by_scalar(c, bank, a=0, b=512):
+            act(cls("mtab", c, a, b), C(bank, 0, b - a), bias=MID + 0.5)
 
-        def by_vector(c, bank):
-            ts(cls("mtab", c), V(bank), 184.0, Op.max, 199.0, Op.min)
+        def by_vector(c, bank, a=0, b=512):
+            ts(cls("mtab", c, a, b), C(bank, 0, b - a), LOW, Op.max, HIGH, Op.min)
 
-        def clip(c, n=1):
-            m = C("mtab", 512 * c, 512 * (c + n))
-            ts(m, m, 184.0, Op.max, 199.0, Op.min)
+        def clip(c, a=0, b=512):
+            m = cls("mtab", c, a, b)
+            ts(m, m, LOW, Op.max, HIGH, Op.min)
 
         if t == 0:
-            prod(0, "ps4", True); prod(1, "ps5", True)
-            prod(2, "ps6", False); prod(3, "ps7", False)
-            by_scalar(0, "ps4"); by_scalar(1, "ps5"); key_a()
-            by_vector(2, "ps6"); by_vector(3, "ps7"); clip(0, 2)
-            prod(4, "ps4", True); prod(5, "ps5", True)
-            by_scalar(4, "ps4"); by_scalar(5, "ps5")
-            prod(7, "ps3", False); prod(6, "ps4", True)
-            key_b("ps1")
-            by_scalar(6, "ps4"); by_vector(7, "ps3"); clip(4, 2); clip(6)
-            act(V("sq", ALL, 16), C("ones", 0, 384), scale=0.0)
+            prod(0, "ps6", False); prod(1, "ps7", False); prod(2, "ps4", True)
+            by_vector(0, "ps6"); by_scalar(2, "ps4"); by_vector(1, "ps7")
+            bias("ps6")
+            candidates()
+            offsets()
+            prod(3, "ps5", True); prod(4, "ps4", True)
+            by_scalar(3, "ps5"); by_scalar(4, "ps4"); key_a()
+            prod(5, "ps3", False); prod(6, "ps0", True)
+            by_vector(5, "ps3"); clip(2, 0, 1536); by_scalar(6, "ps0")
+            prod(7, "ps6", False); key_b("ps1")
+            by_vector(7, "ps6"); clip(6)
             key_delta("ps1")
-            key_start(PARTS[:1])
+            key_start(0)
         else:
-            prod(0, "ps4", True); prod(5, "ps6", False); prod(1, "ps5", True); prod(6, "ps7", False)
-            by_scalar(0, "ps4"); by_vector(5, "ps6"); by_scalar(1, "ps5"); by_vector(6, "ps7")
-            prod(2, "ps4", True); prod(7, "ps3", False)
-            by_scalar(2, "ps4"); clip(0, 2); by_vector(7, "ps3")
-            prod(3, "ps5", True); by_scalar(3, "ps5")
-            prod(4, "ps4", True); clip(2, 2); by_scalar(4, "ps4"); clip(4)
-            key_d("ps0")
-            key_start(PARTS)
+            prod(0, "ps1", True, 256, 512); prod(4, "ps6", False); prod(1, "ps4", True); prod(5, "ps7", False)
+            prod(3, "ps5", True); prod(2, "ps0", True); prod(7, "ps3", False)
+            by_scalar(0, "ps1", 256, 512); by_vector(4, "ps6"); by_scalar(1, "ps4")
+            by_vector(5, "ps7"); by_scalar(3, "ps5"); clip(0, 256, 1024)
+            prod(6, "ps4", True); prod(0, "ps1", True, 0, 256)
+            by_scalar(2, "ps0"); by_vector(7, "ps3"); by_scalar(6, "ps4"); by_scalar(0, "ps1", 0, 256)
+            clip(2, 0, 1024); clip(6); clip(0, 0, 256)
+            key_start(0); key_start(1)
 
-        def entry(k, h, q):
-            return 192 * k + 64 * h + 4 * q
+        def entry(k, row):
+            return 192 * k + 4 * row
 
-        def span(k, h, q0, q1):
-            return 16 * entry(k, h, q0), 16 * entry(k, h, q1)
+        def gather_v(k, r0, r1):
+            a, b = entry(k, r0), entry(k, r1)
+            x = 2048 * t + 1024 * k + 64 * (r0 % 16)
+            tt(C("dif", 16 * a, 16 * b), IND(V("mtab"), C("offm", a, b)), C("xrep", x, x + 16 * (b - a)), Op.add)
 
-        def offs(k, h, q0, q1):
-            return C("offm", entry(k, h, q0), entry(k, h, q1))
+        def sums(k, r0, r1):
+            for row in range(r0, r1):
+                h, q = divmod(row, 16)
+                mm(C(KEYS[k], h, 204, 3), C("za", 15 - q, 143 - q), V("sq", slice(entry(k, row), entry(k, row + 1))), False, row == 47)
 
-        def gather_v(k, h, q0, q1):
-            a, b = span(k, h, q0, q1)
-            j0, nj, bank, x = PARTS[k]
-            x = 2048 * t + 16 * x
-            tt(C("dif", a, b), IND(V("mtab"), offs(k, h, q0, q1)), C("xrep", x + 16 * nj * q0, x + 16 * nj * q1), Op.subtract)
+        def square(k, r0, r1):
+            a, b = entry(k, r0), entry(k, r1)
+            act(V("sq", slice(a, b), slice(0, 16)), C("dif", 16 * a, 16 * b), Fn.Square, scale=1.0 / 64)
+            sums(k, r0, r1)
 
-        def sums(k, h, q0, q1, stop):
-            j0, nj, bank, x = PARTS[k]
-            for q in range(q0, q1):
-                mm(C(bank, h, 51 * nj, 3), C("za", 15 - q, 143 - q), V("sq", slice(entry(k, h, q), entry(k, h, q + 1))), False,
-                   stop and q == q1 - 1)
+        def gather_a(rows):
+            n = 64 * rows
+            width = [min(512, n - 512 * k) for k in range(3)]
+            for k, bank in enumerate(WIDE):
+                x = 2048 * t + 512 * (k % 2)
+                mm(C(bank, 0, width[k]), V("ident"), C("xrep", x, x + width[k]), True, False)
+            act(C("dif", 0, n), IND(V("mtab"), C("offm", 0, n // 16)))
+            for k, bank in enumerate(WIDE):
+                mm(C(bank, 0, width[k]), V("ident"), C("dif", 512 * k, 512 * k + width[k]), False, True)
 
-        def square(k, h, q0, q1, stop=False):
-            a, b = span(k, h, q0, q1)
-            act(V("sq", slice(a // 16, b // 16), slice(0, 16)), C("dif", a, b), Fn.Square)
-            sums(k, h, q0, q1, stop)
-
-        def gather_a(h, n, banks):
-            a, b = span(0, h, 0, n)
-            act(C("dif", a, b), IND(V("mtab"), offs(0, h, 0, n)))
-            for k, bank in enumerate(banks):
-                w = min(512, b - a - 512 * k)
-                mm(C(bank, 0, w), C("xtn", 256 * t + 128 * k, 256 * t + 128 * (k + 1)), C("ee", 0, w), True, False)
-            for k, bank in enumerate(banks):
-                w = min(512, b - a - 512 * k)
-                mm(C(bank, 0, w), V("ident"), C("dif", a + 512 * k, a + 512 * k + w), False, True)
-
-        def square_a(h, n, src, stop=False):
-            a, b = span(0, h, 0, n)
-            act(V("sq", slice(a // 16, b // 16), slice(0, 16)), src, Fn.Square, bias=-192.0)
-            sums(0, h, 0, n, stop)
+        def square_a(rows):
+            src = (T.b_pw[:, 0:64 * rows], V("ps3")[1] + V("ps4")[1] + V("ps5")[1])
+            act(V("sq", slice(0, 4 * rows), slice(0, 16)), src, Fn.Square, scale=1.0 / 64)
+            sums(0, 0, rows)
 
         def scans(k):
-            j0, nj, bank, x = PARTS[k]
-            a, n = 51 * j0, 51 * nj
-            keys = C(bank, 0, n)
-            scan(C("sc", 408 + a, 408 + a + n), C("rst", 0, n), keys, 0.0, Op.add, Op.min)
-            scan(C("sc", a, a + n), C("stp", a, a + n), keys, 0.0, Op.add, Op.min)
+            a, keys = 204 * k, C(KEYS[k], 0, 204)
+            scan(C("sc", 408 + a, 612 + a), V("rst"), keys, 0.0, Op.add, Op.min)
+            scan(C("sc", a, a + 204), C("stp", a, a + 204), keys, 0.0, Op.add, Op.min)
 
-        na = NA[t]
-        chunks = [(0, 1, na, 16)] + CHUNKS
+        chunks = [(0, ROWS, 32)] + CHUNKS
         for ch in chunks:
             gather_v(*ch)
-        gather_a(0, 16, ("ps4", "ps5"))
-        square(*chunks[0])
-        gather_a(1, na, ("ps3",))
-        square_a(0, 16, (T.b_pw[:, :], V("ps4")[1] + V("ps5")[1]))
+        gather_a(ROWS)
         if t == 0:
             key_c("ps6")
-            key_start(PARTS[1:])
+            key_start(1)
+        square(*chunks[0])
+        square_a(ROWS)
         square(*chunks[1])
-        square_a(1, na, C("ps3", 0, 64 * na), True)
         if t == 0:
-            cp(V("stp"), C("ps6", 0, 408))
+            cp(C("stp", 0, 204), C("ps6", 0, 204))
         scans(0)
         for ch in chunks[2:]:
-            square(*ch, stop=ch == chunks[-1])
+            square(*ch)
         if t == 0:
-            act(C("x192", 0, 128), C("frs", 0, 128), bias=192.0)
-            count_tables()
-            frames(1)
+            act(C("stp", 204, 408), C("ps6", 204, 408))
+            frames_off(0)
         scans(1)
 
         kb, ka = C("sc", 50, 408, 51), C("sc", 408 + 50, 816, 51)
-        ts(C("b2", 0, 8), ka, 0xFC0, Op.bitwise_and)
-        ts(C("b2", 8, 16), ka, 9, Op.logical_shift_right, 7, Op.bitwise_and)
-        ts(C("b1", 8, 16), kb, 6, Op.logical_shift_right, 63, Op.bitwise_and)
-        ts(V("hw"), ka, 16, Op.logical_shift_right, 3, Op.bitwise_and)
-        cp(C("off", 16, 24), C("b2", 8, 16))
-        tt(C("off", 8, 16), C("b2", 0, 8), C("b1", 8, 16), Op.add)
-        tt(C("off", 0, 8), C("b2", 8, 16), C("b1", 0, 8), Op.add)
-
         osc, ow, ocl = C("off", 0, 8), C("off", 8, 16), C("off", 16, 24)
-        if last:
-            act(V("muw"), IND(V("mtab"), ow), bias=-192.0)
-            cp(V("en"), IND(V("mus"), ow))
-            mm(C("ps6", 0, 128), V("ident"), C("xtn", 256 * t, 256 * t + 128), True, False)
-        else:
-            act(V("muw"), IND(V("mus"), ow))
-            tt(V("en"), IND(V("mtab"), ow), C("x192", 128 * t, 128 * (t + 1)), Op.subtract)
-        tt(V("st"), V("st"), V("hw"), Op.add)
-        cp(IND(V("win"), osc), V("en"))
-        mm(C("ps6", 0, 128), V("muw"), V("ident"), not last, True)
+        ts(C("b2", 0, 8), ka, 0xFC0, Op.bitwise_and)
+        ts(C("b1", 8, 16), kb, 6, Op.logical_shift_right, 63, Op.bitwise_and)
+        ts(C("b2", 8, 16), ka, 9, Op.logical_shift_right, 7, Op.bitwise_and)
+        tt(ow, C("b2", 0, 8), C("b1", 8, 16), Op.add)
+        tt(osc, C("b2", 8, 16), C("b1", 0, 8), Op.add)
+
         msg, land, dl = "msg%d" % t, "land%d" % t, "dl%d" % t
-
-        def count(l):
-            act(C("junk", 128 * l, 128 * (l + 1)), IND(C("nt", 8 * l, 8 * l + 8), ocl), bias=75.0 * sign + OFFSET / 128,
-                scale=-256.0 * sign, accum=col("ncol", l))
-
-        count(0)
-        act(V("mz", slice(0, 8), slice(112, 128)), C("ps6", 0, 128))
-        count(1)
-        count(2)
+        if last:
+            act(C("en", 16 * JV, 128), IND(V("mus"), C("off", 8 + JV, 16)))
+            act(V("muw"), IND(V("mtab"), ow))
+            cp(C("en", 0, 16 * JV), IND(V("mus"), C("off", 8, 8 + JV)))
+            mm(C("ps6", 0, 128), C("xneg", 128 * t, 128 * (t + 1)), V("ident"), True, False)
+        else:
+            act(C("en", 16 * JV, 128), IND(V("mtab"), C("off", 8 + JV, 16)))
+            act(V("muw"), IND(V("mus"), ow))
+            tt(C("en", 0, 16 * JV), IND(V("mtab"), C("off", 8, 8 + JV)), C("xneg", 128 * t, 128 * t + 16 * JV), Op.add)
+        ts(ocl, C("b2", 8, 16), pg16, Op.add)
+        cp(IND(C("win", 0, 128 * JV), C("off", 0, JV)), C("en", 0, 16 * JV))
+        rest = IND(C("win", 128 * JV, 1024), C("off", JV, 8))
+        if last:
+            cp(rest, C("en", 16 * JV, 128))
+        else:
+            tt(rest, C("en", 16 * JV, 128), C("xneg", 128 * t + 16 * JV, 128 * (t + 1)), Op.add)
+        mm(C("ps6", 0, 128), V("muw"), V("ident"), not last, True)
+        act(V("junk"), IND(V("ident"), ocl), scale=-256.0 * sign, accum=V("ncol"))
+        act(V("mz", slice(0, 8), slice(112, 128)), C("ps6", 0, 128), scale=1.0 / 64)
+        act(V("ncb"), C("ones", 0, 4), scale=V("ncol"))
+        ts(V("hw"), ka, 16, Op.logical_shift_right, 3, Op.bitwise_and)
+        ms(V("msg%d" % t, ALL, 8, 3), 0)
+        tt(V("st"), V("st"), V("hw"), Op.add)
         for c in range(4):
             turn(V("ps2", slice(0, 64), c, ALL), C("win", c, 1024, 8), V("ident"))
         for half in range(2):
             for c in range(4):
                 mm(C("ps%d" % (4 + half), c, 256, 4), C("win", 4 + c, 1024, 8), C("ident", 64 * half, 64 * (half + 1)), True, True)
+        for l in range(3):
+            mm(C("ps1", l, 12, 3), V("tree", l), V("ncb"), True, True)
+        cp(C("w32", 8 * t, 8 * t + 8), ow)
         if not last:
             state_list()
-        cp(C("em", 0, 512), V("ps2", slice(0, 64)))
+        for x in range(2):
+            cp(C("em", 256 * x, 256 * x + 256), V("ps2", slice(32 * x, 32 * x + 32)))
         act(C("em", 512, 768), C("ps4", 0, 256))
         cp(C("em", 768, 1024), C("ps5", 0, 256))
-        for l in range(3):
-            ts(V(msg, ALL, 8, l), C("z8", 0, 4), col("ncol", l), Op.add)
+        ts(V(msg, ALL, 8, slice(0, 3)), C("ps1", 0, 12), OFFSET + sign * 256 * 300 / N, Op.add)
         for half, bank in enumerate(("ps7", "ps3")):
             for k in range(8):
                 a = 512 * half + 64 * k
@@ -541,88 +576,122 @@ def rank_program(g, core, T, topo):
             for b in range(len(pairs)):
                 to = [r for r in peers if r in pairs[b]]
                 mask = sum(1 << e for e in engines[share * b:share * (b + 1)])
-                trs.append(RemoteDMATransfer(dst_ids=[dst(r) for r in to], dma_engine_mask=mask, remote_sem=T.sem["ar%d" % t],
-                                             srcs=[T["b_" + msg][:, b]], dsts=[T["b_" + land][:, rank, 0:9] for r in to]))
+                trs.append(RemoteDMATransfer(dst_ids=[dst(r) for r in to], dma_engine_mask=mask, remote_sem=T.sem["ar%d_%d" % (t, side)],
+                                             srcs=[T["b_" + msg][:, b]], dsts=[T["b_" + land][:, seat(rank, r), 0:9] for r in to]))
             g.remote_dma_fused(trs, local_sem=T.sem.sent)
         emit("g", send_sums, [V(msg)], [], "remote")
         sent[0] += share * len(pairs)
 
+        nine = slice(0, 9)
         if not last:
             candidates()
-        cp(V(land, rank, slice(0, 9)), V(msg, block))
-        cp(C("w32", 8 * t, 8 * t + 8), C("off", 8, 16))
+        cp(V(land, N - 1, nine), V(msg, block))
         if t == 0:
-            spread_frames(1, 0, 8)
-            ts(V("i16"), xi(0, 16), pq, Op.is_equal)
+            frames(1)
+            spread_frames(1, 0, XW)
             owner_constants()
         if not last:
-            turned_frames(t + 1, "ps5")
+            frames_off(t + 1)
             bias("ps6"); bias("ps7"); bias("ps3")
+            if t:
+                keep_matrices()
             key_a(); key_b("ps1")
-            key_delta("ps1")
             if t == 0:
-                for c in range(8):
-                    mm(C("ps4", c, 128, 8), V("bd0", c), V("i16"), True, True)
-                act(V("lo"), V("bg"), scale=-127.0 / 64)
-                act(V("acl"), C("ps4", 0, 128), scale=64.0, bias=127.0)
-            keep_matrices()
+                for c, n, at in PLACES:
+                    act(C("acl", c, 128, 8 // n), diagonal(c, n, at), bias=127.0)
+                keep_matrices()
+            key_delta("ps1")
             key_c("ps0")
             if t == 0:
                 frames(2)
-                act(C("x192", 128, 256), C("frs", 128, 256), bias=192.0)
-                act(V("i16x"), V("i16"), scale=64.0)
-                act(V("m16"), V("i16"))
         else:
             ts(V("s1"), V("st"), 2047, Op.bitwise_and)
             cp(C("w32", 24, 32), V("s1"))
             for c in range(8):
-                mm(C("ps5", 16 * c, 16 * (c + 1)), C("bd", c, 1024, 8), V("i16x"), True, True)
-            for u in range(16):
+                for s, b in enumerate(blocks):
+                    mm(C("ps5", 32 * s + 4 * c, 32 * s + 4 * c + 4), left(c), C("i16", 4 * b, 4 * b + 4), True, True)
+            for u in range(8):
                 act(C("wexp", u, 512, 16), V("w32"), scale=col("m16", u))
+                ts(C("wexp", 8 + u, 512, 16), V("w32"), col("m16", 8 + u), Op.mult)
             mm(V("ps4", part=slice(0, 8)), V("bg"), V("wexp"), True, True)
             act(V("anat"), C("ps5", 0, 128), bias=-192.0)
             act(V("outs", part=slice(0, 8)), V("ps4", part=slice(0, 8)))
             store("s", "d_yw", T.yw[:], C("outs", 0, 384, part=slice(0, 8)))
             store("s", "d_ys", T.ys[:], C("outs", 384, 512, part=slice(0, 8)))
 
-        emit("x", None, [], [V(land, r) for r in peers], "ar%d" % t, share * len(peers))
-        tt(V("s4"), V(land, slice(0, 4), slice(0, 9)), V(land, slice(4, 8), slice(0, 9)), Op.subtract)
-        tt(V("s2"), C("s4", 0, 72), C("s4", 72, 144), Op.add)
+        far = N - 1 - len(plane)
+        other = C("ps7" if last else "ps4", 0, 72)
+        emit("x", None, [], [V(land, slice(0, far))], "ar%d_%d" % (t, 1 - side), share * far)
+        tt(other, V(land, slice(0, 2), nine), V(land, slice(2, 4), nine), Op.add)
+        emit("x", None, [], [V(land, slice(far, N - 1))], "ar%d_%d" % (t, side), share * len(plane))
+        tt(V("s4"), V(land, slice(4, 6), nine), V(land, slice(6, 8), nine), Op.add)
+        if side == 0:
+            tt(V("s2"), V("s4"), other, Op.subtract)
+        else:
+            tt(V("s2"), other, V("s4"), Op.subtract)
         tt(C("yy", 0, 36), C("s2", 0, 36), C("s2", 36, 72), Op.add)
-        for l in range(3):
-            scan(C("yy", 36 + 32 * l, 68 + 32 * l), C("sd", 32 * l, 32 * l + 32), C("yy", 0, 32), 0.0, Op.mult, Op.add)
         for x in range(2):
-            scan(C("osel", x, 6, 2), C("yy", 32, 35), C("pp", 4 * x, 4 * x + 3), col("pp", 4 * x + 3), Op.min, Op.max)
+            scan(C("osel", x, 6, 2), C("yy", 32, 35), C("pp", 4 * x + 1, 4 * x + 4), col("pp", 4 * x), Op.min, Op.max)
+        for l in range(3):
+            a = LEVEL * (l + 1) - (2 << l) + 1
+            scan(C("yy", a, a + 32), C("sd", 32 * l, 32 * l + 32), C("yy", 0, 32), 0.0, Op.mult, Op.add)
         picked = IND(V("yy"), C("osel", 4, 6))
-        mine = C(dl, 32 * block, 32 * block + 32)
+        mine = C(dl, 0, 32)
         if last:
             ts(V("dcl"), picked, -512.0, Op.max, 512.0, Op.min)
             ts(mine, V("dcl"), -1.0 / 256, Op.mult, 192.0 - 0.5 + 1.0 / 512, Op.add)
         else:
             ts(mine, picked, -1.0 / 256, Op.mult, 2.0 - 0.5 + 1.0 / 512, Op.add)
 
-        def send_steps(mine=mine, t=t):
-            tr = RemoteDMATransfer(dst_ids=[dst(r) for r in plane], dma_engine_mask=wide_mask, remote_sem=T.sem["dr%d" % t],
-                                   srcs=[mine[0]], dsts=[mine[0] for r in plane])
+        def send_steps(mine=mine, dl=dl, t=t):
+            at = [32 * senders(r).index(rank) for r in plane]
+            tr = RemoteDMATransfer(dst_ids=[dst(r) for r in plane], dma_engine_mask=wide_mask, remote_sem=T.sem["dr%d_%d" % (t, block)],
+                                   srcs=[mine[0]], dsts=[T["b_" + dl][:, a:a + 32] for a in at])
             g.remote_dma_fused([tr], local_sem=T.sem.sent)
         emit("g", send_steps, [mine], [], "remote")
         sent[0] += wide
 
+        def landed(s):
+            emit("x", None, [], [C(dl, 32 * s, 32 * s + 32)], "dr%d_%d" % (t, blocks[s]), wide)
+
+        def add_steps(s0, s1):
+            tt(C("asum", 32 * s0, 32 * s1), C("ps5", 256 + 32 * s0, 256 + 32 * s1), C(dl, 32 * s0, 32 * s1), Op.add)
+
+        def bound(s0, s1):
+            tt(C("acl", 32 * s0, 32 * s1), C("ps5", 384 + 32 * s0, 384 + 32 * s1), C("asum", 32 * s0, 32 * s1), Op.min)
+
+        def place(c, n, at):
+            tt(diagonal(c, n, at), C("acl", c, 128, 8 // n), C("m127", 0, 16 * n), Op.add)
+
+        def final(s):
+            tt(C("afin", 32 * s, 32 * s + 32), IND(C(dl, 32 * s, 32 * s + 32), V("lfin")), C("anat", 32 * s, 32 * s + 32), Op.add)
+
+        def final_bound(s):
+            mid = slice(4 * blocks[s], 4 * blocks[s] + 4)
+            ts(V("yas", ALL, mid), C("afin", 32 * s, 32 * s + 32), -127.0, Op.max, 127.0, Op.min)
+
         if not last:
             offsets()
+            add_steps(0, 1)
             if t == 0:
-                spread_frames(1, 8, 16)
+                final_lists()
+            bound(0, 1)
+            key_d("ps0")
+            if t == 0:
+                spread_frames(1, XW, 16)
             iota(V("win"), [[0, 1024]], 0, 0)
             if t == 0:
                 spread_frames(2, 0, 16)
-        emit("x", None, [], [C(dl, 32 * b, 32 * b + 32) for b in range(len(pairs)) if b != block], "dr%d" % t, wide * len(plane))
-        if not last:
-            tt(V("asum"), C("ps5", 256, 384), V(dl), Op.add)
-            tt(V("acl"), C("ps5", 384, 512), V("asum"), Op.min)
-            block_diagonal(V("acl"))
+            landed(1); add_steps(1, 2)
+            landed(2); add_steps(2, 3); bound(1, 2)
+            landed(3); add_steps(3, 4); bound(2, 3); bound(3, 4)
+            for piece in [(0, 1, 6), (4, 1, 6)] + PLACES[1:]:
+                place(*piece)
         else:
-            tt(V("afin"), IND(V(dl), V("lfin")), V("anat"), Op.add)
-            ts(V("yas"), V("afin"), -127.0, Op.max, 127.0, Op.min)
+            final(0); final_bound(0)
+            landed(1); final(1)
+            landed(2); final(2); final_bound(1)
+            landed(3); final(3); final_bound(2); final_bound(3)
             store("s", "d_ya", T.ya[0:64, :], V("yas", part=slice(0, 64)))
             store("a", "d_yb", T.ya[64:128, :], V("yas", part=slice(64, 128)))
 

import numpy as np
from concourse.bass import DstId, RemoteDMATransfer
from concourse.mybir import AluOpType, AxisListType, ActivationFunctionType

F, BF, I, U = "float32", "bfloat16", "int32", "uint16"
R = 3
SB = {
    "mus": (4096, BF), "mixs": (2056, I), "frs": (384, BF), "a0s": (128, BF), "st": (8, I),
    "mtab": (4096, BF), "dif": (6144, BF), "xp": (384, BF), "xneg": (384, BF), "xrep": (6144, BF),
    "asum": (128, U), "upb": (128, BF), "acl": (128, BF),
    "lst": (24, U), "cand": (384, F), "tr": (384, F), "hi": (384, BF), "offm": (384, U),
    "sc": (816, I), "b1": (16, I), "b2": (16, I), "off": (24, U), "hw": (8, I),
    "s1": (8, I), "en": (128, BF), "muw": (128, BF), "win": (1024, BF), "em": (1024, BF), "junk": (128, F), "ncol": (1, F),
    "s4": (72, F), "s2": (72, F), "yy": (145, F), "osel": (6, U), "dcl": (32, F),
    "anat": (128, F), "afin": (128, F), "w32": (32, F), "wexp": (512, F), "outs": (512, F),
    "pi": (8, I), "pf": (24, F), "xi": (176, F), "ones": (512, BF), "ident": (128, BF), "in65": (128, BF),
    "identf": (128, F), "za": (144, BF), "stp": (408, F), "kca": (204, BF), "i16": (16, BF), "m16": (16, F), "bg": (8, F),
    "r64": (128, BF), "bd": (1024, BF), "ncb": (4, BF),
    "biasl": (128, BF), "rst": (204, F), "io": (24, F), "lperm": (24, U),
    "l0": (8, U), "lfin": (2, U), "lbd": (8, U), "m4": (4, F), "m127": (64, BF), "selp": (320, BF), "seln": (320, BF),
    "sd": (96, BF), "pp": (8, F), "row": (14, F),
}
SCRATCH = {"b_" + k: ("sbuf", [128, n], d) for k, (n, d) in SB.items()}
SHAPE = {k: (n,) for k, (n, d) in SB.items()}
for _k, _s in (("mz", (8, 240)), ("dlt", (8, 52)), ("sq", (384, 17)), ("bd0", (8, 8, 16)), ("tree", (3, 8, 2, 8))):
    SCRATCH["b_" + _k] = ("sbuf", [128] + list(_s), BF)
    SHAPE[_k] = _s
SCRATCH["b_yas"] = ("sbuf", [128, 8, 16], F)
SHAPE["yas"] = (8, 16)
for _t in range(R):
    SCRATCH["b_msg%d" % _t] = ("sbuf", [128, 4, 9, 4], U)
    SCRATCH["b_land%d" % _t] = ("sbuf", [128, 8, 10, 4], U)
    SCRATCH["b_dl%d" % _t] = ("sbuf", [128, 128], BF if _t == R - 1 else U)
    SHAPE["msg%d" % _t] = (4, 9, 4)
    SHAPE["land%d" % _t] = (8, 10, 4)
    SHAPE["dl%d" % _t] = (128,)
WIDE = ("ps3", "ps4", "ps5")
SCRATCH["b_pw"] = ("psum", [128, 1536], F)
for _b in range(8):
    SHAPE["ps%d" % _b] = (128, 4, 2) if _b == 2 else (512,)
    if "ps%d" % _b not in WIDE:
        SCRATCH["b_ps%d" % _b] = ("psum", [128] + list(SHAPE["ps%d" % _b]), BF if _b == 2 else F)
DMAS = ["d_s0", "d_a0", "d_fr", "d_mix", "d_mx", "d_mu0", "d_mu1", "d_mu2", "d_mu3", "d_mz0", "d_mz1", "d_yw", "d_ys", "d_ya", "d_yb"]
SEMAPHORES = (["qv", "qa", "qp", "qg", "sent"] + DMAS + ["ar%d_%d" % (t, p) for t in range(R) for p in range(2)]
              + ["dr%d_%d" % (t, b) for t in range(R) for b in range(4)])

ALL = slice(None)
KEYS = ["ps0", "ps1"]
ROWS = 19
CHUNKS = [(0, 32, 48), (1, 0, 16), (1, 16, 32), (1, 32, 41), (1, 41, 46), (1, 46, 48)]
OFFSET = 24576.0
SEATS = [0, 4, 1, 3, 5, 7, 2, 6]
PLACES = [(0, 2, 0), (1, 4, 2), (2, 2, 0)]
LOADS = [0, 1536, 2560, 3584, 4096]
EARLY = 1
XS = 2
XW = 5
LEVEL = 40
JV = 2
BV = 5
MID, LOW, HIGH = 64.0 * 192, 64.0 * 184, 64.0 * 199


def rank_program(g, core, T, topo):
    rank = T.rank_of(core)
    if rank is None:
        return
    N = len(T.cores)
    Op, Fn = AluOpType, ActivationFunctionType
    Q = {"v": g.vector, "a": g.scalar, "p": g.tensor, "g": g, "s": g.sync}
    ops = []
    hist = {}
    index = {k: np.arange(int(np.prod(s))).reshape(s) for k, s in SHAPE.items()}

    def V(name, *idx, part=ALL):
        if not idx:
            idx = (ALL,) * len(SHAPE[name])
        bits = np.zeros(index[name].size + 8, np.uint8)
        bits[index[name][idx].reshape(-1)] = 1
        touched = [(name, int.from_bytes(np.packbits(bits).tobytes(), "big"))]
        if name in WIDE:
            a, b, step = idx[0].indices(512)
            o = 512 * WIDE.index(name)
            return (T.b_pw[part, o + a:o + b:step], touched)
        return (T["b_" + name][(part,) + tuple(idx)], touched)

    def C(name, a, b, step=1, part=ALL):
        return V(name, slice(a, b, step), part=part)

    def IND(win, offs):
        return (win[0].indirect(offs[0]), win[1], offs[1])

    def emit(q, call, reads, writes, sem=None, count=0):
        me = len(ops)
        deps = set()
        acc = []
        for r in reads:
            if isinstance(r, tuple):
                for part in r[1:]:
                    acc += [(n, m, False) for n, m in part]
        for w in writes:
            acc += [(n, m, True) for n, m in w[1]]
            for part in w[2:]:
                acc += [(n, m, False) for n, m in part]
        for n, m, wr in acc:
            psum = n.startswith("ps")
            for (m2, o, wr2) in hist.get(n, []):
                same = ops[o][0] == q and ops[o][3] is None and sem is None
                if psum and not same:
                    deps.add(o)
                elif (m & m2) and (wr or wr2) and not (same and q == "p"):
                    deps.add(o)
        ops.append([q, call, deps, sem, count])
        for n, m, wr in acc:
            h = hist.get(n, [])
            if n.startswith("ps"):
                h = [e for e in h if ops[e[1]][0] == q and (q != "p" or e[1] == me)]
            if wr:
                h = [e for e in h if (e[0] & ~m) or e[1] == me]
            h.append((m, me, wr))
            hist[n] = h
        return me

    def ap(x):
        return x[0] if isinstance(x, tuple) else x

    def ts(out, in0, s1, op0, s2=None, op1=None):
        if op1 is None:
            emit("v", lambda: g.vector.tensor_scalar(out[0], in0[0], ap(s1), None, op0), [in0, s1], [out])
        else:
            emit("v", lambda: g.vector.tensor_scalar(out[0], in0[0], ap(s1), ap(s2), op0, op1), [in0, s1, s2], [out])

    def tt(out, in0, in1, op):
        emit("v", lambda: g.vector.tensor_tensor(out[0], in0[0], in1[0], op), [in0, in1], [out])

    def cp(out, in0):
        emit("v", lambda: g.vector.tensor_copy(out[0], in0[0]), [in0], [out])

    def ms(out, val):
        emit("v", lambda: g.vector.memset(out[0], val), [], [out])

    def scan(out, d0, d1, init, op0, op1):
        emit("v", lambda: g.vector.tensor_tensor_scan(out[0], d0[0], d1[0], ap(init), op0, op1), [d0, d1, init], [out])

    def act(out, in0, func=Fn.Identity, bias=0.0, scale=1.0, accum=None):
        if accum is None:
            emit("a", lambda: g.scalar.activation(out[0], in0[0], func, bias=ap(bias), scale=ap(scale)), [in0, bias, scale], [out])
        else:
            emit("a", lambda: g.scalar.activation(out[0], in0[0], func, bias=bias, scale=scale, accum_out=accum[0]), [in0], [out, accum])

    def mm(out, lhsT, rhs, start, stop):
        emit("p", lambda: g.tensor.matmul(out[0], lhsT[0], rhs[0], start, stop), [lhsT, rhs], [out])

    def turn(out, in0, ident):
        emit("p", lambda: g.tensor.transpose(out[0], in0[0], ident[0]), [in0, ident], [out])

    def iota(out, pattern, base, cm, flt=True):
        if flt:
            emit("g", lambda: g.iota(out[0], pattern, base, cm, allow_small_or_imprecise_dtypes=True), [], [out])
        else:
            emit("g", lambda: g.iota(out[0], pattern, base, cm), [], [out])

    def select(out, in0, pattern, op, base, cm, fill=0.0):
        emit("g", lambda: g.affine_select(out[0], in0[0], pattern, op, fill, base, cm), [in0], [out])

    def load(q, sem, out, src):
        emit(q, lambda: Q[q].dma_start(out[0], src), [], [out], sem, 16)

    def store(q, sem, dst, in0):
        emit(q, lambda: Q[q].dma_start(dst, in0[0]), [in0], [], sem, 16)

    def col(name, j):
        return C(name, j, j + 1)

    def nearness(r, s=rank):
        a, b = topo.chip(T.cores[s]), topo.chip(T.cores[r])
        return 2 if topo.mates(a, b) else 1 if topo.same_plane(a, b) else 0

    peers = [(rank + j) % N for j in range(1, N)]
    peers.sort(key=nearness)
    common = topo.mask(core, T.cores[peers[0]])
    for r in peers:
        common &= topo.mask(core, T.cores[r])
    engines = [e for e in topo.engines(core, T.cores[peers[0]]) if common >> e & 1]
    wide = 1
    while 2 * wide <= len(engines):
        wide *= 2
    wide_mask = sum(1 << e for e in engines[:wide])

    def dst(r):
        a = topo.addr(T.cores[r])
        return DstId(rid=a[0], pnc=a[1])

    pairs = []
    for r in range(N):
        if not any(r in p for p in pairs):
            pairs.append([r] + [x for x in range(N) if nearness(x, r) == 2])

    def side_of(r):
        return 0 if r == 0 or nearness(r, 0) == 1 else 1

    def seat(s, r):
        return sorted([x for x in range(N) if x != r], key=lambda x: side_of(x) == side_of(r)).index(s)

    def block_of(r):
        return [b for b, p in enumerate(pairs) if r in p][0]

    def plane_of(s):
        return [r for r in [(s + j) % N for j in range(1, N)] if nearness(r, s) == 1]

    def senders(r):
        return [r] + sorted(plane_of(r), key=lambda s: plane_of(s).index(r))

    block, plane = block_of(rank), plane_of(rank)
    blocks = [block_of(s) for s in senders(rank)]
    side = side_of(rank)
    share = len(engines) // len(pairs)
    sign = 1.0 - 2.0 * side
    sent = [0]

    def load_means(k):
        load("s", "d_mu%d" % k, C("mus", LOADS[k], LOADS[k + 1]), T.mu[:, LOADS[k]:LOADS[k + 1]])

    load("s", "d_a0", V("a0s"), T.a0[:])
    load("a", "d_fr", C("frs", 0, 384), T.fr[:])
    load("s", "d_s0", V("st"), T.s0[:])
    load("a", "d_mx", C("mixs", 2048, 2056), T.mix[:, 0:8])
    for k in range(EARLY):
        load_means(k)
    load("s", "d_mix", C("mixs", 0, 2048), T.mix[:])
    for k in range(EARLY, len(LOADS) - 1):
        load_means(k)

    one = slice(0, 1)

    def xi(a, b):
        return C("xi", 16 + a, 16 + b)

    iota(col("pi", 0), [[1, 1]], 0, 1, False)
    iota(V("io"), [[64, 2], [128, 3], [4, 4]], 0, 0)
    iota(V("xi"), [[1, 176]], -16, 0)
    ms(V("ones"), 1.0)
    select(V("ident"), C("ones", 0, 128), [[-1, 128]], Op.is_equal, 0, 1)

    for j, m in enumerate((8, 12, 14, 15, 16)):
        ts(col("pi", 1 + j), col("pi", 0), m, Op.bitwise_and)
    cp(C("pf", 0, 6), C("pi", 0, 6))
    pp_, m3, m2, m1, pq, m4 = [col("pf", j) for j in range(6)]
    q16, ca, pg16, x1, x0, q8, t1, t2, t3, t4, t5 = [col("pf", j) for j in range(6, 17)]
    ts(q16, pq, 16.0, Op.mult)
    ts(pg16, pp_, pq, Op.subtract)
    ts(ca, m2, -15.75, Op.mult, q16, Op.add)
    ts(V("bg"), xi(0, 8), 16.0, Op.mult, pg16, Op.is_equal)
    ts(C("l0", 0, 4), C("io", 0, 4), ca, Op.add)
    ts(C("l0", 4, 8), C("io", 12, 16), ca, Op.add)
    act(V("biasl", part=slice(0, 32)), C("ones", 0, 128, part=slice(0, 32)), scale=MID / 32)
    act(V("za"), C("ones", 0, 144), scale=0.0)
    act(V("biasl", part=slice(32, 64)), C("ones", 0, 128, part=slice(32, 64)), scale=1.0 / 64)
    act(x1, m4, scale=1.0 / 16)
    act(x0, m4, scale=-1.0 / 16, bias=1.0)
    act(q8, pq, scale=8.0)
    act(C("za", 15, 143, 16), V("bg"), scale=262144.0)
    ts(V("lperm"), V("io"), ca, Op.add)
    ts(C("selp", 0, 160), C("xi", 0, 160), pp_, Op.is_equal, x0, Op.mult)
    ts(C("selp", 160, 320), C("xi", 0, 160), pp_, Op.is_equal, x1, Op.mult)
    iota(V("kca", part=one), [[0, 4], [64, 17], [1024, 3]], -192, 0)
    ts(C("b1", 0, JV), xi(0, JV), 128.0, Op.mult, q8, Op.add)
    ts(C("b1", JV, 8), xi(0, 8 - JV), 128.0, Op.mult, q8, Op.add)

    def bias(bank):
        mm(V(bank), V("biasl", part=slice(0, 64)), V("ones", part=slice(0, 64)), True, False)

    def turn_blocks(out, in0):
        emit("v", lambda: g.vector.transpose(out[0], in0[0]), [in0], [out])

    bias("ps6")
    bias("ps7")
    bias("ps3")

    def state_list():
        for h in range(3):
            ts(C("lst", 8 * h, 8 * h + 8), V("st"), float(h), Op.add)

    def frames(t):
        act(C("xp", 128 * t, 128 * (t + 1)), IND(C("frs", 128 * t, 128 * (t + 1)), V("l0")), bias=-MID, scale=-64.0)

    def frames_off(t):
        act(C("xneg", 128 * t, 128 * (t + 1)), C("frs", 128 * t, 128 * (t + 1)), bias=-MID, scale=-64.0)

    def spread_frames(t, i0, i1, queue="g"):
        for i in range(i0, i1):
            out, src = C("xrep", 2048 * t + i, 2048 * (t + 1), 16), C("xp", 128 * t, 128 * (t + 1))
            if queue == "g":
                select(out, src, [[0, 128]], Op.is_ge, 0, 0)
            else:
                act(out, src)

    frames(0)
    spread_frames(0, XS, 16)
    for k in range(8):
        if k < BV:
            ts(V("bd0", ALL, k), V("a0s"), col("bg", k), Op.mult)
        else:
            act(V("bd0", ALL, k), V("a0s"), scale=col("bg", k))
    for c, n, at in PLACES:
        k = SEATS.index(c)
        turn_blocks(C("bd", 128 * k, 128 * (k + n)), V("bd0", slice(c, 8, 8 // n)))
    state_list()
    act(V("r64", part=one), C("ones", 0, 128, part=one), scale=64.0)
    act(V("identf"), V("ident"))
    act(V("in65"), V("ident"), scale=-65.0 / 64)
    act(V("seln"), V("selp"), scale=-1.0)
    for h in range(3):
        act(C("kca", 48 + h, 204, 51, part=one), C("ones", 0, 4, part=one), scale=16.0e6)
    spread_frames(0, 0, XS, "a")

    iota(V("sq", ALL, 16), [[0, 384]], 0, 0)
    iota(V("dlt", ALL, slice(49, 52)), [[0, 24]], 0, 0)
    select(V("dlt", ALL, 0), C("ones", 0, 8), [[0, 8]], Op.not_equal, 0, 0, 4.0e9)
    iota(V("rst"), [[0, 204]], 0, 0)
    select(C("rst", 0, 204, 51), C("rst", 0, 204, 51), [[0, 4]], Op.not_equal, 0, 0, 4.0e9)
    iota(V("win"), [[0, 1024]], 0, 0)
    for x in range(2):
        out, src = V("mz", slice(4 * x, 4 * x + 4)), C("win", 0, 960)
        emit("s", lambda out=out, src=src: g.sync.dma_start(out[0], src[0]), [src], [out], "d_mz%d" % x, 16)
    select(V("tree", 2), C("ones", 0, 128), [[-16, 8], [0, 2], [-1, 8]], Op.is_equal, 0, 1)
    for l in range(2):
        w = 4 >> l
        for x in range(2):
            select(V("tree", l, ALL, x), C("ones", 0, 64), [[-16, 8], [-w, 8 // w], [0, w]], Op.is_ge, 0, 1)
            select(V("tree", l, ALL, x), V("tree", l, ALL, x), [[16, 8], [w, 8 // w], [0, w]], Op.is_ge, w - 1, -1)
    iota(C("row", 0, 8), [[16, 2], [-LEVEL, 4]], 3 * LEVEL, 0)
    for s, b in enumerate(blocks):
        iota(col("row", 8 + s), [[0, 1]], 4 * b, 0)
    for x in range(2):
        iota(col("row", 12 + x), [[0, 1]], blocks[2 * x + 1] - blocks[2 * x] - 1, 0)
    for l in range(3):
        select(C("sd", 32 * l, 32 * l + 32), C("ones", 0, 32), [[0, 16 >> l], [1, 2 << l]], Op.not_equal, 0, 0)
    iota(C("yy", 36, 113), [[0, 77]], 0, 0)
    iota(V("m127"), [[0, 64]], -127, 0)

    def owner_constants():
        ts(t1, m1, -127.5, Op.mult, pg16, Op.add)
        ts(t4, m2, -127.75, Op.mult, pg16, Op.add)
        ts(C("pf", 20, 22), C("row", 12, 14), m3, Op.mult, 0.5, Op.mult)
        ts(t2, pq, 128.0, Op.mult, t1, Op.add)
        ts(t5, pq, 128.0, Op.mult, t4, Op.add)
        tt(C("pf", 22, 24), C("pf", 20, 22), C("row", 8, 12, 2), Op.add)
        tt(C("pp", 0, 4), C("pf", 1, 5), C("row", 0, 4), Op.add)
        ts(C("lbd", 2, 6), C("row", 8, 12), t5, Op.add)
        ts(C("lbd", 0, 2), C("pf", 22, 24), t2, Op.add)
        tt(C("pp", 4, 8), C("pf", 1, 5), C("row", 4, 8), Op.add)
        ts(V("m4"), xi(0, 4), 4.0, Op.mult, m2, Op.is_equal)
        tt(V("m4"), V("m4"), C("row", 8, 12), Op.mult)
        emit("v", lambda: g.vector.tensor_reduce(t3[0], T.b_m4[:], AxisListType.X, Op.add), [V("m4")], [t3])
        ts(col("lbd", 6), t3, pp_, Op.add, m2, Op.subtract)

    def final_lists():
        ts(t3, m2, -7.75, Op.mult, q8, Op.add)
        ts(V("i16"), xi(0, 16), pq, Op.is_equal)
        ts(V("m16"), xi(0, 16), pq, Op.is_equal)
        ts(V("lfin"), xi(0, 2), 4.0, Op.mult, t3, Op.add)

    def diagonal(c, n, at):
        k = SEATS.index(c)
        return IND(C("bd", 128 * k, 128 * (k + n)), C("lbd", at, at + n))

    def keep_matrices():
        act(V("upb"), V("acl"), Fn.Relu, bias=252.0, scale=-1.0)
        act(C("ps5", 256, 384), V("acl"), bias=-2.0)
        act(C("ps5", 384, 512), V("upb"), bias=254.0, scale=-1.0)

    def candidates():
        cp(V("cand"), IND(C("mixs", 0, 2054), V("lst")))
        turn_blocks(V("tr"), V("cand"))

    def offsets():
        cp(V("offm"), IND(V("cand"), V("lperm")))

    def moved(name, j, e):
        a = 160 * (j % 2) + 16 - 16 * (e - j % 2)
        return C(name, a, a + 128)

    def key_a():
        for h in range(3):
            act(C("hi", h, 384, 3), C("tr", 128 * h, 128 * (h + 1)), bias=MID - 31.5)

    def key_b(bank):
        for h in range(3):
            mm(C(bank, h, 384, 3), V("identf"), C("tr", 128 * h, 128 * (h + 1)), h == 0, False)
        mm(C(bank, 0, 384), V("in65"), V("hi"), False, True)

    def key_start(k):
        mm(C(KEYS[k], 0, 204), V("r64", part=one), V("kca", part=one), True, False)
        for j in range(4 * k, 4 * k + 4):
            for e in range(2):
                b = 48 * (2 * (j // 2) + e)
                mm(C(KEYS[k], 51 * (j % 4), 51 * (j % 4) + 48), moved("selp", j, e), C("hi", b, b + 48), False, False)

    def key_delta(bank):
        act(V("dlt", ALL, slice(1, 49)), C(bank, 0, 384), bias=64.0 * 65 * 192, scale=64.0)

    def key_c(bank):
        for j in range(8):
            for e in range(2):
                b = 2 * (j // 2) + e
                mm(C(bank, 51 * j, 51 * j + 51), moved("selp", j, e), V("dlt", b, slice(0, 51)), e == 0, False)
                mm(C(bank, 51 * j, 51 * j + 51), moved("seln", j, e), V("dlt", b, slice(1, 52)), False, e == 1)

    def key_d(bank):
        act(V("stp"), C(bank, 0, 408))

    def left(c):
        k = SEATS.index(c)
        return C("bd", 128 * k, 128 * (k + 1))

    for t in range(R):
        last = t == R - 1
        def cls(name, c, a=0, b=512):
            return C(name, 512 * c + a, 512 * c + b)

        def prod(c, bank, start, a=0, b=512):
            mm(C(bank, 0, b - a), left(c), cls("mus", c, a, b), start, True)

        def by_scalar(c, bank, a=0, b=512):
            act(cls("mtab", c, a, b), C(bank, 0, b - a), bias=MID + 0.5)

        def by_vector(c, bank, a=0, b=512):
            ts(cls("mtab", c, a, b), C(bank, 0, b - a), LOW, Op.max, HIGH, Op.min)

        def clip(c, a=0, b=512):
            m = cls("mtab", c, a, b)
            ts(m, m, LOW, Op.max, HIGH, Op.min)

        if t == 0:
            prod(0, "ps6", False); prod(1, "ps7", False); prod(2, "ps4", True)
            by_vector(0, "ps6"); by_scalar(2, "ps4"); by_vector(1, "ps7")
            bias("ps6")
            candidates()
            offsets()
            prod(3, "ps5", True); prod(4, "ps4", True)
            by_scalar(3, "ps5"); by_scalar(4, "ps4"); key_a()
            prod(5, "ps3", False); prod(6, "ps0", True)
            by_vector(5, "ps3"); clip(2, 0, 1536); by_scalar(6, "ps0")
            prod(7, "ps6", False); key_b("ps1")
            by_vector(7, "ps6"); clip(6)
            key_delta("ps1")
            key_start(0)
        else:
            prod(0, "ps1", True, 256, 512); prod(4, "ps6", False); prod(1, "ps4", True); prod(5, "ps7", False)
            prod(3, "ps5", True); prod(2, "ps0", True); prod(7, "ps3", False)
            by_scalar(0, "ps1", 256, 512); by_vector(4, "ps6"); by_scalar(1, "ps4")
            by_vector(5, "ps7"); by_scalar(3, "ps5"); clip(0, 256, 1024)
            prod(6, "ps4", True); prod(0, "ps1", True, 0, 256)
            by_scalar(2, "ps0"); by_vector(7, "ps3"); by_scalar(6, "ps4"); by_scalar(0, "ps1", 0, 256)
            clip(2, 0, 1024); clip(6); clip(0, 0, 256)
            key_start(0); key_start(1)

        def entry(k, row):
            return 192 * k + 4 * row

        def gather_v(k, r0, r1):
            a, b = entry(k, r0), entry(k, r1)
            x = 2048 * t + 1024 * k + 64 * (r0 % 16)
            tt(C("dif", 16 * a, 16 * b), IND(V("mtab"), C("offm", a, b)), C("xrep", x, x + 16 * (b - a)), Op.add)

        def sums(k, r0, r1):
            for row in range(r0, r1):
                h, q = divmod(row, 16)
                mm(C(KEYS[k], h, 204, 3), C("za", 15 - q, 143 - q), V("sq", slice(entry(k, row), entry(k, row + 1))), False, row == 47)

        def square(k, r0, r1):
            a, b = entry(k, r0), entry(k, r1)
            act(V("sq", slice(a, b), slice(0, 16)), C("dif", 16 * a, 16 * b), Fn.Square, scale=1.0 / 64)
            sums(k, r0, r1)

        def gather_a(rows):
            n = 64 * rows
            width = [min(512, n - 512 * k) for k in range(3)]
            for k, bank in enumerate(WIDE):
                x = 2048 * t + 512 * (k % 2)
                mm(C(bank, 0, width[k]), V("ident"), C("xrep", x, x + width[k]), True, False)
            act(C("dif", 0, n), IND(V("mtab"), C("offm", 0, n // 16)))
            for k, bank in enumerate(WIDE):
                mm(C(bank, 0, width[k]), V("ident"), C("dif", 512 * k, 512 * k + width[k]), False, True)

        def square_a(rows):
            src = (T.b_pw[:, 0:64 * rows], V("ps3")[1] + V("ps4")[1] + V("ps5")[1])
            act(V("sq", slice(0, 4 * rows), slice(0, 16)), src, Fn.Square, scale=1.0 / 64)
            sums(0, 0, rows)

        def scans(k):
            a, keys = 204 * k, C(KEYS[k], 0, 204)
            scan(C("sc", 408 + a, 612 + a), V("rst"), keys, 0.0, Op.add, Op.min)
            scan(C("sc", a, a + 204), C("stp", a, a + 204), keys, 0.0, Op.add, Op.min)

        chunks = [(0, ROWS, 32)] + CHUNKS
        for ch in chunks:
            gather_v(*ch)
        gather_a(ROWS)
        if t == 0:
            key_c("ps6")
            key_start(1)
        square(*chunks[0])
        square_a(ROWS)
        square(*chunks[1])
        if t == 0:
            cp(C("stp", 0, 204), C("ps6", 0, 204))
        scans(0)
        for ch in chunks[2:]:
            square(*ch)
        if t == 0:
            act(C("stp", 204, 408), C("ps6", 204, 408))
            frames_off(0)
        scans(1)

        kb, ka = C("sc", 50, 408, 51), C("sc", 408 + 50, 816, 51)
        osc, ow, ocl = C("off", 0, 8), C("off", 8, 16), C("off", 16, 24)
        ts(C("b2", 0, 8), ka, 0xFC0, Op.bitwise_and)
        ts(C("b1", 8, 16), kb, 6, Op.logical_shift_right, 63, Op.bitwise_and)
        ts(C("b2", 8, 16), ka, 9, Op.logical_shift_right, 7, Op.bitwise_and)
        tt(ow, C("b2", 0, 8), C("b1", 8, 16), Op.add)
        tt(osc, C("b2", 8, 16), C("b1", 0, 8), Op.add)

        msg, land, dl = "msg%d" % t, "land%d" % t, "dl%d" % t
        if last:
            act(C("en", 16 * JV, 128), IND(V("mus"), C("off", 8 + JV, 16)))
            act(V("muw"), IND(V("mtab"), ow))
            cp(C("en", 0, 16 * JV), IND(V("mus"), C("off", 8, 8 + JV)))
            mm(C("ps6", 0, 128), C("xneg", 128 * t, 128 * (t + 1)), V("ident"), True, False)
        else:
            act(C("en", 16 * JV, 128), IND(V("mtab"), C("off", 8 + JV, 16)))
            act(V("muw"), IND(V("mus"), ow))
            tt(C("en", 0, 16 * JV), IND(V("mtab"), C("off", 8, 8 + JV)), C("xneg", 128 * t, 128 * t + 16 * JV), Op.add)
        ts(ocl, C("b2", 8, 16), pg16, Op.add)
        cp(IND(C("win", 0, 128 * JV), C("off", 0, JV)), C("en", 0, 16 * JV))
        rest = IND(C("win", 128 * JV, 1024), C("off", JV, 8))
        if last:
            cp(rest, C("en", 16 * JV, 128))
        else:
            tt(rest, C("en", 16 * JV, 128), C("xneg", 128 * t + 16 * JV, 128 * (t + 1)), Op.add)
        mm(C("ps6", 0, 128), V("muw"), V("ident"), not last, True)
        act(V("junk"), IND(V("ident"), ocl), scale=-256.0 * sign, accum=V("ncol"))
        act(V("mz", slice(0, 8), slice(112, 128)), C("ps6", 0, 128), scale=1.0 / 64)
        act(V("ncb"), C("ones", 0, 4), scale=V("ncol"))
        ts(V("hw"), ka, 16, Op.logical_shift_right, 3, Op.bitwise_and)
        ms(V("msg%d" % t, ALL, 8, 3), 0)
        tt(V("st"), V("st"), V("hw"), Op.add)
        for c in range(4):
            turn(V("ps2", slice(0, 64), c, ALL), C("win", c, 1024, 8), V("ident"))
        for half in range(2):
            for c in range(4):
                mm(C("ps%d" % (4 + half), c, 256, 4), C("win", 4 + c, 1024, 8), C("ident", 64 * half, 64 * (half + 1)), True, True)
        for l in range(3):
            mm(C("ps1", l, 12, 3), V("tree", l), V("ncb"), True, True)
        cp(C("w32", 8 * t, 8 * t + 8), ow)
        if not last:
            state_list()
        for x in range(2):
            cp(C("em", 256 * x, 256 * x + 256), V("ps2", slice(32 * x, 32 * x + 32)))
        act(C("em", 512, 768), C("ps4", 0, 256))
        cp(C("em", 768, 1024), C("ps5", 0, 256))
        ts(V(msg, ALL, 8, slice(0, 3)), C("ps1", 0, 12), OFFSET + sign * 256 * 300 / N, Op.add)
        for half, bank in enumerate(("ps7", "ps3")):
            for k in range(8):
                a = 512 * half + 64 * k
                mm(C(bank, 0, 64), V("mz", k, slice(112 - 16 * k, 240 - 16 * k)), C("em", a, a + 64), k == 0, k == 7)
            if half == 0:
                for x in range(2):
                    ts(V(msg, ALL, slice(2 * x, 8, 4), ALL), C(bank, x, 64, 2), sign, Op.mult, OFFSET, Op.add)
            else:
                ts(V(msg, ALL, slice(1, 8, 2), ALL), C(bank, 0, 64), sign, Op.mult, OFFSET, Op.add)

        def send_sums(msg=msg, land=land, t=t):
            trs = []
            for b in range(len(pairs)):
                to = [r for r in peers if r in pairs[b]]
                mask = sum(1 << e for e in engines[share * b:share * (b + 1)])
                trs.append(RemoteDMATransfer(dst_ids=[dst(r) for r in to], dma_engine_mask=mask, remote_sem=T.sem["ar%d_%d" % (t, side)],
                                             srcs=[T["b_" + msg][:, b]], dsts=[T["b_" + land][:, seat(rank, r), 0:9] for r in to]))
            g.remote_dma_fused(trs, local_sem=T.sem.sent)
        emit("g", send_sums, [V(msg)], [], "remote")
        sent[0] += share * len(pairs)

        nine = slice(0, 9)
        if not last:
            candidates()
        cp(V(land, N - 1, nine), V(msg, block))
        if t == 0:
            frames(1)
            spread_frames(1, 0, XW)
            owner_constants()
        if not last:
            frames_off(t + 1)
            bias("ps6"); bias("ps7"); bias("ps3")
            if t:
                keep_matrices()
            key_a(); key_b("ps1")
            if t == 0:
                for c, n, at in PLACES:
                    act(C("acl", c, 128, 8 // n), diagonal(c, n, at), bias=127.0)
                keep_matrices()
            key_delta("ps1")
            key_c("ps0")
            if t == 0:
                frames(2)
        else:
            ts(V("s1"), V("st"), 2047, Op.bitwise_and)
            cp(C("w32", 24, 32), V("s1"))
            for c in range(8):
                for s, b in enumerate(blocks):
                    mm(C("ps5", 32 * s + 4 * c, 32 * s + 4 * c + 4), left(c), C("i16", 4 * b, 4 * b + 4), True, True)
            for u in range(8):
                act(C("wexp", u, 512, 16), V("w32"), scale=col("m16", u))
                ts(C("wexp", 8 + u, 512, 16), V("w32"), col("m16", 8 + u), Op.mult)
            mm(V("ps4", part=slice(0, 8)), V("bg"), V("wexp"), True, True)
            act(V("anat"), C("ps5", 0, 128), bias=-192.0)
            act(V("outs", part=slice(0, 8)), V("ps4", part=slice(0, 8)))
            store("s", "d_yw", T.yw[:], C("outs", 0, 384, part=slice(0, 8)))
            store("s", "d_ys", T.ys[:], C("outs", 384, 512, part=slice(0, 8)))

        far = N - 1 - len(plane)
        other = C("ps7" if last else "ps4", 0, 72)
        emit("x", None, [], [V(land, slice(0, far))], "ar%d_%d" % (t, 1 - side), share * far)
        tt(other, V(land, slice(0, 2), nine), V(land, slice(2, 4), nine), Op.add)
        emit("x", None, [], [V(land, slice(far, N - 1))], "ar%d_%d" % (t, side), share * len(plane))
        tt(V("s4"), V(land, slice(4, 6), nine), V(land, slice(6, 8), nine), Op.add)
        if side == 0:
            tt(V("s2"), V("s4"), other, Op.subtract)
        else:
            tt(V("s2"), other, V("s4"), Op.subtract)
        tt(C("yy", 0, 36), C("s2", 0, 36), C("s2", 36, 72), Op.add)
        for x in range(2):
            scan(C("osel", x, 6, 2), C("yy", 32, 35), C("pp", 4 * x + 1, 4 * x + 4), col("pp", 4 * x), Op.min, Op.max)
        for l in range(3):
            a = LEVEL * (l + 1) - (2 << l) + 1
            scan(C("yy", a, a + 32), C("sd", 32 * l, 32 * l + 32), C("yy", 0, 32), 0.0, Op.mult, Op.add)
        picked = IND(V("yy"), C("osel", 4, 6))
        mine = C(dl, 0, 32)
        if last:
            ts(V("dcl"), picked, -512.0, Op.max, 512.0, Op.min)
            ts(mine, V("dcl"), -1.0 / 256, Op.mult, 192.0 - 0.5 + 1.0 / 512, Op.add)
        else:
            ts(mine, picked, -1.0 / 256, Op.mult, 2.0 - 0.5 + 1.0 / 512, Op.add)

        def send_steps(mine=mine, dl=dl, t=t):
            at = [32 * senders(r).index(rank) for r in plane]
            tr = RemoteDMATransfer(dst_ids=[dst(r) for r in plane], dma_engine_mask=wide_mask, remote_sem=T.sem["dr%d_%d" % (t, block)],
                                   srcs=[mine[0]], dsts=[T["b_" + dl][:, a:a + 32] for a in at])
            g.remote_dma_fused([tr], local_sem=T.sem.sent)
        emit("g", send_steps, [mine], [], "remote")
        sent[0] += wide

        def landed(s):
            emit("x", None, [], [C(dl, 32 * s, 32 * s + 32)], "dr%d_%d" % (t, blocks[s]), wide)

        def add_steps(s0, s1):
            tt(C("asum", 32 * s0, 32 * s1), C("ps5", 256 + 32 * s0, 256 + 32 * s1), C(dl, 32 * s0, 32 * s1), Op.add)

        def bound(s0, s1):
            tt(C("acl", 32 * s0, 32 * s1), C("ps5", 384 + 32 * s0, 384 + 32 * s1), C("asum", 32 * s0, 32 * s1), Op.min)

        def place(c, n, at):
            tt(diagonal(c, n, at), C("acl", c, 128, 8 // n), C("m127", 0, 16 * n), Op.add)

        def final(s):
            tt(C("afin", 32 * s, 32 * s + 32), IND(C(dl, 32 * s, 32 * s + 32), V("lfin")), C("anat", 32 * s, 32 * s + 32), Op.add)

        def final_bound(s):
            mid = slice(4 * blocks[s], 4 * blocks[s] + 4)
            ts(V("yas", ALL, mid), C("afin", 32 * s, 32 * s + 32), -127.0, Op.max, 127.0, Op.min)

        if not last:
            offsets()
            add_steps(0, 1)
            if t == 0:
                final_lists()
            bound(0, 1)
            key_d("ps0")
            if t == 0:
                spread_frames(1, XW, 16)
            iota(V("win"), [[0, 1024]], 0, 0)
            if t == 0:
                spread_frames(2, 0, 16)
            landed(1); add_steps(1, 2)
            landed(2); add_steps(2, 3); bound(1, 2)
            landed(3); add_steps(3, 4); bound(2, 3); bound(3, 4)
            for piece in [(0, 1, 6), (4, 1, 6)] + PLACES[1:]:
                place(*piece)
        else:
            final(0); final_bound(0)
            landed(1); final(1)
            landed(2); final(2); final_bound(1)
            landed(3); final(3); final_bound(2); final_bound(3)
            store("s", "d_ya", T.ya[0:64, :], V("yas", part=slice(0, 64)))
            store("a", "d_yb", T.ya[64:128, :], V("yas", part=slice(64, 128)))

    qsem = {"v": "qv", "a": "qa", "p": "qp", "g": "qg"}
    known = {q: {} for q in Q}
    clocks = []
    waits = []
    marked = set()
    for i, (q, call, deps, sem, count) in enumerate(ops):
        need = []
        if q != "x":
            kn = known[q]
            for o in sorted(deps, reverse=True):
                oq, osem = ops[o][0], ops[o][3]
                if osem == "remote":
                    continue
                key = osem if osem is not None else oq
                if osem is None and oq != "p":
                    marked.add(o)
                if kn.get(key, -1) >= o:
                    continue
                need.append(o)
                marked.add(o)
                for k2, v2 in clocks[o].items():
                    if kn.get(k2, -1) < v2:
                        kn[k2] = v2
            ck = dict(kn)
        else:
            ck = {}
        ck[sem if sem is not None else q] = i
        clocks.append(ck)
        waits.append(need)
    number = {}
    total = {q: 0 for q in qsem}
    for i, o in enumerate(ops):
        if o[3] is None and i in marked:
            total[o[0]] += 1
            number[i] = total[o[0]]
    for i, (q, call, deps, sem, count) in enumerate(ops):
        if q == "x":
            continue
        for o in waits[i]:
            if ops[o][3] is None:
                Q[q].wait_ge(T.sem[qsem[ops[o][0]]], number[o])
            else:
                Q[q].wait_ge(T.sem[ops[o][3]], ops[o][4])
        ins = call()
        if sem is None:
            if i in number:
                ins.then_inc(T.sem[qsem[q]], 1)
        elif sem != "remote":
            ins.then_inc(T.sem[sem], 16)
    for q in qsem:
        g.wait_ge(T.sem[qsem[q]], total[q])
    g.wait_ge(T.sem.sent, sent[0])
    for s in ("d_yw", "d_ys", "d_ya", "d_yb"):
        g.sync.wait_ge(T.sem[s], 16)
